import numpy as np
import ml_dtypes


def mxq(x, axis, fmt="e4m3"):
    dtype, down = {"e4m3": (ml_dtypes.float8_e4m3fn, 7), "e5m2": (ml_dtypes.float8_e5m2, 14)}[fmt]
    v = np.moveaxis(np.asarray(x, np.float32).astype(ml_dtypes.bfloat16).astype(np.float64), axis, -1)
    blocks = v.reshape(v.shape[:-1] + (-1, 32))
    amax = np.abs(blocks).max(-1, keepdims=True)
    byte = np.maximum(np.where(amax > 0, np.frexp(amax)[1] - 1 + 127, 0) - down, 1)
    scale = np.exp2(byte - 127.0)
    codes = (blocks / scale).astype(np.float32).astype(dtype).astype(np.float64)
    return np.moveaxis((codes * scale).reshape(v.shape), -1, axis)


WIDE = False


def mx_kscale(k):
    if not WIDE:
        return np.ones(k)
    levels = np.array([18, -18])
    if k % 512:
        return np.exp2(np.random.permutation(np.resize(levels, k // 32))).repeat(32)
    a = np.empty((k // 512, 16))
    for p in range(k // 512):
        a[p, :8] = np.random.permutation(np.resize(levels, 8))
        for g in range(8):
            far = levels[np.abs(levels - a[p, g]) >= 10]
            a[p, g + 8] = far[np.random.randint(len(far))]
    return np.exp2(a.ravel()).repeat(32)


def f64(x):
    return np.asarray(x).astype(np.float64)


def striped(idx):
    return np.tile(np.asarray(idx).reshape(-1, 16).T, (8, 1)).astype(np.uint16)


def unstriped(offs):
    return offs[:16].T.reshape(-1).astype(np.int64)

def planes(y):
    n, m = y.shape
    v = y.astype(np.float32).astype(ml_dtypes.bfloat16).astype(np.float64).reshape(n // 32, 32, m)
    top = np.abs(v).max(1)
    byte = np.clip(np.where(top > 0, np.frexp(top)[1] - 1 + 127 - 7, 1), 1, 254)
    codes = (v * np.exp2(127.0 - byte)[:, None, :]).reshape(n, m).astype(np.float32).astype(ml_dtypes.float8_e4m3fn).view(np.uint8)
    words = codes.reshape(n // 512, 128, 4, m).transpose(0, 1, 3, 2)
    return np.ascontiguousarray(words), np.ascontiguousarray(byte.astype(np.uint8).reshape(n // 512, 16, m))


B, N, T, D, DV, R = 1, 512, 2048, 512, 512, 1024


def setup_inputs():
    n = np.random.standard_normal
    idx = np.random.permutation(T)[:B * N]
    s = mx_kscale(D)[:, None]
    z = mx_kscale(R)[:, None]
    v = mx_kscale(DV)[:, None]
    q = n((B, D, R))
    do = n((B, DV, R))
    return {
        "qT": (q * s).astype(np.float32),
        "kT": (n((D, T)) * (1.00 / np.sqrt(D)) / s).astype(np.float32),
        "vT": (n((DV, T)) / np.sqrt(DV) / v).astype(np.float32),
        "doT": (do * v).astype(np.float32),
        "rw": (np.random.uniform(0.5, 1.5, (B, R, 1)) * 1.0 / np.sqrt(R) * z).astype(np.float32),
        "qm": (q.transpose(0, 2, 1) / z).astype(np.float32),
        "offs": striped(idx),
    }


def reference(qT, kT, vT, doT, rw, qm, offs):
    idx = unstriped(offs)
    pick = lambda x: x[:, idx].reshape(x.shape[0], B, N).transpose(1, 0, 2)
    a = mxq(f64(qT), 1, "e4m3").transpose(0, 2, 1) @ mxq(pick(f64(kT)), 1, "e4m3")
    dp = mxq(f64(doT), 1, "e5m2").transpose(0, 2, 1) @ mxq(pick(f64(vT)), 1, "e4m3")
    ds = f64(rw) * dp * 2.0 * np.maximum(a, 0.0)
    dk = mxq(f64(qm), 1, "e4m3").transpose(0, 2, 1) @ mxq(ds, 1, "e5m2")
    gk = np.zeros((D, T))
    gk[:, idx] = dk.transpose(1, 0, 2).reshape(D, B * N)
    out_0 = gk
    return (out_0,) + planes(out_0)

@@ -1,0 +1,298 @@
+from contextlib import ExitStack
+
+import concourse.mybir as mybir
+
+N, T, D, DV, R = 512, 2048, 512, 512, 1024
+FLOPS = 2 * R * N * (D + DV + D)
+
+F32 = mybir.dt.float32
+BF16 = mybir.dt.bfloat16
+I32 = mybir.dt.int32
+U32 = mybir.dt.uint32
+U16 = mybir.dt.uint16
+U8 = mybir.dt.uint8
+E4M3 = mybir.dt.float8_e4m3fn_x4
+E5M2 = mybir.dt.float8_e5m2_x4
+ACT = mybir.ActivationFunctionType
+ALU = mybir.AluOpType
+
+P = 128
+PACK = 4
+K_PASS = P * PACK
+PASSES = R // K_PASS
+BLOCK = 128
+CHUNK = 512
+CHUNKS = T // CHUNK
+
+
+def tile_attend_gat_pl_k_kernel(tc, qT, kT, vT, doT, rw, qm, offs, out_0, out_1, out_2):
+    nc = tc.nc
+    with ExitStack() as ctx:
+        keep = ctx.enter_context(tc.tile_pool(name="keep", bufs=1))
+        raws = ctx.enter_context(tc.tile_pool(name="raws", bufs=5))
+        grp = ctx.enter_context(tc.tile_pool(name="grp", bufs=8))
+        ps_dp = ctx.enter_context(tc.psum_pool(name="ps_dp", bufs=4))
+        ps_a = ctx.enter_context(tc.psum_pool(name="ps_a", bufs=2))
+        ps_dk = ctx.enter_context(tc.psum_pool(name="ps_dk", bufs=2))
+
+        offsets = keep.tile([P, N // 16], U16, name="offsets")
+        nc.sync.dma_start(offsets[:], offs)
+
+        def load_pool(src, name):
+            planes = []
+            rows = src.rearrange("(p j) t -> p j t", j=PACK)
+            for j in range(PACK):
+                plane = keep.tile([P, T], F32, name="%s%d" % (name, j))
+                nc.sync.dma_start(plane[:], rows[:, j, :])
+                planes.append(plane)
+            return planes
+
+        def load_raw(src):
+            raw = raws.tile([P, PACK, K_PASS], F32, name="raw")
+            nc.sync.dma_start(raw[:], src.rearrange("(p j) c -> p j c", j=PACK))
+            return raw
+
+        def cols(g):
+            return slice(g * K_PASS, (g + 1) * K_PASS)
+
+        v_planes = load_pool(vT, "v")
+        gate = keep.tile([P, PASSES, PACK], F32, name="gate")
+        nc.scalar.dma_start(gate[:], rw[0].rearrange("(g p j) o -> p g (j o)", g=PASSES, j=PACK))
+        do_raw0 = load_raw(doT[0][:, cols(0)])
+        k_planes = load_pool(kT, "k")
+        q_raw0 = load_raw(qT[0][:, cols(0)])
+        do_raw1 = load_raw(doT[0][:, cols(1)])
+        q_raw1 = load_raw(qT[0][:, cols(1)])
+        qm_raw = [load_raw(qm[0][cols(g), :]) for g in range(PASSES)]
+
+        windows = []
+        for t in range(PACK):
+            window = keep.tile([P, T], F32, name="window%d" % t)
+            nc.vector.memset(window[:], 0.0)
+            windows.append(window)
+
+        gate2 = keep.tile([P, PASSES, PACK], F32, name="gate2")
+        nc.scalar.mul(gate2[:], gate[:], 2.0)
+
+        def mx_tiles(name, width):
+            codes = keep.tile([P, width], U32, name=name + "_codes", align_bytes=64)
+            scales = keep.tile([P, width], U8, name=name + "_scales", align_bytes=64)
+            return codes, scales
+
+        def new_grouped():
+            return grp.tile([P, K_PASS * PACK], BF16, name="grouped", align_bytes=64)
+
+        def quantize(mx, fmt, grouped, first, count):
+            codes, scales = mx
+            nc.vector.quantize_mx(
+                out=codes[:, first : first + count].bitcast(fmt),
+                scales=scales[:, first : first + count],
+                in_=grouped[:, PACK * first : PACK * (first + count)],
+            )
+
+        def gather(planes, name):
+            grouped = new_grouped()
+            words = grouped[:].rearrange("p (n j) -> p n j", j=PACK)
+            for j in range(PACK):
+                nc.vector.tensor_copy(words[:, :, j], planes[j][:].indirect(offsets[:]))
+            mx = mx_tiles(name, N)
+            quantize(mx, E4M3, grouped, 0, N)
+            return mx
+
+        def deal(on_vector, raw, grouped, half):
+            dst = grouped[:].rearrange("p (t m j) -> p m j t", t=PACK, j=PACK)[:, :, :, 2 * half : 2 * half + 2]
+            src = raw[:].rearrange("p j (m t) -> p m j t", t=PACK)[:, :, :, 2 * half : 2 * half + 2]
+            if on_vector:
+                nc.vector.tensor_copy(dst, src)
+            else:
+                nc.scalar.copy(dst, src)
+
+        def matmul(out, lhs, lhs_fmt, lhs_cols, rhs, rhs_fmt, rhs_cols, start, stop):
+            nc.tensor.matmul_mx(
+                out=out,
+                lhsT=lhs[0][:, lhs_cols].bitcast(lhs_fmt),
+                lhsT_scale=lhs[1][:, lhs_cols],
+                rhs=rhs[0][:, rhs_cols].bitcast(rhs_fmt),
+                rhs_scale=rhs[1][:, rhs_cols],
+                start=start,
+                stop=stop,
+            )
+
+        def place(j):
+            return slice(j * P, (j + 1) * P)
+
+        def gated_dp(g, do_mx, v_mx):
+            banks = []
+            for j in range(PACK):
+                bank = ps_dp.tile([P, N], F32, name="dp")
+                matmul(bank[:], do_mx, E5M2, place(j), v_mx, E4M3, slice(0, N), True, True)
+                banks.append(bank)
+            halves = []
+            for h in range(2):
+                half = keep.tile([P, PACK, N // 2], F32, name="gdp%d_%d" % (g, h), align_bytes=64)
+                for j in range(PACK):
+                    nc.scalar.activation(
+                        half[:, j, :], banks[j][:, h * (N // 2) : (h + 1) * (N // 2)], ACT.Copy, scale=gate2[:, g, j : j + 1]
+                    )
+                halves.append(half)
+            return halves
+
+        def ds_block(c, q_mx, k_mx, gdp, ds_grouped):
+            bank = ps_a.tile([P, PACK, BLOCK], F32, name="a")
+            for j in range(PACK):
+                matmul(bank[:, j, :], q_mx, E4M3, place(j), k_mx, E4M3, slice(c * BLOCK, (c + 1) * BLOCK), True, True)
+            first = (c % 2) * BLOCK
+            nc.vector.scalar_tensor_tensor(
+                out=ds_grouped[:, PACK * c * BLOCK : PACK * (c + 1) * BLOCK].rearrange("p (n j) -> p n j", j=PACK),
+                in0=bank[:].rearrange("p j n -> p n j"),
+                scalar=0.0,
+                in1=gdp[c // 2][:, :, first : first + BLOCK].rearrange("p j n -> p n j"),
+                op0=ALU.max,
+                op1=ALU.mult,
+            )
+
+        v_mx = gather(v_planes, "v")
+
+        do_grp0 = new_grouped()
+        deal(False, do_raw0, do_grp0, 0)
+        deal(False, do_raw0, do_grp0, 1)
+        do_mx0 = mx_tiles("do0", K_PASS)
+        quantize(do_mx0, E5M2, do_grp0, 0, K_PASS)
+        gdp0 = gated_dp(0, do_mx0, v_mx)
+
+        k_mx = gather(k_planes, "k")
+
+        q_grp0 = new_grouped()
+        q_mx0 = mx_tiles("q0", K_PASS)
+        deal(False, q_raw0, q_grp0, 0)
+        deal(True, q_raw0, q_grp0, 1)
+        quantize(q_mx0, E4M3, q_grp0, 256, 256)
+        quantize(q_mx0, E4M3, q_grp0, 0, 256)
+
+        do_grp1 = new_grouped()
+        deal(False, do_raw1, do_grp1, 0)
+        deal(False, do_raw1, do_grp1, 1)
+
+        ds_grp0 = new_grouped()
+        ds_mx0 = mx_tiles("ds0", N)
+        for c in range(4):
+            ds_block(c, q_mx0, k_mx, gdp0, ds_grp0)
+
+        do_mx1 = mx_tiles("do1", K_PASS)
+        quantize(do_mx1, E5M2, do_grp1, 0, K_PASS)
+        q_grp1 = new_grouped()
+        q_mx1 = mx_tiles("q1", K_PASS)
+        deal(False, q_raw1, q_grp1, 0)
+        deal(True, q_raw1, q_grp1, 1)
+        gdp1 = gated_dp(1, do_mx1, v_mx)
+        quantize(q_mx1, E4M3, q_grp1, 0, K_PASS)
+        quantize(ds_mx0, E5M2, ds_grp0, 0, N)
+
+        ds_grp1 = keep.tile([P, K_PASS * PACK], BF16, name="ds_grp1", align_bytes=64)
+        ds_mx1 = mx_tiles("ds1", N)
+
+        def deal_qm(h, grouped):
+            for g in range(PASSES):
+                dst = grouped[:, g, :].rearrange("p (t m j) -> p m j t", t=2, j=PACK)
+                src = qm_raw[g][:].rearrange("p j (m t) -> p m j t", t=PACK)[:, :, :, 2 * h : 2 * h + 2]
+                nc.scalar.copy(dst, src)
+
+        def quantize_qm(codes, scales, grouped):
+            nc.vector.quantize_mx(out=codes.bitcast(E4M3), scales=scales, in_=grouped)
+            return codes, scales
+
+        qm_grp_a = grp.tile([P, PASSES, 1024], BF16, name="grouped", align_bytes=64)
+        qm_grp_b = grp.tile([P, PASSES, 1024], BF16, name="grouped", align_bytes=64)
+        qm_scales = keep.tile([P, 2, PASSES, 256], U8, name="qm_scales", align_bytes=64)
+        deal_qm(0, qm_grp_a)
+        deal_qm(1, qm_grp_b)
+        for c in range(3):
+            ds_block(c, q_mx1, k_mx, gdp1, ds_grp1)
+        quantize(ds_mx1, E5M2, ds_grp1, 0, 256)
+        codes_a0 = keep.tile([P, 256], U32, name="gdp1_0", align_bytes=64)
+        qm_a = [quantize_qm(codes_a0[:], qm_scales[:, 0, 0, :], qm_grp_a[:, 0, :])]
+        ds_block(3, q_mx1, k_mx, gdp1, ds_grp1)
+        codes_a1 = keep.tile([P, 256], U32, name="gdp1_1", align_bytes=64)
+        qm_a.append(quantize_qm(codes_a1[:], qm_scales[:, 0, 1, :], qm_grp_a[:, 1, :]))
+        quantize(ds_mx1, E5M2, ds_grp1, 256, 256)
+        codes_b = keep.tile([P, PASSES, 256], U32, name="ds_grp1", align_bytes=64)
+        qm_b = [quantize_qm(codes_b[:, g, :], qm_scales[:, 1, g, :], qm_grp_b[:, g, :]) for g in range(PASSES)]
+        ds_mx = [ds_mx0, ds_mx1]
+
+        out_rows = out_0.rearrange("(p t) c -> p t c", t=PACK)
+        pairs = [grp.tile([P, K_PASS * PACK], BF16, name="grouped", align_bytes=64) for c in range(CHUNKS)]
+
+        def round_plane(on_vector, t, c):
+            dst = pairs[c][:].rearrange("p (u n e) -> p u n e", u=2, e=2)[:, t // 2, :, t % 2]
+            src = windows[t][:, c * CHUNK : (c + 1) * CHUNK]
+            if t == 2 and c < 2:
+                dst = pairs[c][:].rearrange("p (u n e) -> p u n e", u=2, e=2)[:, 1, :, :]
+                src = src.unsqueeze(2).to_broadcast([P, CHUNK, 2])
+            if on_vector:
+                nc.vector.tensor_copy(dst, src)
+            else:
+                nc.scalar.copy(dst, src)
+
+        def dk_plane(t, qm_mx):
+            bank = ps_dk.tile([P, N], F32, name="dk")
+            for g in range(PASSES):
+                matmul(bank[:], qm_mx[g], E4M3, place(t % 2), ds_mx[g], E5M2, slice(0, N), g == 0, g == PASSES - 1)
+            dk = keep.tile([P, N], F32, name="dk_sb%d" % t, align_bytes=64)
+            nc.scalar.copy(dk[:], bank[:])
+            return dk
+
+        def scatter(t, dk):
+            nc.vector.tensor_copy(windows[t][:].indirect(offsets[:]), dk[:])
+            nc.sync.dma_start(out_rows[:, t, :], windows[t][:])
+
+        dk0 = dk_plane(0, qm_a)
+        dk1 = dk_plane(1, qm_a)
+        scatter(0, dk0)
+        dk2 = dk_plane(2, qm_b)
+        dk3 = dk_plane(3, qm_b)
+        for c in range(CHUNKS):
+            round_plane(False, 0, c)
+        scatter(1, dk1)
+        for c in range(CHUNKS):
+            round_plane(False, 1, c)
+        scatter(2, dk2)
+        for c in range(CHUNKS):
+            round_plane(False, 2, c)
+        scatter(3, dk3)
+
+        y_codes = [keep.tile([P, CHUNK], U32, name="y_codes%d" % c, align_bytes=64) for c in range(CHUNKS)]
+        y_scales = keep.tile([P, T], U8, name="y_scales", align_bytes=64)
+        words_out = out_1[0].rearrange("p t l -> p (t l)").bitcast(I32)
+
+        def weave(on_vector, c):
+            grouped = new_grouped()
+            dst = grouped[:].bitcast(F32).rearrange("p (n u) -> p n u", u=2)
+            src = pairs[c][:].bitcast(F32).rearrange("p (u n) -> p n u", u=2)
+            if on_vector:
+                nc.vector.tensor_copy(dst, src)
+            else:
+                nc.scalar.copy(dst, src)
+            return grouped
+
+        def finish(c, grouped):
+            span = slice(c * CHUNK, (c + 1) * CHUNK)
+            nc.vector.quantize_mx(out=y_codes[c][:].bitcast(E4M3), scales=y_scales[:, span], in_=grouped[:])
+            nc.sync.dma_start(words_out[:, span], y_codes[c][:].bitcast(I32))
+
+        round_plane(True, 3, 0)
+        round_plane(True, 3, 1)
+        round_plane(False, 3, 2)
+        round_plane(False, 3, 3)
+        y3 = weave(False, 3)
+        y0 = weave(True, 0)
+        y1 = weave(True, 1)
+        finish(0, y0)
+        y2 = weave(True, 2)
+        finish(1, y1)
+        finish(2, y2)
+        finish(3, y3)
+        for quad in range(4):
+            queue = nc.scalar if quad % 2 else nc.sync
+            queue.dma_start(
+                out_2[0][4 * quad : 4 * quad + 4, :].bitcast(I32), y_scales[32 * quad : 32 * quad + 4, :].bitcast(I32)
+            )

@@ -29,10 +29,9 @@ def tile_attend_gat_pl_k_kernel(tc, qT, kT, vT, doT, rw, qm, offs, out_0, out_1,
     nc = tc.nc
     with ExitStack() as ctx:
         keep = ctx.enter_context(tc.tile_pool(name="keep", bufs=1))
-        raws = ctx.enter_context(tc.tile_pool(name="raws", bufs=5))
+        raws = ctx.enter_context(tc.tile_pool(name="raws", bufs=1))
         grp = ctx.enter_context(tc.tile_pool(name="grp", bufs=8))
-        ps_dp = ctx.enter_context(tc.psum_pool(name="ps_dp", bufs=4))
-        ps_a = ctx.enter_context(tc.psum_pool(name="ps_a", bufs=2))
+        ps_dp = ctx.enter_context(tc.psum_pool(name="ps_dp", bufs=6))
         ps_dk = ctx.enter_context(tc.psum_pool(name="ps_dk", bufs=2))
 
         offsets = keep.tile([P, N // 16], U16, name="offsets")
@@ -42,28 +41,24 @@ def tile_attend_gat_pl_k_kernel(tc, qT, kT, vT, doT, rw, qm, offs, out_0, out_1,
             planes = []
             rows = src.rearrange("(p j) t -> p j t", j=PACK)
             for j in range(PACK):
-                plane = keep.tile([P, T], F32, name="%s%d" % (name, j))
+                plane = keep.tile([P, T], F32, name="%s%d" % (name, j), align_bytes=64)
                 nc.sync.dma_start(plane[:], rows[:, j, :])
                 planes.append(plane)
             return planes
 
-        def load_raw(src):
-            raw = raws.tile([P, PACK, K_PASS], F32, name="raw")
+        def load_raw(src, name):
+            raw = raws.tile([P, PACK, src.shape[1]], F32, name=name)
             nc.sync.dma_start(raw[:], src.rearrange("(p j) c -> p j c", j=PACK))
             return raw
 
-        def cols(g):
-            return slice(g * K_PASS, (g + 1) * K_PASS)
-
-        v_planes = load_pool(vT, "v")
+        do_raw = [load_raw(doT[0][:, 0:K_PASS], "do_raw0")]
         gate = keep.tile([P, PASSES, PACK], F32, name="gate")
         nc.scalar.dma_start(gate[:], rw[0].rearrange("(g p j) o -> p g (j o)", g=PASSES, j=PACK))
-        do_raw0 = load_raw(doT[0][:, cols(0)])
+        v_planes = load_pool(vT, "v")
+        do_raw.append(load_raw(doT[0][:, K_PASS:R], "do_raw1"))
         k_planes = load_pool(kT, "k")
-        q_raw0 = load_raw(qT[0][:, cols(0)])
-        do_raw1 = load_raw(doT[0][:, cols(1)])
-        q_raw1 = load_raw(qT[0][:, cols(1)])
-        qm_raw = [load_raw(qm[0][cols(g), :]) for g in range(PASSES)]
+        q_raw = [load_raw(qT[0][:, i * 256 : (i + 1) * 256], "q_raw%d" % i) for i in range(4)]
+        qm_raw = [load_raw(qm[0][g * K_PASS : (g + 1) * K_PASS, :], "qm_raw%d" % g) for g in range(PASSES)]
 
         windows = []
         for t in range(PACK):
@@ -90,18 +85,15 @@ def tile_attend_gat_pl_k_kernel(tc, qT, kT, vT, doT, rw, qm, offs, out_0, out_1,
                 in_=grouped[:, PACK * first : PACK * (first + count)],
             )
 
-        def gather(planes, name):
-            grouped = new_grouped()
+        def gather(grouped, planes, j):
             words = grouped[:].rearrange("p (n j) -> p n j", j=PACK)
-            for j in range(PACK):
-                nc.vector.tensor_copy(words[:, :, j], planes[j][:].indirect(offsets[:]))
-            mx = mx_tiles(name, N)
-            quantize(mx, E4M3, grouped, 0, N)
-            return mx
+            nc.vector.tensor_copy(words[:, :, j], planes[j][:].indirect(offsets[:]))
 
-        def deal(on_vector, raw, grouped, half):
-            dst = grouped[:].rearrange("p (t m j) -> p m j t", t=PACK, j=PACK)[:, :, :, 2 * half : 2 * half + 2]
-            src = raw[:].rearrange("p j (m t) -> p m j t", t=PACK)[:, :, :, 2 * half : 2 * half + 2]
+        def deal(on_vector, raw, grouped, half, first):
+            count = raw.shape[2] // PACK
+            dst = grouped[:].rearrange("p (t m j) -> p m j t", t=PACK, j=PACK)
+            dst = dst[:, first : first + count, :, 2 * half : 2 * half + 2]
+            src = raw.rearrange("p j (m t) -> p m j t", t=PACK)[:, :, :, 2 * half : 2 * half + 2]
             if on_vector:
                 nc.vector.tensor_copy(dst, src)
             else:
@@ -122,101 +114,132 @@ def tile_attend_gat_pl_k_kernel(tc, qT, kT, vT, doT, rw, qm, offs, out_0, out_1,
             return slice(j * P, (j + 1) * P)
 
         def gated_dp(g, do_mx, v_mx):
-            banks = []
+            flat = keep.tile([P, PACK, N], F32, name="v%d" % g, align_bytes=64)
             for j in range(PACK):
                 bank = ps_dp.tile([P, N], F32, name="dp")
                 matmul(bank[:], do_mx, E5M2, place(j), v_mx, E4M3, slice(0, N), True, True)
-                banks.append(bank)
-            halves = []
-            for h in range(2):
-                half = keep.tile([P, PACK, N // 2], F32, name="gdp%d_%d" % (g, h), align_bytes=64)
-                for j in range(PACK):
-                    nc.scalar.activation(
-                        half[:, j, :], banks[j][:, h * (N // 2) : (h + 1) * (N // 2)], ACT.Copy, scale=gate2[:, g, j : j + 1]
-                    )
-                halves.append(half)
-            return halves
+                nc.scalar.activation(flat[:, j, :], bank[:], ACT.Copy, scale=gate2[:, g, j : j + 1])
+            return flat
+
+        def weave_dp(on_vector, flat, c, name):
+            block = keep.tile([P, BLOCK, PACK], F32, name=name, align_bytes=64)
+            src = flat[:, :, c * BLOCK : (c + 1) * BLOCK].rearrange("p j n -> p n j")
+            if on_vector:
+                nc.vector.tensor_copy(block[:], src)
+            else:
+                nc.scalar.copy(block[:], src)
+            return block
 
         def ds_block(c, q_mx, k_mx, gdp, ds_grouped):
-            bank = ps_a.tile([P, PACK, BLOCK], F32, name="a")
-            for j in range(PACK):
+            bank = ps_dp.tile([P, PACK, BLOCK], F32, name="dp")
+            for j in (2, 3, 0, 1):
                 matmul(bank[:, j, :], q_mx, E4M3, place(j), k_mx, E4M3, slice(c * BLOCK, (c + 1) * BLOCK), True, True)
-            first = (c % 2) * BLOCK
             nc.vector.scalar_tensor_tensor(
                 out=ds_grouped[:, PACK * c * BLOCK : PACK * (c + 1) * BLOCK].rearrange("p (n j) -> p n j", j=PACK),
                 in0=bank[:].rearrange("p j n -> p n j"),
                 scalar=0.0,
-                in1=gdp[c // 2][:, :, first : first + BLOCK].rearrange("p j n -> p n j"),
+                in1=gdp[c][:],
                 op0=ALU.max,
                 op1=ALU.mult,
             )
 
-        v_mx = gather(v_planes, "v")
+        def quantize_do(on_vector, g):
+            grouped = new_grouped()
+            for half in range(2):
+                deal(on_vector, do_raw[g][:], grouped, half, 0)
+            mx = mx_tiles("do%d" % g, K_PASS)
+            quantize(mx, E5M2, grouped, 0, K_PASS)
+            return mx
 
-        do_grp0 = new_grouped()
-        deal(False, do_raw0, do_grp0, 0)
-        deal(False, do_raw0, do_grp0, 1)
-        do_mx0 = mx_tiles("do0", K_PASS)
-        quantize(do_mx0, E5M2, do_grp0, 0, K_PASS)
-        gdp0 = gated_dp(0, do_mx0, v_mx)
+        do_mx0 = quantize_do(False, 0)
+        v_grp = new_grouped()
+        for j in range(PACK):
+            gather(v_grp, v_planes, j)
+        v_mx = mx_tiles("v", N)
+        quantize(v_mx, E4M3, v_grp, 0, N)
+        do_mx1 = quantize_do(True, 1)
+        flat0 = gated_dp(0, do_mx0, v_mx)
+        flat1 = gated_dp(1, do_mx1, v_mx)
+        gdp0 = [weave_dp(False, flat0, c, "gdp0_%d" % c) for c in range(3)]
+        gdp1 = [weave_dp(False, flat1, c, "gdp1_%d" % c) for c in range(2)]
+        k_grp = new_grouped()
+        gather(k_grp, k_planes, 0)
+        gdp0.append(weave_dp(True, flat0, 3, "k0"))
+        gather(k_grp, k_planes, 1)
+        gdp1.append(weave_dp(True, flat1, 2, "k1"))
+        gather(k_grp, k_planes, 2)
+        gdp1.append(weave_dp(True, flat1, 3, "k2"))
+        gather(k_grp, k_planes, 3)
+        k_mx = mx_tiles("k", N)
+        quantize(k_mx, E4M3, k_grp, 0, N)
 
-        k_mx = gather(k_planes, "k")
+        def deal_half(on_vector, raw, grouped, half, first):
+            count = raw.shape[2] // PACK
+            dst = grouped.rearrange("p (t m j) -> p m j t", t=2, j=PACK)[:, first : first + count]
+            src = raw.rearrange("p j (m t) -> p m j t", t=PACK)[:, :, :, 2 * half : 2 * half + 2]
+            if on_vector:
+                nc.vector.tensor_copy(dst, src)
+            else:
+                nc.scalar.copy(dst, src)
 
-        q_grp0 = new_grouped()
+        q_grp0 = [grp.tile([P, 1024], BF16, name="grouped", align_bytes=64) for half in range(2)]
         q_mx0 = mx_tiles("q0", K_PASS)
-        deal(False, q_raw0, q_grp0, 0)
-        deal(True, q_raw0, q_grp0, 1)
-        quantize(q_mx0, E4M3, q_grp0, 256, 256)
-        quantize(q_mx0, E4M3, q_grp0, 0, 256)
+        deal_half(False, q_raw[0][:], q_grp0[1][:], 1, 0)
+        deal_half(False, q_raw[0][:], q_grp0[0][:], 0, 0)
+        deal_half(True, q_raw[1][:], q_grp0[1][:], 1, 64)
+        deal_half(False, q_raw[1][:], q_grp0[0][:], 0, 64)
+        for half in (1, 0):
+            span = slice(256 * half, 256 * (half + 1))
+            nc.vector.quantize_mx(out=q_mx0[0][:, span].bitcast(E4M3), scales=q_mx0[1][:, span], in_=q_grp0[half][:])
 
-        do_grp1 = new_grouped()
-        deal(False, do_raw1, do_grp1, 0)
-        deal(False, do_raw1, do_grp1, 1)
+        q_grp1 = new_grouped()
+        for i in range(2):
+            for half in range(2):
+                deal(False, q_raw[2 + i][:], q_grp1, half, 64 * i)
 
         ds_grp0 = new_grouped()
         ds_mx0 = mx_tiles("ds0", N)
         for c in range(4):
             ds_block(c, q_mx0, k_mx, gdp0, ds_grp0)
-
-        do_mx1 = mx_tiles("do1", K_PASS)
-        quantize(do_mx1, E5M2, do_grp1, 0, K_PASS)
-        q_grp1 = new_grouped()
-        q_mx1 = mx_tiles("q1", K_PASS)
-        deal(False, q_raw1, q_grp1, 0)
-        deal(True, q_raw1, q_grp1, 1)
-        gdp1 = gated_dp(1, do_mx1, v_mx)
+        q_mx1 = (
+            keep.tile([P, K_PASS], U32, name="k0", align_bytes=64),
+            keep.tile([P, K_PASS], U8, name="q1_scales", align_bytes=64),
+        )
         quantize(q_mx1, E4M3, q_grp1, 0, K_PASS)
         quantize(ds_mx0, E5M2, ds_grp0, 0, N)
 
         ds_grp1 = keep.tile([P, K_PASS * PACK], BF16, name="ds_grp1", align_bytes=64)
         ds_mx1 = mx_tiles("ds1", N)
 
-        def deal_qm(h, grouped):
-            for g in range(PASSES):
-                dst = grouped[:, g, :].rearrange("p (t m j) -> p m j t", t=2, j=PACK)
-                src = qm_raw[g][:].rearrange("p j (m t) -> p m j t", t=PACK)[:, :, :, 2 * h : 2 * h + 2]
-                nc.scalar.copy(dst, src)
+        def deal_qm(g, h, grouped):
+            dst = grouped[:, g, :].rearrange("p (t m j) -> p m j t", t=2, j=PACK)
+            src = qm_raw[g][:].rearrange("p j (m t) -> p m j t", t=PACK)[:, :, :, 2 * h : 2 * h + 2]
+            nc.scalar.copy(dst, src)
 
         def quantize_qm(codes, scales, grouped):
             nc.vector.quantize_mx(out=codes.bitcast(E4M3), scales=scales, in_=grouped)
             return codes, scales
 
-        qm_grp_a = grp.tile([P, PASSES, 1024], BF16, name="grouped", align_bytes=64)
+        qm_grp_a = keep.tile([P, PASSES, 1024], BF16, name="qm_grp_a", align_bytes=64)
         qm_grp_b = grp.tile([P, PASSES, 1024], BF16, name="grouped", align_bytes=64)
-        qm_scales = keep.tile([P, 2, PASSES, 256], U8, name="qm_scales", align_bytes=64)
-        deal_qm(0, qm_grp_a)
-        deal_qm(1, qm_grp_b)
-        for c in range(3):
-            ds_block(c, q_mx1, k_mx, gdp1, ds_grp1)
+        scales_a = keep.tile([P, PASSES, 256], U8, name="scales_a", align_bytes=64)
+        for g in range(PASSES):
+            deal_qm(g, 0, qm_grp_a)
+            deal_qm(g, 1, qm_grp_b)
+        ds_block(0, q_mx1, k_mx, gdp1, ds_grp1)
+        ds_block(1, q_mx1, k_mx, gdp1, ds_grp1)
+        codes_a0 = keep.tile([P, 256], U32, name="gdp1_1", align_bytes=64)
+        qm_a = [quantize_qm(codes_a0[:], scales_a[:, 0, :], qm_grp_a[:, 0, :])]
+        ds_block(2, q_mx1, k_mx, gdp1, ds_grp1)
         quantize(ds_mx1, E5M2, ds_grp1, 0, 256)
-        codes_a0 = keep.tile([P, 256], U32, name="gdp1_0", align_bytes=64)
-        qm_a = [quantize_qm(codes_a0[:], qm_scales[:, 0, 0, :], qm_grp_a[:, 0, :])]
+        codes_a1 = keep.tile([P, 256], U32, name="k1", align_bytes=64)
+        qm_a.append(quantize_qm(codes_a1[:], scales_a[:, 1, :], qm_grp_a[:, 1, :]))
         ds_block(3, q_mx1, k_mx, gdp1, ds_grp1)
-        codes_a1 = keep.tile([P, 256], U32, name="gdp1_1", align_bytes=64)
-        qm_a.append(quantize_qm(codes_a1[:], qm_scales[:, 0, 1, :], qm_grp_a[:, 1, :]))
-        quantize(ds_mx1, E5M2, ds_grp1, 256, 256)
+        quantize(ds_mx1, E5M2, ds_grp1, 256, 128)
+        quantize(ds_mx1, E5M2, ds_grp1, 384, 128)
         codes_b = keep.tile([P, PASSES, 256], U32, name="ds_grp1", align_bytes=64)
-        qm_b = [quantize_qm(codes_b[:, g, :], qm_scales[:, 1, g, :], qm_grp_b[:, g, :]) for g in range(PASSES)]
+        scales_b = keep.tile([P, PASSES, 256], U8, name="qm_grp_a", align_bytes=64)
+        qm_b = [quantize_qm(codes_b[:, g, :], scales_b[:, g, :], qm_grp_b[:, g, :]) for g in range(PASSES)]
         ds_mx = [ds_mx0, ds_mx1]
 
         out_rows = out_0.rearrange("(p t) c -> p t c", t=PACK)
@@ -225,9 +248,6 @@ def tile_attend_gat_pl_k_kernel(tc, qT, kT, vT, doT, rw, qm, offs, out_0, out_1,
         def round_plane(on_vector, t, c):
             dst = pairs[c][:].rearrange("p (u n e) -> p u n e", u=2, e=2)[:, t // 2, :, t % 2]
             src = windows[t][:, c * CHUNK : (c + 1) * CHUNK]
-            if t == 2 and c < 2:
-                dst = pairs[c][:].rearrange("p (u n e) -> p u n e", u=2, e=2)[:, 1, :, :]
-                src = src.unsqueeze(2).to_broadcast([P, CHUNK, 2])
             if on_vector:
                 nc.vector.tensor_copy(dst, src)
             else:
@@ -256,7 +276,7 @@ def tile_attend_gat_pl_k_kernel(tc, qT, kT, vT, doT, rw, qm, offs, out_0, out_1,
         for c in range(CHUNKS):
             round_plane(False, 1, c)
         scatter(2, dk2)
-        for c in range(CHUNKS):
+        for c in range(1, CHUNKS):
             round_plane(False, 2, c)
         scatter(3, dk3)
 
@@ -279,10 +299,10 @@ def tile_attend_gat_pl_k_kernel(tc, qT, kT, vT, doT, rw, qm, offs, out_0, out_1,
             nc.vector.quantize_mx(out=y_codes[c][:].bitcast(E4M3), scales=y_scales[:, span], in_=grouped[:])
             nc.sync.dma_start(words_out[:, span], y_codes[c][:].bitcast(I32))
 
+        round_plane(True, 2, 0)
         round_plane(True, 3, 0)
-        round_plane(True, 3, 1)
-        round_plane(False, 3, 2)
-        round_plane(False, 3, 3)
+        for c in range(1, CHUNKS):
+            round_plane(False, 3, c)
         y3 = weave(False, 3)
         y0 = weave(True, 0)
         y1 = weave(True, 1)

@@ -133,7 +133,7 @@ def tile_attend_gat_pl_k_kernel(tc, qT, kT, vT, doT, rw, qm, offs, out_0, out_1,
         def ds_block(c, q_mx, k_mx, gdp, ds_grouped):
             bank = ps_dp.tile([P, PACK, BLOCK], F32, name="dp")
             for j in (2, 3, 0, 1):
-                matmul(bank[:, j, :], q_mx, E4M3, place(j), k_mx, E4M3, slice(c * BLOCK, (c + 1) * BLOCK), True, True)
+                matmul(bank[:, j, :], q_mx[j // 2], E4M3, place(j % 2), k_mx, E4M3, slice(c * BLOCK, (c + 1) * BLOCK), True, True)
             nc.vector.scalar_tensor_tensor(
                 out=ds_grouped[:, PACK * c * BLOCK : PACK * (c + 1) * BLOCK].rearrange("p (n j) -> p n j", j=PACK),
                 in0=bank[:].rearrange("p j n -> p n j"),
@@ -160,15 +160,12 @@ def tile_attend_gat_pl_k_kernel(tc, qT, kT, vT, doT, rw, qm, offs, out_0, out_1,
         do_mx1 = quantize_do(True, 1)
         flat0 = gated_dp(0, do_mx0, v_mx)
         flat1 = gated_dp(1, do_mx1, v_mx)
-        gdp0 = [weave_dp(False, flat0, c, "gdp0_%d" % c) for c in range(3)]
-        gdp1 = [weave_dp(False, flat1, c, "gdp1_%d" % c) for c in range(2)]
+        gdp0 = [weave_dp(False, flat0, 0, "gdp0_0"), None, None, None]
+        gdp1 = [weave_dp(False, flat1, c, "gdp1_%d" % c) for c in range(4)]
         k_grp = new_grouped()
-        gather(k_grp, k_planes, 0)
-        gdp0.append(weave_dp(True, flat0, 3, "k0"))
-        gather(k_grp, k_planes, 1)
-        gdp1.append(weave_dp(True, flat1, 2, "k1"))
-        gather(k_grp, k_planes, 2)
-        gdp1.append(weave_dp(True, flat1, 3, "k2"))
+        for j in range(3):
+            gather(k_grp, k_planes, j)
+            gdp0[3 - j] = weave_dp(True, flat0, 3 - j, "k%d" % j)
         gather(k_grp, k_planes, 3)
         k_mx = mx_tiles("k", N)
         quantize(k_mx, E4M3, k_grp, 0, N)
@@ -183,14 +180,13 @@ def tile_attend_gat_pl_k_kernel(tc, qT, kT, vT, doT, rw, qm, offs, out_0, out_1,
                 nc.scalar.copy(dst, src)
 
         q_grp0 = [grp.tile([P, 1024], BF16, name="grouped", align_bytes=64) for half in range(2)]
-        q_mx0 = mx_tiles("q0", K_PASS)
+        q_mx0 = [mx_tiles("q0_%d" % half, 256) for half in range(2)]
         deal_half(False, q_raw[0][:], q_grp0[1][:], 1, 0)
         deal_half(False, q_raw[0][:], q_grp0[0][:], 0, 0)
         deal_half(True, q_raw[1][:], q_grp0[1][:], 1, 64)
         deal_half(False, q_raw[1][:], q_grp0[0][:], 0, 64)
         for half in (1, 0):
-            span = slice(256 * half, 256 * (half + 1))
-            nc.vector.quantize_mx(out=q_mx0[0][:, span].bitcast(E4M3), scales=q_mx0[1][:, span], in_=q_grp0[half][:])
+            quantize(q_mx0[half], E4M3, q_grp0[half], 0, 256)
 
         q_grp1 = new_grouped()
         for i in range(2):
@@ -207,6 +203,7 @@ def tile_attend_gat_pl_k_kernel(tc, qT, kT, vT, doT, rw, qm, offs, out_0, out_1,
         )
         quantize(q_mx1, E4M3, q_grp1, 0, K_PASS)
         quantize(ds_mx0, E5M2, ds_grp0, 0, N)
+        q_mx1 = [(q_mx1[0][:, 256 * half : 256 * (half + 1)], q_mx1[1][:, 256 * half : 256 * (half + 1)]) for half in range(2)]
 
         ds_grp1 = keep.tile([P, K_PASS * PACK], BF16, name="ds_grp1", align_bytes=64)
         ds_mx1 = mx_tiles("ds1", N)
@@ -232,7 +229,7 @@ def tile_attend_gat_pl_k_kernel(tc, qT, kT, vT, doT, rw, qm, offs, out_0, out_1,
         qm_a = [quantize_qm(codes_a0[:], scales_a[:, 0, :], qm_grp_a[:, 0, :])]
         ds_block(2, q_mx1, k_mx, gdp1, ds_grp1)
         quantize(ds_mx1, E5M2, ds_grp1, 0, 256)
-        codes_a1 = keep.tile([P, 256], U32, name="k1", align_bytes=64)
+        codes_a1 = keep.tile([P, 256], U32, name="gdp1_2", align_bytes=64)
         qm_a.append(quantize_qm(codes_a1[:], scales_a[:, 1, :], qm_grp_a[:, 1, :]))
         ds_block(3, q_mx1, k_mx, gdp1, ds_grp1)
         quantize(ds_mx1, E5M2, ds_grp1, 256, 128)
@@ -258,11 +255,17 @@ def tile_attend_gat_pl_k_kernel(tc, qT, kT, vT, doT, rw, qm, offs, out_0, out_1,
             for g in range(PASSES):
                 matmul(bank[:], qm_mx[g], E4M3, place(t % 2), ds_mx[g], E5M2, slice(0, N), g == 0, g == PASSES - 1)
             dk = keep.tile([P, N], F32, name="dk_sb%d" % t, align_bytes=64)
-            nc.scalar.copy(dk[:], bank[:])
+            pieces = 2 if t == 0 else 1
+            for i in range(pieces):
+                span = slice(i * N // pieces, (i + 1) * N // pieces)
+                nc.scalar.copy(dk[:, span], bank[:, span])
             return dk
 
         def scatter(t, dk):
-            nc.vector.tensor_copy(windows[t][:].indirect(offsets[:]), dk[:])
+            pieces = 2 if t == 0 else 1
+            for i in range(pieces):
+                first, last = i * N // pieces, (i + 1) * N // pieces
+                nc.vector.tensor_copy(windows[t][:].indirect(offsets[:, first // 16 : last // 16]), dk[:, first:last])
             nc.sync.dma_start(out_rows[:, t, :], windows[t][:])
 
         dk0 = dk_plane(0, qm_a)

@@ -240,15 +240,18 @@ def tile_attend_gat_pl_k_kernel(tc, qT, kT, vT, doT, rw, qm, offs, out_0, out_1,
         ds_mx = [ds_mx0, ds_mx1]
 
         out_rows = out_0.rearrange("(p t) c -> p t c", t=PACK)
-        pairs = [grp.tile([P, K_PASS * PACK], BF16, name="grouped", align_bytes=64) for c in range(CHUNKS)]
+        split = T // 2
+        rounded = keep.tile([P, PACK, split], BF16, name="k3", align_bytes=64)
+        pairs = [grp.tile([P, PACK * CHUNK], BF16, name="grouped", align_bytes=64) for c in range(2)]
 
-        def round_plane(on_vector, t, c):
+        def round_pairs(t, c):
             dst = pairs[c][:].rearrange("p (u n e) -> p u n e", u=2, e=2)[:, t // 2, :, t % 2]
-            src = windows[t][:, c * CHUNK : (c + 1) * CHUNK]
-            if on_vector:
-                nc.vector.tensor_copy(dst, src)
-            else:
-                nc.scalar.copy(dst, src)
+            nc.scalar.copy(dst, windows[t][:, split + c * CHUNK : split + (c + 1) * CHUNK])
+
+        def round_plane(t):
+            nc.scalar.copy(rounded[:, t, :], windows[t][:, 0:split])
+            for c in range(2):
+                round_pairs(t, c)
 
         def dk_plane(t, qm_mx):
             bank = ps_dk.tile([P, N], F32, name="dk")
@@ -273,28 +276,28 @@ def tile_attend_gat_pl_k_kernel(tc, qT, kT, vT, doT, rw, qm, offs, out_0, out_1,
         scatter(0, dk0)
         dk2 = dk_plane(2, qm_b)
         dk3 = dk_plane(3, qm_b)
-        for c in range(CHUNKS):
-            round_plane(False, 0, c)
+        round_plane(0)
         scatter(1, dk1)
-        for c in range(CHUNKS):
-            round_plane(False, 1, c)
+        round_plane(1)
         scatter(2, dk2)
-        for c in range(1, CHUNKS):
-            round_plane(False, 2, c)
+        round_plane(2)
         scatter(3, dk3)
 
         y_codes = [keep.tile([P, CHUNK], U32, name="y_codes%d" % c, align_bytes=64) for c in range(CHUNKS)]
         y_scales = keep.tile([P, T], U8, name="y_scales", align_bytes=64)
         words_out = out_1[0].rearrange("p t l -> p (t l)").bitcast(I32)
 
-        def weave(on_vector, c):
+        def weave_pairs(c):
             grouped = new_grouped()
             dst = grouped[:].bitcast(F32).rearrange("p (n u) -> p n u", u=2)
-            src = pairs[c][:].bitcast(F32).rearrange("p (u n) -> p n u", u=2)
-            if on_vector:
-                nc.vector.tensor_copy(dst, src)
-            else:
-                nc.scalar.copy(dst, src)
+            nc.scalar.copy(dst, pairs[c][:].bitcast(F32).rearrange("p (u n) -> p n u", u=2))
+            return grouped
+
+        def weave_planes(c):
+            grouped = new_grouped()
+            dst = grouped[:].rearrange("p (n i t) -> p n t i", i=4, t=PACK)
+            src = rounded[:, :, c * CHUNK : (c + 1) * CHUNK].rearrange("p t (n i) -> p n t i", i=4)
+            nc.vector.tensor_copy(dst, src)
             return grouped
 
         def finish(c, grouped):
@@ -302,17 +305,18 @@ def tile_attend_gat_pl_k_kernel(tc, qT, kT, vT, doT, rw, qm, offs, out_0, out_1,
             nc.vector.quantize_mx(out=y_codes[c][:].bitcast(E4M3), scales=y_scales[:, span], in_=grouped[:])
             nc.sync.dma_start(words_out[:, span], y_codes[c][:].bitcast(I32))
 
-        round_plane(True, 2, 0)
-        round_plane(True, 3, 0)
-        for c in range(1, CHUNKS):
-            round_plane(False, 3, c)
-        y3 = weave(False, 3)
-        y0 = weave(True, 0)
-        y1 = weave(True, 1)
+        for c in range(2):
+            span = slice(c * CHUNK, (c + 1) * CHUNK)
+            nc.vector.tensor_copy(rounded[:, 3, span], windows[3][:, span])
+        round_pairs(3, 0)
+        y2 = weave_pairs(0)
+        round_pairs(3, 1)
+        y3 = weave_pairs(1)
+        y0 = weave_planes(0)
+        y1 = weave_planes(1)
         finish(0, y0)
-        y2 = weave(True, 2)
-        finish(1, y1)
         finish(2, y2)
+        finish(1, y1)
         finish(3, y3)
         for quad in range(4):
             queue = nc.scalar if quad % 2 else nc.sync

@@ -51,11 +51,10 @@ def tile_attend_gat_pl_k_kernel(tc, qT, kT, vT, doT, rw, qm, offs, out_0, out_1,
             nc.sync.dma_start(raw[:], src.rearrange("(p j) c -> p j c", j=PACK))
             return raw
 
-        do_raw = [load_raw(doT[0][:, 0:K_PASS], "do_raw0")]
+        do_raw = load_raw(doT[0], "do_raw")
         gate = keep.tile([P, PASSES, PACK], F32, name="gate")
         nc.scalar.dma_start(gate[:], rw[0].rearrange("(g p j) o -> p g (j o)", g=PASSES, j=PACK))
         v_planes = load_pool(vT, "v")
-        do_raw.append(load_raw(doT[0][:, K_PASS:R], "do_raw1"))
         k_planes = load_pool(kT, "k")
         q_raw = [load_raw(qT[0][:, i * 256 : (i + 1) * 256], "q_raw%d" % i) for i in range(4)]
         qm_raw = [load_raw(qm[0][g * K_PASS : (g + 1) * K_PASS, :], "qm_raw%d" % g) for g in range(PASSES)]
@@ -121,15 +120,6 @@ def tile_attend_gat_pl_k_kernel(tc, qT, kT, vT, doT, rw, qm, offs, out_0, out_1,
                 nc.scalar.activation(flat[:, j, :], bank[:], ACT.Copy, scale=gate2[:, g, j : j + 1])
             return flat
 
-        def weave_dp(on_vector, flat, c, name):
-            block = keep.tile([P, BLOCK, PACK], F32, name=name, align_bytes=64)
-            src = flat[:, :, c * BLOCK : (c + 1) * BLOCK].rearrange("p j n -> p n j")
-            if on_vector:
-                nc.vector.tensor_copy(block[:], src)
-            else:
-                nc.scalar.copy(block[:], src)
-            return block
-
         def ds_block(c, q_mx, k_mx, gdp, ds_grouped):
             bank = ps_dp.tile([P, PACK, BLOCK], F32, name="dp")
             for j in (2, 3, 0, 1):
@@ -138,7 +128,7 @@ def tile_attend_gat_pl_k_kernel(tc, qT, kT, vT, doT, rw, qm, offs, out_0, out_1,
                 out=ds_grouped[:, PACK * c * BLOCK : PACK * (c + 1) * BLOCK].rearrange("p (n j) -> p n j", j=PACK),
                 in0=bank[:].rearrange("p j n -> p n j"),
                 scalar=0.0,
-                in1=gdp[c][:],
+                in1=gdp[:, :, c * BLOCK : (c + 1) * BLOCK].rearrange("p j n -> p n j"),
                 op0=ALU.max,
                 op1=ALU.mult,
             )
@@ -146,27 +136,23 @@ def tile_attend_gat_pl_k_kernel(tc, qT, kT, vT, doT, rw, qm, offs, out_0, out_1,
         def quantize_do(on_vector, g):
             grouped = new_grouped()
             for half in range(2):
-                deal(on_vector, do_raw[g][:], grouped, half, 0)
+                deal(on_vector, do_raw[:, :, g * K_PASS : (g + 1) * K_PASS], grouped, half, 0)
             mx = mx_tiles("do%d" % g, K_PASS)
             quantize(mx, E5M2, grouped, 0, K_PASS)
             return mx
 
         do_mx0 = quantize_do(False, 0)
+        do_mx1 = quantize_do(False, 1)
         v_grp = new_grouped()
         for j in range(PACK):
             gather(v_grp, v_planes, j)
         v_mx = mx_tiles("v", N)
         quantize(v_mx, E4M3, v_grp, 0, N)
-        do_mx1 = quantize_do(True, 1)
-        flat0 = gated_dp(0, do_mx0, v_mx)
-        flat1 = gated_dp(1, do_mx1, v_mx)
-        gdp0 = [weave_dp(False, flat0, 0, "gdp0_0"), None, None, None]
-        gdp1 = [weave_dp(False, flat1, c, "gdp1_%d" % c) for c in range(4)]
+        gdp0 = gated_dp(0, do_mx0, v_mx)
+        gdp1 = gated_dp(1, do_mx1, v_mx)
         k_grp = new_grouped()
-        for j in range(3):
+        for j in range(PACK):
             gather(k_grp, k_planes, j)
-            gdp0[3 - j] = weave_dp(True, flat0, 3 - j, "k%d" % j)
-        gather(k_grp, k_planes, 3)
         k_mx = mx_tiles("k", N)
         quantize(k_mx, E4M3, k_grp, 0, N)
 
@@ -225,11 +211,11 @@ def tile_attend_gat_pl_k_kernel(tc, qT, kT, vT, doT, rw, qm, offs, out_0, out_1,
             deal_qm(g, 1, qm_grp_b)
         ds_block(0, q_mx1, k_mx, gdp1, ds_grp1)
         ds_block(1, q_mx1, k_mx, gdp1, ds_grp1)
-        codes_a0 = keep.tile([P, 256], U32, name="gdp1_1", align_bytes=64)
+        codes_a0 = keep.tile([P, 256], U32, name="codes_a0", align_bytes=64)
         qm_a = [quantize_qm(codes_a0[:], scales_a[:, 0, :], qm_grp_a[:, 0, :])]
         ds_block(2, q_mx1, k_mx, gdp1, ds_grp1)
         quantize(ds_mx1, E5M2, ds_grp1, 0, 256)
-        codes_a1 = keep.tile([P, 256], U32, name="gdp1_2", align_bytes=64)
+        codes_a1 = keep.tile([P, 256], U32, name="codes_a1", align_bytes=64)
         qm_a.append(quantize_qm(codes_a1[:], scales_a[:, 1, :], qm_grp_a[:, 1, :]))
         ds_block(3, q_mx1, k_mx, gdp1, ds_grp1)
         quantize(ds_mx1, E5M2, ds_grp1, 256, 128)

@@ -35,7 +35,6 @@ def tile_attend_gat_pl_k_kernel(tc, qT, kT, vT, doT, rw, qm, offs, out_0, out_1,
         ps_dk = ctx.enter_context(tc.psum_pool(name="ps_dk", bufs=2))
 
         offsets = keep.tile([P, N // 16], U16, name="offsets")
-        nc.sync.dma_start(offsets[:], offs)
 
         def load_pool(src, name):
             planes = []
@@ -52,6 +51,7 @@ def tile_attend_gat_pl_k_kernel(tc, qT, kT, vT, doT, rw, qm, offs, out_0, out_1,
             return raw
 
         do_raw = load_raw(doT[0], "do_raw")
+        nc.sync.dma_start(offsets[:], offs)
         gate = keep.tile([P, PASSES, PACK], F32, name="gate")
         nc.scalar.dma_start(gate[:], rw[0].rearrange("(g p j) o -> p g (j o)", g=PASSES, j=PACK))
         v_planes = load_pool(vT, "v")
@@ -120,6 +120,19 @@ def tile_attend_gat_pl_k_kernel(tc, qT, kT, vT, doT, rw, qm, offs, out_0, out_1,
                 nc.scalar.activation(flat[:, j, :], bank[:], ACT.Copy, scale=gate2[:, g, j : j + 1])
             return flat
 
+        def unwoven(flat, c):
+            return flat[:, :, c * BLOCK : (c + 1) * BLOCK].rearrange("p j n -> p n j")
+
+        def weave_dp(on_vector, flat, c, name):
+            woven = keep.tile([P, BLOCK, PACK], F32, name=name, align_bytes=64)
+            src = flat[:, :, c * BLOCK : (c + 1) * BLOCK].rearrange("p j (n i) -> p n j i", i=2)
+            dst = woven[:].rearrange("p (n i) j -> p n j i", i=2)
+            if on_vector:
+                nc.vector.tensor_copy(dst, src)
+            else:
+                nc.scalar.copy(dst, src)
+            return woven[:]
+
         def ds_block(c, q_mx, k_mx, gdp, ds_grouped):
             bank = ps_dp.tile([P, PACK, BLOCK], F32, name="dp")
             for j in (2, 3, 0, 1):
@@ -128,7 +141,7 @@ def tile_attend_gat_pl_k_kernel(tc, qT, kT, vT, doT, rw, qm, offs, out_0, out_1,
                 out=ds_grouped[:, PACK * c * BLOCK : PACK * (c + 1) * BLOCK].rearrange("p (n j) -> p n j", j=PACK),
                 in0=bank[:].rearrange("p j n -> p n j"),
                 scalar=0.0,
-                in1=gdp[:, :, c * BLOCK : (c + 1) * BLOCK].rearrange("p j n -> p n j"),
+                in1=gdp[c],
                 op0=ALU.max,
                 op1=ALU.mult,
             )
@@ -148,11 +161,15 @@ def tile_attend_gat_pl_k_kernel(tc, qT, kT, vT, doT, rw, qm, offs, out_0, out_1,
             gather(v_grp, v_planes, j)
         v_mx = mx_tiles("v", N)
         quantize(v_mx, E4M3, v_grp, 0, N)
-        gdp0 = gated_dp(0, do_mx0, v_mx)
-        gdp1 = gated_dp(1, do_mx1, v_mx)
+        flat0 = gated_dp(0, do_mx0, v_mx)
+        flat1 = gated_dp(1, do_mx1, v_mx)
+        gdp0 = [unwoven(flat0, c) for c in range(4)]
+        gdp1 = [weave_dp(False, flat1, c, "gdp1_%d" % c) for c in range(4)]
         k_grp = new_grouped()
         for j in range(PACK):
             gather(k_grp, k_planes, j)
+            if j in (1, 2):
+                gdp0[j] = weave_dp(True, flat0, j, "k%d" % j)
         k_mx = mx_tiles("k", N)
         quantize(k_mx, E4M3, k_grp, 0, N)
 
@@ -194,35 +211,29 @@ def tile_attend_gat_pl_k_kernel(tc, qT, kT, vT, doT, rw, qm, offs, out_0, out_1,
         ds_grp1 = keep.tile([P, K_PASS * PACK], BF16, name="ds_grp1", align_bytes=64)
         ds_mx1 = mx_tiles("ds1", N)
 
-        def deal_qm(g, h, grouped):
-            dst = grouped[:, g, :].rearrange("p (t m j) -> p m j t", t=2, j=PACK)
-            src = qm_raw[g][:].rearrange("p j (m t) -> p m j t", t=PACK)[:, :, :, 2 * h : 2 * h + 2]
-            nc.scalar.copy(dst, src)
+        def deal_qm(g, h):
+            grouped = keep.tile([P, 1024], BF16, name="qm_grp%d_%d" % (g, h), align_bytes=64)
+            deal_half(False, qm_raw[g][:], grouped[:], h, 0)
+            return grouped
 
-        def quantize_qm(codes, scales, grouped):
-            nc.vector.quantize_mx(out=codes.bitcast(E4M3), scales=scales, in_=grouped)
+        def quantize_qm(grouped, codes_name, scales_name):
+            codes = keep.tile([P, 256], U32, name=codes_name, align_bytes=64)
+            scales = keep.tile([P, 256], U8, name=scales_name, align_bytes=64)
+            quantize((codes, scales), E4M3, grouped, 0, 256)
             return codes, scales
 
-        qm_grp_a = keep.tile([P, PASSES, 1024], BF16, name="qm_grp_a", align_bytes=64)
-        qm_grp_b = grp.tile([P, PASSES, 1024], BF16, name="grouped", align_bytes=64)
-        scales_a = keep.tile([P, PASSES, 256], U8, name="scales_a", align_bytes=64)
-        for g in range(PASSES):
-            deal_qm(g, 0, qm_grp_a)
-            deal_qm(g, 1, qm_grp_b)
+        qm_grp = [[deal_qm(g, h) for h in range(2)] for g in range(PASSES)]
         ds_block(0, q_mx1, k_mx, gdp1, ds_grp1)
         ds_block(1, q_mx1, k_mx, gdp1, ds_grp1)
-        codes_a0 = keep.tile([P, 256], U32, name="codes_a0", align_bytes=64)
-        qm_a = [quantize_qm(codes_a0[:], scales_a[:, 0, :], qm_grp_a[:, 0, :])]
+        qm_a = [quantize_qm(qm_grp[0][0], "qm_a0_codes", "qm_a0_scales")]
         ds_block(2, q_mx1, k_mx, gdp1, ds_grp1)
         quantize(ds_mx1, E5M2, ds_grp1, 0, 256)
-        codes_a1 = keep.tile([P, 256], U32, name="codes_a1", align_bytes=64)
-        qm_a.append(quantize_qm(codes_a1[:], scales_a[:, 1, :], qm_grp_a[:, 1, :]))
         ds_block(3, q_mx1, k_mx, gdp1, ds_grp1)
         quantize(ds_mx1, E5M2, ds_grp1, 256, 128)
+        qm_a.append(quantize_qm(qm_grp[1][0], "gdp1_3", "qm_a1_scales"))
         quantize(ds_mx1, E5M2, ds_grp1, 384, 128)
-        codes_b = keep.tile([P, PASSES, 256], U32, name="ds_grp1", align_bytes=64)
-        scales_b = keep.tile([P, PASSES, 256], U8, name="qm_grp_a", align_bytes=64)
-        qm_b = [quantize_qm(codes_b[:, g, :], scales_b[:, g, :], qm_grp_b[:, g, :]) for g in range(PASSES)]
+        qm_b = [quantize_qm(qm_grp[0][1], "ds_grp1", "qm_b0_scales")]
+        qm_b.append(quantize_qm(qm_grp[1][1], "qm_b1_codes", "qm_grp1_0"))
         ds_mx = [ds_mx0, ds_mx1]
 
         out_rows = out_0.rearrange("(p t) c -> p t c", t=PACK)

@@ -46,7 +46,7 @@ def tile_attend_gat_pl_k_kernel(tc, qT, kT, vT, doT, rw, qm, offs, out_0, out_1,
             return planes
 
         def load_raw(src, name):
-            raw = raws.tile([P, PACK, src.shape[1]], F32, name=name)
+            raw = raws.tile([P, PACK, src.shape[1]], F32, name=name, align_bytes=64)
             nc.sync.dma_start(raw[:], src.rearrange("(p j) c -> p j c", j=PACK))
             return raw
 
@@ -120,11 +120,8 @@ def tile_attend_gat_pl_k_kernel(tc, qT, kT, vT, doT, rw, qm, offs, out_0, out_1,
                 nc.scalar.activation(flat[:, j, :], bank[:], ACT.Copy, scale=gate2[:, g, j : j + 1])
             return flat
 
-        def unwoven(flat, c):
-            return flat[:, :, c * BLOCK : (c + 1) * BLOCK].rearrange("p j n -> p n j")
-
-        def weave_dp(on_vector, flat, c, name):
-            woven = keep.tile([P, BLOCK, PACK], F32, name=name, align_bytes=64)
+        def weave_dp(on_vector, flat, c, name, pool=keep):
+            woven = pool.tile([P, BLOCK, PACK], F32, name=name, align_bytes=64)
             src = flat[:, :, c * BLOCK : (c + 1) * BLOCK].rearrange("p j (n i) -> p n j i", i=2)
             dst = woven[:].rearrange("p (n i) j -> p n j i", i=2)
             if on_vector:
@@ -163,15 +160,15 @@ def tile_attend_gat_pl_k_kernel(tc, qT, kT, vT, doT, rw, qm, offs, out_0, out_1,
         quantize(v_mx, E4M3, v_grp, 0, N)
         flat0 = gated_dp(0, do_mx0, v_mx)
         flat1 = gated_dp(1, do_mx1, v_mx)
-        gdp0 = [unwoven(flat0, c) for c in range(4)]
-        gdp1 = [weave_dp(False, flat1, c, "gdp1_%d" % c) for c in range(4)]
+        gdp0 = [weave_dp(False, flat0, 0, "gdp0_0"), None, None, weave_dp(False, flat0, 3, "gdp0_3")]
+        gdp1 = [weave_dp(False, flat1, c, "gdp1_%d" % c) for c in range(2)]
         k_grp = new_grouped()
         for j in range(PACK):
             gather(k_grp, k_planes, j)
             if j in (1, 2):
                 gdp0[j] = weave_dp(True, flat0, j, "k%d" % j)
         k_mx = mx_tiles("k", N)
-        quantize(k_mx, E4M3, k_grp, 0, N)
+        quantize(k_mx, E4M3, k_grp, 0, BLOCK)
 
         def deal_half(on_vector, raw, grouped, half, first):
             count = raw.shape[2] // PACK
@@ -190,11 +187,14 @@ def tile_attend_gat_pl_k_kernel(tc, qT, kT, vT, doT, rw, qm, offs, out_0, out_1,
         deal_half(False, q_raw[1][:], q_grp0[0][:], 0, 64)
         for half in (1, 0):
             quantize(q_mx0[half], E4M3, q_grp0[half], 0, 256)
+        quantize(k_mx, E4M3, k_grp, BLOCK, BLOCK)
+        quantize(k_mx, E4M3, k_grp, 2 * BLOCK, 2 * BLOCK)
 
         q_grp1 = new_grouped()
         for i in range(2):
             for half in range(2):
                 deal(False, q_raw[2 + i][:], q_grp1, half, 64 * i)
+        gdp1.extend(weave_dp(False, flat1, c, "q_raw%d" % c, raws) for c in range(2, 4))
 
         ds_grp0 = new_grouped()
         ds_mx0 = mx_tiles("ds0", N)
@@ -216,24 +216,28 @@ def tile_attend_gat_pl_k_kernel(tc, qT, kT, vT, doT, rw, qm, offs, out_0, out_1,
             deal_half(False, qm_raw[g][:], grouped[:], h, 0)
             return grouped
 
-        def quantize_qm(grouped, codes_name, scales_name):
-            codes = keep.tile([P, 256], U32, name=codes_name, align_bytes=64)
-            scales = keep.tile([P, 256], U8, name=scales_name, align_bytes=64)
-            quantize((codes, scales), E4M3, grouped, 0, 256)
-            return codes, scales
+        def quantize_qm(grouped, first, count, codes_name, scales_name, pool=keep):
+            codes = pool.tile([P, count], U32, name=codes_name, align_bytes=64)
+            scales = keep.tile([P, count], U8, name=scales_name, align_bytes=64)
+            nc.vector.quantize_mx(
+                out=codes[:].bitcast(E4M3), scales=scales[:], in_=grouped[:, PACK * first : PACK * (first + count)]
+            )
+            return [(codes[:, i : i + P], scales[:, i : i + P]) for i in range(0, count, P)]
 
         qm_grp = [[deal_qm(g, h) for h in range(2)] for g in range(PASSES)]
         ds_block(0, q_mx1, k_mx, gdp1, ds_grp1)
         ds_block(1, q_mx1, k_mx, gdp1, ds_grp1)
-        qm_a = [quantize_qm(qm_grp[0][0], "qm_a0_codes", "qm_a0_scales")]
+        qm_mx = [quantize_qm(qm_grp[0][0], 0, P, "qm00_codes", "qm00_scales")]
         ds_block(2, q_mx1, k_mx, gdp1, ds_grp1)
         quantize(ds_mx1, E5M2, ds_grp1, 0, 256)
         ds_block(3, q_mx1, k_mx, gdp1, ds_grp1)
         quantize(ds_mx1, E5M2, ds_grp1, 256, 128)
-        qm_a.append(quantize_qm(qm_grp[1][0], "gdp1_3", "qm_a1_scales"))
+        qm_mx.append(quantize_qm(qm_grp[1][0], 0, P, "q_raw3", "qm10_scales", raws))
         quantize(ds_mx1, E5M2, ds_grp1, 384, 128)
-        qm_b = [quantize_qm(qm_grp[0][1], "ds_grp1", "qm_b0_scales")]
-        qm_b.append(quantize_qm(qm_grp[1][1], "qm_b1_codes", "qm_grp1_0"))
+        qm_mx[0].extend(quantize_qm(qm_grp[0][0], P, P, "ds_grp1", "qm01_scales"))
+        qm_mx[1].extend(quantize_qm(qm_grp[1][0], P, P, "qm11_codes", "qm_grp0_0"))
+        qm_mx[0].extend(quantize_qm(qm_grp[0][1], 0, 2 * P, "qm02_codes", "qm_grp1_0"))
+        qm_mx[1].extend(quantize_qm(qm_grp[1][1], 0, 2 * P, "qm12_codes", "qm_grp0_1"))
         ds_mx = [ds_mx0, ds_mx1]
 
         out_rows = out_0.rearrange("(p t) c -> p t c", t=PACK)
@@ -250,10 +254,10 @@ def tile_attend_gat_pl_k_kernel(tc, qT, kT, vT, doT, rw, qm, offs, out_0, out_1,
             for c in range(2):
                 round_pairs(t, c)
 
-        def dk_plane(t, qm_mx):
+        def dk_plane(t):
             bank = ps_dk.tile([P, N], F32, name="dk")
             for g in range(PASSES):
-                matmul(bank[:], qm_mx[g], E4M3, place(t % 2), ds_mx[g], E5M2, slice(0, N), g == 0, g == PASSES - 1)
+                matmul(bank[:], qm_mx[g][t], E4M3, slice(0, P), ds_mx[g], E5M2, slice(0, N), g == 0, g == PASSES - 1)
             dk = keep.tile([P, N], F32, name="dk_sb%d" % t, align_bytes=64)
             pieces = 2 if t == 0 else 1
             for i in range(pieces):
@@ -268,11 +272,11 @@ def tile_attend_gat_pl_k_kernel(tc, qT, kT, vT, doT, rw, qm, offs, out_0, out_1,
                 nc.vector.tensor_copy(windows[t][:].indirect(offsets[:, first // 16 : last // 16]), dk[:, first:last])
             nc.sync.dma_start(out_rows[:, t, :], windows[t][:])
 
-        dk0 = dk_plane(0, qm_a)
-        dk1 = dk_plane(1, qm_a)
+        dk0 = dk_plane(0)
+        dk1 = dk_plane(1)
         scatter(0, dk0)
-        dk2 = dk_plane(2, qm_b)
-        dk3 = dk_plane(3, qm_b)
+        dk2 = dk_plane(2)
+        dk3 = dk_plane(3)
         round_plane(0)
         scatter(1, dk1)
         round_plane(1)
@@ -281,7 +285,7 @@ def tile_attend_gat_pl_k_kernel(tc, qT, kT, vT, doT, rw, qm, offs, out_0, out_1,
         scatter(3, dk3)
 
         y_codes = [keep.tile([P, CHUNK], U32, name="y_codes%d" % c, align_bytes=64) for c in range(CHUNKS)]
-        y_scales = keep.tile([P, T], U8, name="y_scales", align_bytes=64)
+        y_scales = keep.tile([P, CHUNK], U8, name="y_scales", align_bytes=64)
         words_out = out_1[0].rearrange("p t l -> p (t l)").bitcast(I32)
 
         def weave_pairs(c):
@@ -299,7 +303,8 @@ def tile_attend_gat_pl_k_kernel(tc, qT, kT, vT, doT, rw, qm, offs, out_0, out_1,
 
         def finish(c, grouped):
             span = slice(c * CHUNK, (c + 1) * CHUNK)
-            nc.vector.quantize_mx(out=y_codes[c][:].bitcast(E4M3), scales=y_scales[:, span], in_=grouped[:])
+            for half in range(2):
+                quantize((y_codes[c], y_scales[4 * c :, :]), E4M3, grouped, 256 * half, 256)
             nc.sync.dma_start(words_out[:, span], y_codes[c][:].bitcast(I32))
 
         for c in range(2):
@@ -312,11 +317,10 @@ def tile_attend_gat_pl_k_kernel(tc, qT, kT, vT, doT, rw, qm, offs, out_0, out_1,
         y0 = weave_planes(0)
         y1 = weave_planes(1)
         finish(0, y0)
-        finish(2, y2)
         finish(1, y1)
+        finish(2, y2)
         finish(3, y3)
         for quad in range(4):
             queue = nc.scalar if quad % 2 else nc.sync
-            queue.dma_start(
-                out_2[0][4 * quad : 4 * quad + 4, :].bitcast(I32), y_scales[32 * quad : 32 * quad + 4, :].bitcast(I32)
-            )
+            rows = out_2[0][4 * quad : 4 * quad + 4, :].bitcast(I32).rearrange("r (c x) -> c r x", c=CHUNKS)
+            queue.dma_start(rows, y_scales[32 * quad : 32 * quad + 16, :].bitcast(I32))

@@ -241,18 +241,30 @@ def tile_attend_gat_pl_k_kernel(tc, qT, kT, vT, doT, rw, qm, offs, out_0, out_1,
         ds_mx = [ds_mx0, ds_mx1]
 
         out_rows = out_0.rearrange("(p t) c -> p t c", t=PACK)
-        split = T // 2
-        rounded = keep.tile([P, PACK, split], BF16, name="k3", align_bytes=64)
-        pairs = [grp.tile([P, PACK * CHUNK], BF16, name="grouped", align_bytes=64) for c in range(2)]
+        pairs = [grp.tile([P, PACK * CHUNK], BF16, name="grouped", align_bytes=64) for c in range(CHUNKS - 1)]
+        y3 = new_grouped()
+
+        def round_lane(t):
+            nc.scalar.copy(y3[:].rearrange("p (n j) -> p n j", j=PACK)[:, :, t], tokens(t, 3))
+
+        def pair_place(t, c):
+            return pairs[c][:].rearrange("p (u n e) -> p u n e", u=2, e=2)[:, t // 2]
+
+        def tokens(t, c):
+            return windows[t][:, c * CHUNK : (c + 1) * CHUNK]
 
         def round_pairs(t, c):
-            dst = pairs[c][:].rearrange("p (u n e) -> p u n e", u=2, e=2)[:, t // 2, :, t % 2]
-            nc.scalar.copy(dst, windows[t][:, split + c * CHUNK : split + (c + 1) * CHUNK])
+            nc.scalar.copy(pair_place(t, c)[:, :, t % 2], tokens(t, c))
 
         def round_plane(t):
-            nc.scalar.copy(rounded[:, t, :], windows[t][:, 0:split])
             for c in range(2):
-                round_pairs(t, c)
+                if t == 2:
+                    dst, src = pair_place(t, c), tokens(t, c).unsqueeze(2).to_broadcast([P, CHUNK, 2])
+                else:
+                    dst, src = pair_place(t, c)[:, :, t % 2], tokens(t, c)
+                nc.gpsimd.tensor_scalar(dst, src, 1.0, -0.0, ALU.mult, ALU.add)
+            round_pairs(t, 2)
+            round_lane(t)
 
         def dk_plane(t):
             bank = ps_dk.tile([P, N], F32, name="dk")
@@ -288,17 +300,14 @@ def tile_attend_gat_pl_k_kernel(tc, qT, kT, vT, doT, rw, qm, offs, out_0, out_1,
         y_scales = keep.tile([P, CHUNK], U8, name="y_scales", align_bytes=64)
         words_out = out_1[0].rearrange("p t l -> p (t l)").bitcast(I32)
 
-        def weave_pairs(c):
+        def weave_pairs(on_vector, c):
             grouped = new_grouped()
             dst = grouped[:].bitcast(F32).rearrange("p (n u) -> p n u", u=2)
-            nc.scalar.copy(dst, pairs[c][:].bitcast(F32).rearrange("p (u n) -> p n u", u=2))
-            return grouped
-
-        def weave_planes(c):
-            grouped = new_grouped()
-            dst = grouped[:].rearrange("p (n i t) -> p n t i", i=4, t=PACK)
-            src = rounded[:, :, c * CHUNK : (c + 1) * CHUNK].rearrange("p t (n i) -> p n t i", i=4)
-            nc.vector.tensor_copy(dst, src)
+            src = pairs[c][:].bitcast(F32).rearrange("p (u n) -> p n u", u=2)
+            if on_vector:
+                nc.vector.tensor_copy(dst, src)
+            else:
+                nc.scalar.copy(dst, src)
             return grouped
 
         def finish(c, grouped):
@@ -308,18 +317,16 @@ def tile_attend_gat_pl_k_kernel(tc, qT, kT, vT, doT, rw, qm, offs, out_0, out_1,
             nc.sync.dma_start(words_out[:, span], y_codes[c][:].bitcast(I32))
 
         for c in range(2):
-            span = slice(c * CHUNK, (c + 1) * CHUNK)
-            nc.vector.tensor_copy(rounded[:, 3, span], windows[3][:, span])
-        round_pairs(3, 0)
-        y2 = weave_pairs(0)
-        round_pairs(3, 1)
-        y3 = weave_pairs(1)
-        y0 = weave_planes(0)
-        y1 = weave_planes(1)
+            nc.vector.tensor_copy(pair_place(3, c)[:, :, 1], tokens(3, c))
+        round_lane(3)
+        round_pairs(3, 2)
+        y2 = weave_pairs(False, 2)
+        y0 = weave_pairs(True, 0)
+        y1 = weave_pairs(True, 1)
         finish(0, y0)
         finish(1, y1)
-        finish(2, y2)
         finish(3, y3)
+        finish(2, y2)
         for quad in range(4):
             queue = nc.scalar if quad % 2 else nc.sync
             rows = out_2[0][4 * quad : 4 * quad + 4, :].bitcast(I32).rearrange("r (c x) -> c r x", c=CHUNKS)

@@ -209,7 +209,10 @@ def tile_attend_gat_pl_k_kernel(tc, qT, kT, vT, doT, rw, qm, offs, out_0, out_1,
         q_mx1 = [(q_mx1[0][:, 256 * half : 256 * (half + 1)], q_mx1[1][:, 256 * half : 256 * (half + 1)]) for half in range(2)]
 
         ds_grp1 = keep.tile([P, K_PASS * PACK], BF16, name="ds_grp1", align_bytes=64)
-        ds_mx1 = mx_tiles("ds1", N)
+        ds_mx1 = (
+            keep.tile([P, N], U32, name="v2", align_bytes=64),
+            keep.tile([P, N], U8, name="v3", align_bytes=64),
+        )
 
         def deal_qm(g, h):
             grouped = keep.tile([P, 1024], BF16, name="qm_grp%d_%d" % (g, h), align_bytes=64)
@@ -241,8 +244,6 @@ def tile_attend_gat_pl_k_kernel(tc, qT, kT, vT, doT, rw, qm, offs, out_0, out_1,
         ds_mx = [ds_mx0, ds_mx1]
 
         out_rows = out_0.rearrange("(p t) c -> p t c", t=PACK)
-        pairs = [grp.tile([P, PACK * CHUNK], BF16, name="grouped", align_bytes=64) for c in range(CHUNKS - 1)]
-        y3 = new_grouped()
 
         def round_lane(t):
             nc.scalar.copy(y3[:].rearrange("p (n j) -> p n j", j=PACK)[:, :, t], tokens(t, 3))
@@ -253,12 +254,12 @@ def tile_attend_gat_pl_k_kernel(tc, qT, kT, vT, doT, rw, qm, offs, out_0, out_1,
         def tokens(t, c):
             return windows[t][:, c * CHUNK : (c + 1) * CHUNK]
 
-        def round_pairs(t, c):
-            nc.scalar.copy(pair_place(t, c)[:, :, t % 2], tokens(t, c))
+        def round_pairs(t, c, span=slice(0, CHUNK)):
+            nc.scalar.copy(pair_place(t, c)[:, span, t % 2], tokens(t, c)[:, span])
 
         def round_plane(t):
             for c in range(2):
-                if t == 2:
+                if t == 0:
                     dst, src = pair_place(t, c), tokens(t, c).unsqueeze(2).to_broadcast([P, CHUNK, 2])
                 else:
                     dst, src = pair_place(t, c)[:, :, t % 2], tokens(t, c)
@@ -285,47 +286,61 @@ def tile_attend_gat_pl_k_kernel(tc, qT, kT, vT, doT, rw, qm, offs, out_0, out_1,
             nc.sync.dma_start(out_rows[:, t, :], windows[t][:])
 
         dk0 = dk_plane(0)
-        dk1 = dk_plane(1)
-        scatter(0, dk0)
         dk2 = dk_plane(2)
+        scatter(0, dk0)
         dk3 = dk_plane(3)
+        dk1 = dk_plane(1)
+        pairs = [new_grouped(), new_grouped(), keep.tile([P, PACK * CHUNK], BF16, name="v3", align_bytes=64)]
+        y3 = keep.tile([P, PACK * CHUNK], BF16, name="v2", align_bytes=64)
         round_plane(0)
-        scatter(1, dk1)
-        round_plane(1)
         scatter(2, dk2)
         round_plane(2)
         scatter(3, dk3)
+        round_plane(3)
+        scatter(1, dk1)
 
-        y_codes = [keep.tile([P, CHUNK], U32, name="y_codes%d" % c, align_bytes=64) for c in range(CHUNKS)]
+        first_codes = keep.tile([P, 2 * CHUNK], U32, name="y_codes01", align_bytes=64)
+        y_codes = [first_codes[:, 0:CHUNK], first_codes[:, CHUNK : 2 * CHUNK]]
+        y_codes.extend(keep.tile([P, CHUNK], U32, name="y_codes%d" % c, align_bytes=64)[:] for c in range(2, CHUNKS))
         y_scales = keep.tile([P, CHUNK], U8, name="y_scales", align_bytes=64)
         words_out = out_1[0].rearrange("p t l -> p (t l)").bitcast(I32)
 
-        def weave_pairs(on_vector, c):
-            grouped = new_grouped()
+        def weave_pairs(on_vector, c, span, grouped):
             dst = grouped[:].bitcast(F32).rearrange("p (n u) -> p n u", u=2)
-            src = pairs[c][:].bitcast(F32).rearrange("p (u n) -> p n u", u=2)
+            src = pairs[c][:].bitcast(F32).rearrange("p (u n) -> p n u", u=2)[:, span]
             if on_vector:
                 nc.vector.tensor_copy(dst, src)
             else:
                 nc.scalar.copy(dst, src)
             return grouped
 
-        def finish(c, grouped):
+        def finish(c, halves):
             span = slice(c * CHUNK, (c + 1) * CHUNK)
             for half in range(2):
-                quantize((y_codes[c], y_scales[4 * c :, :]), E4M3, grouped, 256 * half, 256)
-            nc.sync.dma_start(words_out[:, span], y_codes[c][:].bitcast(I32))
+                cols = slice(256 * half, 256 * (half + 1))
+                nc.vector.quantize_mx(out=y_codes[c][:, cols].bitcast(E4M3), scales=y_scales[4 * c :, cols], in_=halves[half])
+            if c == 1:
+                nc.sync.dma_start(words_out[:, 0 : 2 * CHUNK], first_codes[:].bitcast(I32))
+            elif c > 1:
+                nc.sync.dma_start(words_out[:, span], y_codes[c].bitcast(I32))
+
+        def halves_of(grouped):
+            return [grouped[:, 1024 * half : 1024 * (half + 1)] for half in range(2)]
 
         for c in range(2):
-            nc.vector.tensor_copy(pair_place(3, c)[:, :, 1], tokens(3, c))
-        round_lane(3)
-        round_pairs(3, 2)
-        y2 = weave_pairs(False, 2)
-        y0 = weave_pairs(True, 0)
-        y1 = weave_pairs(True, 1)
-        finish(0, y0)
-        finish(1, y1)
-        finish(3, y3)
+            nc.vector.tensor_copy(pair_place(1, c)[:, :, 1], tokens(1, c))
+        round_lane(1)
+        y2 = []
+        for half in range(2):
+            span = slice(256 * half, 256 * (half + 1))
+            round_pairs(1, 2, span)
+            grouped = keep.tile([P, 1024], BF16, name="k%d" % (1 + half), align_bytes=64)
+            y2.append(weave_pairs(False, 2, span, grouped)[:])
+        y0 = weave_pairs(True, 0, slice(0, CHUNK), new_grouped())
+        y1 = weave_pairs(True, 1, slice(0, CHUNK), new_grouped())
+        finish(0, halves_of(y0))
+        finish(1, halves_of(y1))
+        finish(3, halves_of(y3))
         finish(2, y2)
         for quad in range(4):
             queue = nc.scalar if quad % 2 else nc.sync

@@ -299,9 +299,7 @@ def tile_attend_gat_pl_k_kernel(tc, qT, kT, vT, doT, rw, qm, offs, out_0, out_1,
         round_plane(3)
         scatter(1, dk1)
 
-        first_codes = keep.tile([P, 2 * CHUNK], U32, name="y_codes01", align_bytes=64)
-        y_codes = [first_codes[:, 0:CHUNK], first_codes[:, CHUNK : 2 * CHUNK]]
-        y_codes.extend(keep.tile([P, CHUNK], U32, name="y_codes%d" % c, align_bytes=64)[:] for c in range(2, CHUNKS))
+        y_codes = [keep.tile([P, CHUNK], U32, name="y_codes%d" % c, align_bytes=64)[:] for c in range(CHUNKS)]
         y_scales = keep.tile([P, CHUNK], U8, name="y_scales", align_bytes=64)
         words_out = out_1[0].rearrange("p t l -> p (t l)").bitcast(I32)
 
@@ -319,10 +317,7 @@ def tile_attend_gat_pl_k_kernel(tc, qT, kT, vT, doT, rw, qm, offs, out_0, out_1,
             for half in range(2):
                 cols = slice(256 * half, 256 * (half + 1))
                 nc.vector.quantize_mx(out=y_codes[c][:, cols].bitcast(E4M3), scales=y_scales[4 * c :, cols], in_=halves[half])
-            if c == 1:
-                nc.sync.dma_start(words_out[:, 0 : 2 * CHUNK], first_codes[:].bitcast(I32))
-            elif c > 1:
-                nc.sync.dma_start(words_out[:, span], y_codes[c].bitcast(I32))
+            nc.sync.dma_start(words_out[:, span], y_codes[c].bitcast(I32))
 
         def halves_of(grouped):
             return [grouped[:, 1024 * half : 1024 * (half + 1)] for half in range(2)]
@@ -343,6 +338,5 @@ def tile_attend_gat_pl_k_kernel(tc, qT, kT, vT, doT, rw, qm, offs, out_0, out_1,
         finish(3, halves_of(y3))
         finish(2, y2)
         for quad in range(4):
-            queue = nc.scalar if quad % 2 else nc.sync
             rows = out_2[0][4 * quad : 4 * quad + 4, :].bitcast(I32).rearrange("r (c x) -> c r x", c=CHUNKS)
-            queue.dma_start(rows, y_scales[32 * quad : 32 * quad + 16, :].bitcast(I32))
+            nc.sync.dma_start(rows, y_scales[32 * quad : 32 * quad + 16, :].bitcast(I32))

@@ -20,9 +20,16 @@ P = 128
 PACK = 4
 K_PASS = P * PACK
 PASSES = R // K_PASS
+HALF = K_PASS // 2
+BAND = 16
 BLOCK = 128
+BLOCKS = N // BLOCK
 CHUNK = 512
 CHUNKS = T // CHUNK
+SCALE_ROWS = 4
+GROUPED_BUFFERS = 8
+SLOT_BANKS = 6
+RESULT_BANKS = 2
 
 
 def tile_attend_gat_pl_k_kernel(tc, qT, kT, vT, doT, rw, qm, offs, out_0, out_1, out_2):
@@ -30,18 +37,18 @@ def tile_attend_gat_pl_k_kernel(tc, qT, kT, vT, doT, rw, qm, offs, out_0, out_1,
     with ExitStack() as ctx:
         keep = ctx.enter_context(tc.tile_pool(name="keep", bufs=1))
         raws = ctx.enter_context(tc.tile_pool(name="raws", bufs=1))
-        grp = ctx.enter_context(tc.tile_pool(name="grp", bufs=8))
-        ps_dp = ctx.enter_context(tc.psum_pool(name="ps_dp", bufs=6))
-        ps_dk = ctx.enter_context(tc.psum_pool(name="ps_dk", bufs=2))
+        grp = ctx.enter_context(tc.tile_pool(name="grp", bufs=GROUPED_BUFFERS))
+        ps_slots = ctx.enter_context(tc.psum_pool(name="ps_dp", bufs=SLOT_BANKS))
+        ps_result = ctx.enter_context(tc.psum_pool(name="ps_dk", bufs=RESULT_BANKS))
 
-        offsets = keep.tile([P, N // 16], U16, name="offsets")
+        offsets = keep.tile([P, N // BAND], U16, name="offsets")
 
-        def load_pool(src, name):
+        def load_planes(src, name):
             planes = []
             rows = src.rearrange("(p j) t -> p j t", j=PACK)
-            for j in range(PACK):
-                plane = keep.tile([P, T], F32, name="%s%d" % (name, j), align_bytes=64)
-                nc.sync.dma_start(plane[:], rows[:, j, :])
+            for lane in range(PACK):
+                plane = keep.tile([P, T], F32, name="%s%d" % (name, lane), align_bytes=64)
+                nc.sync.dma_start(plane[:], rows[:, lane, :])
                 planes.append(plane)
             return planes
 
@@ -52,25 +59,34 @@ def tile_attend_gat_pl_k_kernel(tc, qT, kT, vT, doT, rw, qm, offs, out_0, out_1,
 
         do_raw = load_raw(doT[0], "do_raw")
         nc.sync.dma_start(offsets[:], offs)
-        gate = keep.tile([P, PASSES, PACK], F32, name="gate")
-        nc.scalar.dma_start(gate[:], rw[0].rearrange("(g p j) o -> p g (j o)", g=PASSES, j=PACK))
-        v_planes = load_pool(vT, "v")
-        k_planes = load_pool(kT, "k")
-        q_raw = [load_raw(qT[0][:, i * 256 : (i + 1) * 256], "q_raw%d" % i) for i in range(4)]
+        gate = keep.tile([P, PASSES, 2 * PACK], F32, name="gate")
+        nc.scalar.dma_start(gate[:, :, 0:PACK], rw[0].rearrange("(g p j) o -> p g (j o)", g=PASSES, j=PACK))
+        v_planes = load_planes(vT, "v")
+        k_planes = load_planes(kT, "k")
+        q_raw = [load_raw(qT[0][:, i * HALF : (i + 1) * HALF], "q_raw%d" % i) for i in range(R // HALF)]
         qm_raw = [load_raw(qm[0][g * K_PASS : (g + 1) * K_PASS, :], "qm_raw%d" % g) for g in range(PASSES)]
 
         windows = []
-        for t in range(PACK):
-            window = keep.tile([P, T], F32, name="window%d" % t)
+        for lane in range(PACK):
+            window = keep.tile([P, T], F32, name="window%d" % lane)
             nc.vector.memset(window[:], 0.0)
             windows.append(window)
 
         gate2 = keep.tile([P, PASSES, PACK], F32, name="gate2")
-        nc.scalar.mul(gate2[:], gate[:], 2.0)
+        nc.scalar.mul(gate2[:], gate[:, :, 0:PACK], 2.0)
 
-        def mx_tiles(name, width):
-            codes = keep.tile([P, width], U32, name=name + "_codes", align_bytes=64)
-            scales = keep.tile([P, width], U8, name=name + "_scales", align_bytes=64)
+        def copy(on_vector, dst, src):
+            if on_vector:
+                nc.vector.tensor_copy(dst, src)
+            else:
+                nc.scalar.copy(dst, src)
+
+        def gpsimd_copy(dst, src):
+            nc.gpsimd.tensor_scalar(dst, src, 1.0, -0.0, ALU.mult, ALU.add)
+
+        def mx_tiles(width, codes_name, scales_name):
+            codes = keep.tile([P, width], U32, name=codes_name, align_bytes=64)
+            scales = keep.tile([P, width], U8, name=scales_name, align_bytes=64)
             return codes, scales
 
         def new_grouped():
@@ -84,19 +100,20 @@ def tile_attend_gat_pl_k_kernel(tc, qT, kT, vT, doT, rw, qm, offs, out_0, out_1,
                 in_=grouped[:, PACK * first : PACK * (first + count)],
             )
 
-        def gather(grouped, planes, j):
+        def gather(grouped, planes, lane):
             words = grouped[:].rearrange("p (n j) -> p n j", j=PACK)
-            nc.vector.tensor_copy(words[:, :, j], planes[j][:].indirect(offsets[:]))
+            nc.vector.tensor_copy(words[:, :, lane], planes[lane][:].indirect(offsets[:]))
 
-        def deal(on_vector, raw, grouped, half, first):
+        def deal(on_vector, raw, dealt, half, first):
             count = raw.shape[2] // PACK
-            dst = grouped[:].rearrange("p (t m j) -> p m j t", t=PACK, j=PACK)
-            dst = dst[:, first : first + count, :, 2 * half : 2 * half + 2]
             src = raw.rearrange("p j (m t) -> p m j t", t=PACK)[:, :, :, 2 * half : 2 * half + 2]
-            if on_vector:
-                nc.vector.tensor_copy(dst, src)
-            else:
-                nc.scalar.copy(dst, src)
+            copy(on_vector, dealt[:, first : first + count], src)
+
+        def dealt_half_of_whole(grouped, half):
+            return grouped[:].rearrange("p (t m j) -> p m j t", t=PACK, j=PACK)[:, :, :, 2 * half : 2 * half + 2]
+
+        def dealt_half_alone(grouped):
+            return grouped[:].rearrange("p (t m j) -> p m j t", t=2, j=PACK)
 
         def matmul(out, lhs, lhs_fmt, lhs_cols, rhs, rhs_fmt, rhs_cols, start, stop):
             nc.tensor.matmul_mx(
@@ -109,134 +126,116 @@ def tile_attend_gat_pl_k_kernel(tc, qT, kT, vT, doT, rw, qm, offs, out_0, out_1,
                 stop=stop,
             )
 
-        def place(j):
-            return slice(j * P, (j + 1) * P)
+        def nth(i, width):
+            return slice(i * width, (i + 1) * width)
 
-        def gated_dp(g, do_mx, v_mx):
-            flat = keep.tile([P, PACK, N], F32, name="v%d" % g, align_bytes=64)
-            for j in range(PACK):
-                bank = ps_dp.tile([P, N], F32, name="dp")
-                matmul(bank[:], do_mx, E5M2, place(j), v_mx, E4M3, slice(0, N), True, True)
-                nc.scalar.activation(flat[:, j, :], bank[:], ACT.Copy, scale=gate2[:, g, j : j + 1])
-            return flat
+        def quantize_do(g):
+            grouped = new_grouped()
+            for half in range(2):
+                deal(False, do_raw[:, :, nth(g, K_PASS)], dealt_half_of_whole(grouped, half), half, 0)
+            mx = mx_tiles(K_PASS, "do%d_codes" % g, "do%d_scales" % g)
+            quantize(mx, E5M2, grouped, 0, K_PASS)
+            return mx
 
-        def weave_dp(on_vector, flat, c, name, pool=keep):
-            woven = pool.tile([P, BLOCK, PACK], F32, name=name, align_bytes=64)
-            src = flat[:, :, c * BLOCK : (c + 1) * BLOCK].rearrange("p j (n i) -> p n j i", i=2)
-            dst = woven[:].rearrange("p (n i) j -> p n j i", i=2)
-            if on_vector:
-                nc.vector.tensor_copy(dst, src)
+        def gated_dp(g):
+            by_lane = keep.tile([P, PACK, N], F32, name="v%d" % g, align_bytes=64)
+            for lane in range(PACK):
+                bank = ps_slots.tile([P, N], F32, name="dp")
+                matmul(bank[:], do_mx[g], E5M2, nth(lane, P), v_mx, E4M3, slice(0, N), True, True)
+                nc.scalar.activation(by_lane[:, lane, :], bank[:], ACT.Copy, scale=gate2[:, g, lane : lane + 1])
+            return by_lane
+
+        def weave_dp(on_gpsimd, g, block, woven):
+            src = dp_by_lane[g][:, :, nth(block, BLOCK)]
+            if on_gpsimd:
+                gpsimd_copy(woven, src.rearrange("p j n -> p n j"))
             else:
-                nc.scalar.copy(dst, src)
-            return woven[:]
+                nc.scalar.copy(woven.rearrange("p (n i) j -> p n j i", i=2), src.rearrange("p j (n i) -> p n j i", i=2))
+            return woven
 
-        def ds_block(c, q_mx, k_mx, gdp, ds_grouped):
-            bank = ps_dp.tile([P, PACK, BLOCK], F32, name="dp")
-            for j in (2, 3, 0, 1):
-                matmul(bank[:, j, :], q_mx[j // 2], E4M3, place(j % 2), k_mx, E4M3, slice(c * BLOCK, (c + 1) * BLOCK), True, True)
+        def new_woven(g, block):
+            return keep.tile([P, BLOCK, PACK], F32, name="gdp%d_%d" % (g, block), align_bytes=64)[:]
+
+        do_mx = [quantize_do(g) for g in range(PASSES)]
+        v_grp = new_grouped()
+        for lane in range(PACK):
+            gather(v_grp, v_planes, lane)
+        v_mx = mx_tiles(N, "v_codes", "v_scales")
+        quantize(v_mx, E4M3, v_grp, 0, N)
+        dp_by_lane = [gated_dp(g) for g in range(PASSES)]
+        dp_blocks0 = [weave_dp(True, 0, block, new_woven(0, block)) for block in range(BLOCKS)]
+        dp_blocks1 = [weave_dp(False, 1, block, new_woven(1, block)) for block in range(BLOCKS // 2)]
+        k_grp = keep.tile([P, N * PACK], BF16, name="k_grp", align_bytes=64)
+        for lane in range(PACK):
+            gather(k_grp, k_planes, lane)
+        k_mx = mx_tiles(N, "k_codes", "k_scales")
+        quantize(k_mx, E4M3, k_grp, 0, BLOCK)
+
+        def ds_block(block, q_mx, dp_blocks, ds_grp):
+            bank = ps_slots.tile([P, PACK, BLOCK], F32, name="dp")
+            for lane in (2, 3, 0, 1):
+                matmul(bank[:, lane, :], q_mx[lane // 2], E4M3, nth(lane % 2, P), k_mx, E4M3, nth(block, BLOCK), True, True)
             nc.vector.scalar_tensor_tensor(
-                out=ds_grouped[:, PACK * c * BLOCK : PACK * (c + 1) * BLOCK].rearrange("p (n j) -> p n j", j=PACK),
+                out=ds_grp[:, nth(block, PACK * BLOCK)].rearrange("p (n j) -> p n j", j=PACK),
                 in0=bank[:].rearrange("p j n -> p n j"),
                 scalar=0.0,
-                in1=gdp[c],
+                in1=dp_blocks[block],
                 op0=ALU.max,
                 op1=ALU.mult,
             )
 
-        def quantize_do(on_vector, g):
-            grouped = new_grouped()
-            for half in range(2):
-                deal(on_vector, do_raw[:, :, g * K_PASS : (g + 1) * K_PASS], grouped, half, 0)
-            mx = mx_tiles("do%d" % g, K_PASS)
-            quantize(mx, E5M2, grouped, 0, K_PASS)
-            return mx
-
-        do_mx0 = quantize_do(False, 0)
-        do_mx1 = quantize_do(False, 1)
-        v_grp = new_grouped()
-        for j in range(PACK):
-            gather(v_grp, v_planes, j)
-        v_mx = mx_tiles("v", N)
-        quantize(v_mx, E4M3, v_grp, 0, N)
-        flat0 = gated_dp(0, do_mx0, v_mx)
-        flat1 = gated_dp(1, do_mx1, v_mx)
-        gdp0 = [weave_dp(False, flat0, 0, "gdp0_0"), None, None, weave_dp(False, flat0, 3, "gdp0_3")]
-        gdp1 = [weave_dp(False, flat1, c, "gdp1_%d" % c) for c in range(2)]
-        k_grp = new_grouped()
-        for j in range(PACK):
-            gather(k_grp, k_planes, j)
-            if j in (1, 2):
-                gdp0[j] = weave_dp(True, flat0, j, "k%d" % j)
-        k_mx = mx_tiles("k", N)
-        quantize(k_mx, E4M3, k_grp, 0, BLOCK)
-
-        def deal_half(on_vector, raw, grouped, half, first):
-            count = raw.shape[2] // PACK
-            dst = grouped.rearrange("p (t m j) -> p m j t", t=2, j=PACK)[:, first : first + count]
-            src = raw.rearrange("p j (m t) -> p m j t", t=PACK)[:, :, :, 2 * half : 2 * half + 2]
-            if on_vector:
-                nc.vector.tensor_copy(dst, src)
-            else:
-                nc.scalar.copy(dst, src)
-
-        q_grp0 = [grp.tile([P, 1024], BF16, name="grouped", align_bytes=64) for half in range(2)]
-        q_mx0 = [mx_tiles("q0_%d" % half, 256) for half in range(2)]
-        deal_half(False, q_raw[0][:], q_grp0[1][:], 1, 0)
-        deal_half(False, q_raw[0][:], q_grp0[0][:], 0, 0)
-        deal_half(True, q_raw[1][:], q_grp0[1][:], 1, 64)
-        deal_half(False, q_raw[1][:], q_grp0[0][:], 0, 64)
+        q_grp0 = [grp.tile([P, HALF * PACK], BF16, name="grouped", align_bytes=64) for half in range(2)]
+        q_mx0 = [mx_tiles(HALF, "q0_%d_codes" % half, "q0_%d_scales" % half) for half in range(2)]
+        deal(False, q_raw[0][:], dealt_half_alone(q_grp0[1]), 1, 0)
+        deal(False, q_raw[0][:], dealt_half_alone(q_grp0[0]), 0, 0)
+        deal(True, q_raw[1][:], dealt_half_alone(q_grp0[1]), 1, HALF // PACK)
+        deal(False, q_raw[1][:], dealt_half_alone(q_grp0[0]), 0, HALF // PACK)
         for half in (1, 0):
-            quantize(q_mx0[half], E4M3, q_grp0[half], 0, 256)
+            quantize(q_mx0[half], E4M3, q_grp0[half], 0, HALF)
         quantize(k_mx, E4M3, k_grp, BLOCK, BLOCK)
         quantize(k_mx, E4M3, k_grp, 2 * BLOCK, 2 * BLOCK)
+        late = keep.tile([P, BLOCKS // 2, BLOCK, PACK], F32, name="k_grp", align_bytes=64)
+        dp_blocks1.extend(weave_dp(True, 1, BLOCKS // 2 + i, late[:, i]) for i in range(BLOCKS // 2))
 
         q_grp1 = new_grouped()
-        for i in range(2):
+        for piece in range(2):
             for half in range(2):
-                deal(False, q_raw[2 + i][:], q_grp1, half, 64 * i)
-        gdp1.extend(weave_dp(False, flat1, c, "q_raw%d" % c, raws) for c in range(2, 4))
+                deal(False, q_raw[2 + piece][:], dealt_half_of_whole(q_grp1, half), half, piece * HALF // PACK)
 
         ds_grp0 = new_grouped()
-        ds_mx0 = mx_tiles("ds0", N)
-        for c in range(4):
-            ds_block(c, q_mx0, k_mx, gdp0, ds_grp0)
-        q_mx1 = (
-            keep.tile([P, K_PASS], U32, name="k0", align_bytes=64),
-            keep.tile([P, K_PASS], U8, name="q1_scales", align_bytes=64),
-        )
-        quantize(q_mx1, E4M3, q_grp1, 0, K_PASS)
+        ds_mx0 = mx_tiles(N, "ds0_codes", "ds0_scales")
+        for block in range(BLOCKS):
+            ds_block(block, q_mx0, dp_blocks0, ds_grp0)
+        q_codes1, q_scales1 = mx_tiles(K_PASS, "k0", "q1_scales")
+        quantize((q_codes1, q_scales1), E4M3, q_grp1, 0, K_PASS)
         quantize(ds_mx0, E5M2, ds_grp0, 0, N)
-        q_mx1 = [(q_mx1[0][:, 256 * half : 256 * (half + 1)], q_mx1[1][:, 256 * half : 256 * (half + 1)]) for half in range(2)]
+        q_mx1 = [(q_codes1[:, nth(half, HALF)], q_scales1[:, nth(half, HALF)]) for half in range(2)]
 
-        ds_grp1 = keep.tile([P, K_PASS * PACK], BF16, name="ds_grp1", align_bytes=64)
-        ds_mx1 = (
-            keep.tile([P, N], U32, name="v2", align_bytes=64),
-            keep.tile([P, N], U8, name="v3", align_bytes=64),
-        )
+        ds_grp1 = keep.tile([P, N * PACK], BF16, name="ds_grp1", align_bytes=64)
+        ds_mx1 = mx_tiles(N, "v2", "v3")
 
-        def deal_qm(g, h):
-            grouped = keep.tile([P, 1024], BF16, name="qm_grp%d_%d" % (g, h), align_bytes=64)
-            deal_half(False, qm_raw[g][:], grouped[:], h, 0)
+        def deal_qm(g, half):
+            grouped = keep.tile([P, HALF * PACK], BF16, name="qm_grp%d_%d" % (g, half), align_bytes=64)
+            deal(False, qm_raw[g][:], dealt_half_alone(grouped), half, 0)
             return grouped
 
-        def quantize_qm(grouped, first, count, codes_name, scales_name, pool=keep):
-            codes = pool.tile([P, count], U32, name=codes_name, align_bytes=64)
-            scales = keep.tile([P, count], U8, name=scales_name, align_bytes=64)
+        def quantize_qm(grouped, first, count, codes_name, scales_name):
+            codes, scales = mx_tiles(count, codes_name, scales_name)
             nc.vector.quantize_mx(
                 out=codes[:].bitcast(E4M3), scales=scales[:], in_=grouped[:, PACK * first : PACK * (first + count)]
             )
             return [(codes[:, i : i + P], scales[:, i : i + P]) for i in range(0, count, P)]
 
-        qm_grp = [[deal_qm(g, h) for h in range(2)] for g in range(PASSES)]
-        ds_block(0, q_mx1, k_mx, gdp1, ds_grp1)
-        ds_block(1, q_mx1, k_mx, gdp1, ds_grp1)
+        qm_grp = [[deal_qm(g, half) for half in range(2)] for g in range(PASSES)]
+        ds_block(0, q_mx1, dp_blocks1, ds_grp1)
+        ds_block(1, q_mx1, dp_blocks1, ds_grp1)
         qm_mx = [quantize_qm(qm_grp[0][0], 0, P, "qm00_codes", "qm00_scales")]
-        ds_block(2, q_mx1, k_mx, gdp1, ds_grp1)
-        quantize(ds_mx1, E5M2, ds_grp1, 0, 256)
-        ds_block(3, q_mx1, k_mx, gdp1, ds_grp1)
-        quantize(ds_mx1, E5M2, ds_grp1, 256, 128)
-        qm_mx.append(quantize_qm(qm_grp[1][0], 0, P, "q_raw3", "qm10_scales", raws))
-        quantize(ds_mx1, E5M2, ds_grp1, 384, 128)
+        ds_block(2, q_mx1, dp_blocks1, ds_grp1)
+        quantize(ds_mx1, E5M2, ds_grp1, 0, 2 * BLOCK)
+        ds_block(3, q_mx1, dp_blocks1, ds_grp1)
+        quantize(ds_mx1, E5M2, ds_grp1, 2 * BLOCK, BLOCK)
+        qm_mx.append(quantize_qm(qm_grp[1][0], 0, P, "k_grp", "qm10_scales"))
+        quantize(ds_mx1, E5M2, ds_grp1, 3 * BLOCK, BLOCK)
         qm_mx[0].extend(quantize_qm(qm_grp[0][0], P, P, "ds_grp1", "qm01_scales"))
         qm_mx[1].extend(quantize_qm(qm_grp[1][0], P, P, "qm11_codes", "qm_grp0_0"))
         qm_mx[0].extend(quantize_qm(qm_grp[0][1], 0, 2 * P, "qm02_codes", "qm_grp1_0"))
@@ -245,45 +244,45 @@ def tile_attend_gat_pl_k_kernel(tc, qT, kT, vT, doT, rw, qm, offs, out_0, out_1,
 
         out_rows = out_0.rearrange("(p t) c -> p t c", t=PACK)
 
-        def round_lane(t):
-            nc.scalar.copy(y3[:].rearrange("p (n j) -> p n j", j=PACK)[:, :, t], tokens(t, 3))
+        def pieces_of(lane):
+            count = 2 if lane == 0 else 1
+            return [nth(i, N // count) for i in range(count)]
 
-        def pair_place(t, c):
-            return pairs[c][:].rearrange("p (u n e) -> p u n e", u=2, e=2)[:, t // 2]
-
-        def tokens(t, c):
-            return windows[t][:, c * CHUNK : (c + 1) * CHUNK]
-
-        def round_pairs(t, c, span=slice(0, CHUNK)):
-            nc.scalar.copy(pair_place(t, c)[:, span, t % 2], tokens(t, c)[:, span])
-
-        def round_plane(t):
-            for c in range(2):
-                if t == 0:
-                    dst, src = pair_place(t, c), tokens(t, c).unsqueeze(2).to_broadcast([P, CHUNK, 2])
-                else:
-                    dst, src = pair_place(t, c)[:, :, t % 2], tokens(t, c)
-                nc.gpsimd.tensor_scalar(dst, src, 1.0, -0.0, ALU.mult, ALU.add)
-            round_pairs(t, 2)
-            round_lane(t)
-
-        def dk_plane(t):
-            bank = ps_dk.tile([P, N], F32, name="dk")
+        def dk_plane(lane):
+            bank = ps_result.tile([P, N], F32, name="dk")
             for g in range(PASSES):
-                matmul(bank[:], qm_mx[g][t], E4M3, slice(0, P), ds_mx[g], E5M2, slice(0, N), g == 0, g == PASSES - 1)
-            dk = keep.tile([P, N], F32, name="dk_sb%d" % t, align_bytes=64)
-            pieces = 2 if t == 0 else 1
-            for i in range(pieces):
-                span = slice(i * N // pieces, (i + 1) * N // pieces)
-                nc.scalar.copy(dk[:, span], bank[:, span])
+                matmul(bank[:], qm_mx[g][lane], E4M3, slice(0, P), ds_mx[g], E5M2, slice(0, N), g == 0, g == PASSES - 1)
+            dk = keep.tile([P, N], F32, name="gdp0_%d" % lane, align_bytes=64)
+            for slots in pieces_of(lane):
+                nc.scalar.copy(dk[:, slots], bank[:, slots])
             return dk
 
-        def scatter(t, dk):
-            pieces = 2 if t == 0 else 1
-            for i in range(pieces):
-                first, last = i * N // pieces, (i + 1) * N // pieces
-                nc.vector.tensor_copy(windows[t][:].indirect(offsets[:, first // 16 : last // 16]), dk[:, first:last])
-            nc.sync.dma_start(out_rows[:, t, :], windows[t][:])
+        def scatter(lane, dk):
+            for slots in pieces_of(lane):
+                listed = offsets[:, slots.start // BAND : slots.stop // BAND]
+                nc.vector.tensor_copy(windows[lane][:].indirect(listed), dk[:, slots])
+            nc.sync.dma_start(out_rows[:, lane, :], windows[lane][:])
+
+        def tokens(lane, chunk):
+            return windows[lane][:, nth(chunk, CHUNK)]
+
+        def pair_words(lane, chunk):
+            return pairs[chunk][:].rearrange("p (u n e) -> p u n e", u=2, e=2)[:, lane // 2]
+
+        def round_into_pairs(lane, span):
+            nc.scalar.copy(pair_words(lane, 2)[:, span, lane % 2], tokens(lane, 2)[:, span])
+
+        def round_into_grouped(lane):
+            nc.scalar.copy(y_grp3[:].rearrange("p (n j) -> p n j", j=PACK)[:, :, lane], tokens(lane, 3))
+
+        def round_plane(lane):
+            for chunk in range(2):
+                if lane == 0:
+                    gpsimd_copy(pair_words(lane, chunk), tokens(lane, chunk).unsqueeze(2).to_broadcast([P, CHUNK, 2]))
+                else:
+                    gpsimd_copy(pair_words(lane, chunk)[:, :, lane % 2], tokens(lane, chunk))
+            round_into_pairs(lane, slice(0, CHUNK))
+            round_into_grouped(lane)
 
         dk0 = dk_plane(0)
         dk2 = dk_plane(2)
@@ -291,7 +290,7 @@ def tile_attend_gat_pl_k_kernel(tc, qT, kT, vT, doT, rw, qm, offs, out_0, out_1,
         dk3 = dk_plane(3)
         dk1 = dk_plane(1)
         pairs = [new_grouped(), new_grouped(), keep.tile([P, PACK * CHUNK], BF16, name="v3", align_bytes=64)]
-        y3 = keep.tile([P, PACK * CHUNK], BF16, name="v2", align_bytes=64)
+        y_grp3 = keep.tile([P, PACK * CHUNK], BF16, name="v2", align_bytes=64)
         round_plane(0)
         scatter(2, dk2)
         round_plane(2)
@@ -299,44 +298,41 @@ def tile_attend_gat_pl_k_kernel(tc, qT, kT, vT, doT, rw, qm, offs, out_0, out_1,
         round_plane(3)
         scatter(1, dk1)
 
-        y_codes = [keep.tile([P, CHUNK], U32, name="y_codes%d" % c, align_bytes=64)[:] for c in range(CHUNKS)]
+        y_codes = [keep.tile([P, CHUNK], U32, name="y_codes%d" % chunk, align_bytes=64) for chunk in range(CHUNKS)]
         y_scales = keep.tile([P, CHUNK], U8, name="y_scales", align_bytes=64)
         words_out = out_1[0].rearrange("p t l -> p (t l)").bitcast(I32)
 
-        def weave_pairs(on_vector, c, span, grouped):
+        def weave_pairs(on_vector, chunk, span, grouped):
             dst = grouped[:].bitcast(F32).rearrange("p (n u) -> p n u", u=2)
-            src = pairs[c][:].bitcast(F32).rearrange("p (u n) -> p n u", u=2)[:, span]
-            if on_vector:
-                nc.vector.tensor_copy(dst, src)
-            else:
-                nc.scalar.copy(dst, src)
+            copy(on_vector, dst, pairs[chunk][:].bitcast(F32).rearrange("p (u n) -> p n u", u=2)[:, span])
             return grouped
 
-        def finish(c, halves):
-            span = slice(c * CHUNK, (c + 1) * CHUNK)
-            for half in range(2):
-                cols = slice(256 * half, 256 * (half + 1))
-                nc.vector.quantize_mx(out=y_codes[c][:, cols].bitcast(E4M3), scales=y_scales[4 * c :, cols], in_=halves[half])
-            nc.sync.dma_start(words_out[:, span], y_codes[c].bitcast(I32))
-
         def halves_of(grouped):
-            return [grouped[:, 1024 * half : 1024 * (half + 1)] for half in range(2)]
+            return [grouped[:, nth(half, HALF * PACK)] for half in range(2)]
 
-        for c in range(2):
-            nc.vector.tensor_copy(pair_place(1, c)[:, :, 1], tokens(1, c))
-        round_lane(1)
-        y2 = []
+        def finish(chunk, halves):
+            for half in range(2):
+                nc.vector.quantize_mx(
+                    out=y_codes[chunk][:, nth(half, HALF)].bitcast(E4M3),
+                    scales=y_scales[SCALE_ROWS * chunk :, nth(half, HALF)],
+                    in_=halves[half],
+                )
+            nc.sync.dma_start(words_out[:, nth(chunk, CHUNK)], y_codes[chunk][:].bitcast(I32))
+
+        for chunk in range(2):
+            nc.vector.tensor_copy(pair_words(1, chunk)[:, :, 1], tokens(1, chunk))
+        round_into_grouped(1)
+        y_halves2 = []
         for half in range(2):
-            span = slice(256 * half, 256 * (half + 1))
-            round_pairs(1, 2, span)
-            grouped = keep.tile([P, 1024], BF16, name="k%d" % (1 + half), align_bytes=64)
-            y2.append(weave_pairs(False, 2, span, grouped)[:])
-        y0 = weave_pairs(True, 0, slice(0, CHUNK), new_grouped())
-        y1 = weave_pairs(True, 1, slice(0, CHUNK), new_grouped())
-        finish(0, halves_of(y0))
-        finish(1, halves_of(y1))
-        finish(3, halves_of(y3))
-        finish(2, y2)
-        for quad in range(4):
-            rows = out_2[0][4 * quad : 4 * quad + 4, :].bitcast(I32).rearrange("r (c x) -> c r x", c=CHUNKS)
-            nc.sync.dma_start(rows, y_scales[32 * quad : 32 * quad + 16, :].bitcast(I32))
+            round_into_pairs(1, nth(half, HALF))
+            grouped = keep.tile([P, HALF * PACK], BF16, name="k%d" % (1 + half), align_bytes=64)
+            y_halves2.append(weave_pairs(False, 2, nth(half, HALF), grouped)[:])
+        y_grp0 = weave_pairs(True, 0, slice(0, CHUNK), new_grouped())
+        y_grp1 = weave_pairs(True, 1, slice(0, CHUNK), new_grouped())
+        finish(0, halves_of(y_grp0))
+        finish(1, halves_of(y_grp1))
+        finish(3, halves_of(y_grp3))
+        finish(2, y_halves2)
+        for quad in range(P // 32):
+            rows = out_2[0][nth(quad, SCALE_ROWS), :].bitcast(I32).rearrange("r (c x) -> c r x", c=CHUNKS)
+            nc.sync.dma_start(rows, y_scales[32 * quad : 32 * quad + SCALE_ROWS * CHUNKS, :].bitcast(I32))

@@ -171,6 +171,13 @@ def tile_attend_gat_pl_k_kernel(tc, qT, kT, vT, doT, rw, qm, offs, out_0, out_1,
         k_mx = mx_tiles(N, "k_codes", "k_scales")
         quantize(k_mx, E4M3, k_grp, 0, BLOCK)
 
+        def warm_up(lhs, lhs_fmt, rhs):
+            bank = ps_slots.tile([P, N], F32, name="dp")
+            for repeat in range(2):
+                matmul(bank[:], lhs, lhs_fmt, slice(0, P), rhs, E4M3, slice(0, N), True, True)
+
+        warm_up(k_mx, E4M3, v_mx)
+
         def ds_block(block, q_mx, dp_blocks, ds_grp):
             bank = ps_slots.tile([P, PACK, BLOCK], F32, name="dp")
             for lane in (2, 3, 0, 1):
@@ -233,6 +240,7 @@ def tile_attend_gat_pl_k_kernel(tc, qT, kT, vT, doT, rw, qm, offs, out_0, out_1,
         ds_block(2, q_mx1, dp_blocks1, ds_grp1)
         quantize(ds_mx1, E5M2, ds_grp1, 0, 2 * BLOCK)
         ds_block(3, q_mx1, dp_blocks1, ds_grp1)
+        warm_up(ds_mx1, E5M2, k_mx)
         quantize(ds_mx1, E5M2, ds_grp1, 2 * BLOCK, BLOCK)
         qm_mx.append(quantize_qm(qm_grp[1][0], 0, P, "k_grp", "qm10_scales"))
         quantize(ds_mx1, E5M2, ds_grp1, 3 * BLOCK, BLOCK)

@@ -221,11 +221,6 @@ def tile_attend_gat_pl_k_kernel(tc, qT, kT, vT, doT, rw, qm, offs, out_0, out_1,
         ds_grp1 = keep.tile([P, N * PACK], BF16, name="ds_grp1", align_bytes=64)
         ds_mx1 = mx_tiles(N, "v2", "v3")
 
-        def deal_qm(g, half):
-            grouped = keep.tile([P, HALF * PACK], BF16, name="qm_grp%d_%d" % (g, half), align_bytes=64)
-            deal(False, qm_raw[g][:], dealt_half_alone(grouped), half, 0)
-            return grouped
-
         def quantize_qm(grouped, first, count, codes_name, scales_name):
             codes, scales = mx_tiles(count, codes_name, scales_name)
             nc.vector.quantize_mx(
@@ -233,21 +228,23 @@ def tile_attend_gat_pl_k_kernel(tc, qT, kT, vT, doT, rw, qm, offs, out_0, out_1,
             )
             return [(codes[:, i : i + P], scales[:, i : i + P]) for i in range(0, count, P)]
 
-        qm_grp = [[deal_qm(g, half) for half in range(2)] for g in range(PASSES)]
+        qm_grp = [keep.tile([P, K_PASS * PACK], BF16, name="qm_grp%d" % half, align_bytes=64) for half in range(2)]
+        for g in range(PASSES):
+            for half in range(2):
+                dealt = qm_grp[half][:].rearrange("p (t g m j) -> p g m j t", t=2, g=PASSES, j=PACK)[:, g]
+                deal(False, qm_raw[g][:], dealt, half, 0)
         ds_block(0, q_mx1, dp_blocks1, ds_grp1)
         ds_block(1, q_mx1, dp_blocks1, ds_grp1)
-        qm_mx = [quantize_qm(qm_grp[0][0], 0, P, "qm00_codes", "qm00_scales")]
+        qm_mx = quantize_qm(qm_grp[0], 0, P, "qm00_codes", "qm00_scales")
         ds_block(2, q_mx1, dp_blocks1, ds_grp1)
         quantize(ds_mx1, E5M2, ds_grp1, 0, 2 * BLOCK)
         ds_block(3, q_mx1, dp_blocks1, ds_grp1)
         warm_up(ds_mx1, E5M2, k_mx)
         quantize(ds_mx1, E5M2, ds_grp1, 2 * BLOCK, BLOCK)
-        qm_mx.append(quantize_qm(qm_grp[1][0], 0, P, "k_grp", "qm10_scales"))
+        qm_mx.extend(quantize_qm(qm_grp[0], P, P, "k_grp", "qm10_scales"))
         quantize(ds_mx1, E5M2, ds_grp1, 3 * BLOCK, BLOCK)
-        qm_mx[0].extend(quantize_qm(qm_grp[0][0], P, P, "ds_grp1", "qm01_scales"))
-        qm_mx[1].extend(quantize_qm(qm_grp[1][0], P, P, "qm11_codes", "qm_grp0_0"))
-        qm_mx[0].extend(quantize_qm(qm_grp[0][1], 0, 2 * P, "qm02_codes", "qm_grp1_0"))
-        qm_mx[1].extend(quantize_qm(qm_grp[1][1], 0, 2 * P, "qm12_codes", "qm_grp0_1"))
+        qm_mx.extend(quantize_qm(qm_grp[0], 2 * P, 2 * P, "ds_grp1", "qm1_scales"))
+        qm_mx.extend(quantize_qm(qm_grp[1], 0, 4 * P, "qm23_codes", "qm_grp0"))
         ds_mx = [ds_mx0, ds_mx1]
 
         out_rows = out_0.rearrange("(p t) c -> p t c", t=PACK)
@@ -259,7 +256,7 @@ def tile_attend_gat_pl_k_kernel(tc, qT, kT, vT, doT, rw, qm, offs, out_0, out_1,
         def dk_plane(lane):
             bank = ps_result.tile([P, N], F32, name="dk")
             for g in range(PASSES):
-                matmul(bank[:], qm_mx[g][lane], E4M3, slice(0, P), ds_mx[g], E5M2, slice(0, N), g == 0, g == PASSES - 1)
+                matmul(bank[:], qm_mx[PASSES * lane + g], E4M3, slice(0, P), ds_mx[g], E5M2, slice(0, N), g == 0, g == PASSES - 1)
             dk = keep.tile([P, N], F32, name="gdp0_%d" % lane, align_bytes=64)
             for slots in pieces_of(lane):
                 nc.scalar.copy(dk[:, slots], bank[:, slots])

@@ -243,8 +243,15 @@ def tile_attend_gat_pl_k_kernel(tc, qT, kT, vT, doT, rw, qm, offs, out_0, out_1,
         quantize(ds_mx1, E5M2, ds_grp1, 2 * BLOCK, BLOCK)
         qm_mx.extend(quantize_qm(qm_grp[0], P, P, "k_grp", "qm10_scales"))
         quantize(ds_mx1, E5M2, ds_grp1, 3 * BLOCK, BLOCK)
-        qm_mx.extend(quantize_qm(qm_grp[0], 2 * P, 2 * P, "ds_grp1", "qm1_scales"))
-        qm_mx.extend(quantize_qm(qm_grp[1], 0, 4 * P, "qm23_codes", "qm_grp0"))
+        late_codes = keep.tile([P, 6 * P], U32, name="ds_grp1", align_bytes=64)
+        for half, first, count, place in ((0, 2 * P, 2 * P, 0), (1, 0, 4 * P, 2 * P)):
+            scales = keep.tile([P, count], U8, name="qm_late%d_scales" % half, align_bytes=64)
+            nc.vector.quantize_mx(
+                out=late_codes[:, place : place + count].bitcast(E4M3),
+                scales=scales[:],
+                in_=qm_grp[half][:, PACK * first : PACK * (first + count)],
+            )
+            qm_mx.extend((late_codes[:, place + i : place + i + P], scales[:, i : i + P]) for i in range(0, count, P))
         ds_mx = [ds_mx0, ds_mx1]
 
         out_rows = out_0.rearrange("(p t) c -> p t c", t=PACK)

@@ -256,68 +256,40 @@ def tile_attend_gat_pl_k_kernel(tc, qT, kT, vT, doT, rw, qm, offs, out_0, out_1,
 
         out_rows = out_0.rearrange("(p t) c -> p t c", t=PACK)
 
-        def pieces_of(lane):
-            count = 2 if lane == 0 else 1
-            return [nth(i, N // count) for i in range(count)]
-
         def dk_plane(lane):
             bank = ps_result.tile([P, N], F32, name="dk")
             for g in range(PASSES):
                 matmul(bank[:], qm_mx[PASSES * lane + g], E4M3, slice(0, P), ds_mx[g], E5M2, slice(0, N), g == 0, g == PASSES - 1)
             dk = keep.tile([P, N], F32, name="gdp0_%d" % lane, align_bytes=64)
-            for slots in pieces_of(lane):
-                nc.scalar.copy(dk[:, slots], bank[:, slots])
+            copy(lane % 2 == 0, dk[:], bank[:])
             return dk
 
         def scatter(lane, dk):
-            for slots in pieces_of(lane):
-                listed = offsets[:, slots.start // BAND : slots.stop // BAND]
-                nc.vector.tensor_copy(windows[lane][:].indirect(listed), dk[:, slots])
+            if lane % 2 == 0:
+                nc.vector.tensor_copy(windows[lane][:].indirect(offsets[:]), dk[:])
+            else:
+                for half in range(2):
+                    listed = offsets[:, nth(half, HALF // BAND)]
+                    nc.scalar.activation(windows[lane][:].indirect(listed), dk[:, nth(half, HALF)], ACT.Copy)
             nc.sync.dma_start(out_rows[:, lane, :], windows[lane][:])
 
-        def tokens(lane, chunk):
-            return windows[lane][:, nth(chunk, CHUNK)]
+        for lane in range(PACK):
+            scatter(lane, dk_plane(lane))
 
-        def pair_words(lane, chunk):
-            return pairs[chunk][:].rearrange("p (u n e) -> p u n e", u=2, e=2)[:, lane // 2]
+        rounded = [keep.tile([P, PACK, CHUNK], BF16, name="k%d" % (1 + chunk), align_bytes=64) for chunk in range(3)]
+        rounded.append(keep.tile([P, PACK, CHUNK], BF16, name="gdp0_3", align_bytes=64))
 
-        def round_into_pairs(lane, span):
-            nc.scalar.copy(pair_words(lane, 2)[:, span, lane % 2], tokens(lane, 2)[:, span])
+        def round_chunk(how, lane, chunk):
+            how(rounded[chunk][:, lane, :], windows[lane][:, nth(chunk, CHUNK)])
 
-        def round_into_grouped(lane):
-            nc.scalar.copy(y_grp3[:].rearrange("p (n j) -> p n j", j=PACK)[:, :, lane], tokens(lane, 3))
-
-        def round_plane(lane):
-            for chunk in range(2):
-                if lane == 0:
-                    gpsimd_copy(pair_words(lane, chunk), tokens(lane, chunk).unsqueeze(2).to_broadcast([P, CHUNK, 2]))
-                else:
-                    gpsimd_copy(pair_words(lane, chunk)[:, :, lane % 2], tokens(lane, chunk))
-            round_into_pairs(lane, slice(0, CHUNK))
-            round_into_grouped(lane)
-
-        dk0 = dk_plane(0)
-        dk2 = dk_plane(2)
-        scatter(0, dk0)
-        dk3 = dk_plane(3)
-        dk1 = dk_plane(1)
-        pairs = [new_grouped(), new_grouped(), keep.tile([P, PACK * CHUNK], BF16, name="v3", align_bytes=64)]
-        y_grp3 = keep.tile([P, PACK * CHUNK], BF16, name="v2", align_bytes=64)
-        round_plane(0)
-        scatter(2, dk2)
-        round_plane(2)
-        scatter(3, dk3)
-        round_plane(3)
-        scatter(1, dk1)
+        def group(how, chunk, span, grouped):
+            src = rounded[chunk][:, :, span].rearrange("p j (c i) -> p c j i", i=PACK)
+            how(grouped[:].rearrange("p (c i j) -> p c j i", i=PACK, j=PACK), src)
+            return grouped
 
         y_codes = [keep.tile([P, CHUNK], U32, name="y_codes%d" % chunk, align_bytes=64) for chunk in range(CHUNKS)]
         y_scales = keep.tile([P, CHUNK], U8, name="y_scales", align_bytes=64)
         words_out = out_1[0].rearrange("p t l -> p (t l)").bitcast(I32)
-
-        def weave_pairs(on_vector, chunk, span, grouped):
-            dst = grouped[:].bitcast(F32).rearrange("p (n u) -> p n u", u=2)
-            copy(on_vector, dst, pairs[chunk][:].bitcast(F32).rearrange("p (u n) -> p n u", u=2)[:, span])
-            return grouped
 
         def halves_of(grouped):
             return [grouped[:, nth(half, HALF * PACK)] for half in range(2)]
@@ -331,20 +303,27 @@ def tile_attend_gat_pl_k_kernel(tc, qT, kT, vT, doT, rw, qm, offs, out_0, out_1,
                 )
             nc.sync.dma_start(words_out[:, nth(chunk, CHUNK)], y_codes[chunk][:].bitcast(I32))
 
-        for chunk in range(2):
-            nc.vector.tensor_copy(pair_words(1, chunk)[:, :, 1], tokens(1, chunk))
-        round_into_grouped(1)
-        y_halves2 = []
-        for half in range(2):
-            round_into_pairs(1, nth(half, HALF))
-            grouped = keep.tile([P, HALF * PACK], BF16, name="k%d" % (1 + half), align_bytes=64)
-            y_halves2.append(weave_pairs(False, 2, nth(half, HALF), grouped)[:])
-        y_grp0 = weave_pairs(True, 0, slice(0, CHUNK), new_grouped())
-        y_grp1 = weave_pairs(True, 1, slice(0, CHUNK), new_grouped())
+        on_vector, on_scalar = nc.vector.tensor_copy, nc.scalar.copy
+        for lane in range(2):
+            for chunk in range(3):
+                round_chunk(gpsimd_copy, lane, chunk)
+        round_chunk(on_scalar, 3, 0)
+        for chunk in range(3):
+            round_chunk(on_vector, 2, chunk)
+        for chunk in (1, 2):
+            round_chunk(on_vector, 3, chunk)
+        for lane in range(PACK):
+            round_chunk(on_scalar, lane, 3)
+        whole = slice(0, CHUNK)
+        y_grp3 = group(on_scalar, 3, whole, new_grouped())
+        y_half2b = group(on_scalar, 2, nth(1, HALF), keep.tile([P, HALF * PACK], BF16, name="v2", align_bytes=64))
+        y_grp0 = group(on_vector, 0, whole, new_grouped())
+        y_grp1 = group(on_vector, 1, whole, new_grouped())
         finish(0, halves_of(y_grp0))
+        y_half2a = group(on_vector, 2, nth(0, HALF), keep.tile([P, HALF * PACK], BF16, name="v3", align_bytes=64))
         finish(1, halves_of(y_grp1))
         finish(3, halves_of(y_grp3))
-        finish(2, y_halves2)
+        finish(2, [y_half2a[:], y_half2b[:]])
         for quad in range(P // 32):
             rows = out_2[0][nth(quad, SCALE_ROWS), :].bitcast(I32).rearrange("r (c x) -> c r x", c=CHUNKS)
             nc.sync.dma_start(rows, y_scales[32 * quad : 32 * quad + SCALE_ROWS * CHUNKS, :].bitcast(I32))

@@ -27,9 +27,7 @@ BLOCKS = N // BLOCK
 CHUNK = 512
 CHUNKS = T // CHUNK
 SCALE_ROWS = 4
-GROUPED_BUFFERS = 8
-SLOT_BANKS = 6
-RESULT_BANKS = 2
+GROUPED_BUFFERS = 6
 
 
 def tile_attend_gat_pl_k_kernel(tc, qT, kT, vT, doT, rw, qm, offs, out_0, out_1, out_2):
@@ -38,8 +36,10 @@ def tile_attend_gat_pl_k_kernel(tc, qT, kT, vT, doT, rw, qm, offs, out_0, out_1,
         keep = ctx.enter_context(tc.tile_pool(name="keep", bufs=1))
         raws = ctx.enter_context(tc.tile_pool(name="raws", bufs=1))
         grp = ctx.enter_context(tc.tile_pool(name="grp", bufs=GROUPED_BUFFERS))
-        ps_slots = ctx.enter_context(tc.psum_pool(name="ps_dp", bufs=SLOT_BANKS))
-        ps_result = ctx.enter_context(tc.psum_pool(name="ps_dk", bufs=RESULT_BANKS))
+        psum = ctx.enter_context(tc.psum_pool(name="psum", bufs=1))
+
+        def in_bank(number, shape):
+            return psum.tile(shape, F32, name="bank%d" % number)
 
         offsets = keep.tile([P, N // BAND], U16, name="offsets")
 
@@ -140,7 +140,7 @@ def tile_attend_gat_pl_k_kernel(tc, qT, kT, vT, doT, rw, qm, offs, out_0, out_1,
         def gated_dp(g):
             by_lane = keep.tile([P, PACK, N], F32, name="v%d" % g, align_bytes=64)
             for lane in range(PACK):
-                bank = ps_slots.tile([P, N], F32, name="dp")
+                bank = in_bank(PACK * g + lane, [P, N])
                 matmul(bank[:], do_mx[g], E5M2, nth(lane, P), v_mx, E4M3, slice(0, N), True, True)
                 nc.scalar.activation(by_lane[:, lane, :], bank[:], ACT.Copy, scale=gate2[:, g, lane : lane + 1])
             return by_lane
@@ -172,14 +172,14 @@ def tile_attend_gat_pl_k_kernel(tc, qT, kT, vT, doT, rw, qm, offs, out_0, out_1,
         quantize(k_mx, E4M3, k_grp, 0, BLOCK)
 
         def warm_up(lhs, lhs_fmt, rhs):
-            bank = ps_slots.tile([P, N], F32, name="dp")
+            bank = in_bank(7, [P, N])
             for repeat in range(2):
                 matmul(bank[:], lhs, lhs_fmt, slice(0, P), rhs, E4M3, slice(0, N), True, True)
 
         warm_up(k_mx, E4M3, v_mx)
 
-        def ds_block(block, q_mx, dp_blocks, ds_grp):
-            bank = ps_slots.tile([P, PACK, BLOCK], F32, name="dp")
+        def ds_block(block, q_mx, dp_blocks, ds_grp, number):
+            bank = in_bank(number, [P, PACK, BLOCK])
             for lane in (2, 3, 0, 1):
                 matmul(bank[:, lane, :], q_mx[lane // 2], E4M3, nth(lane % 2, P), k_mx, E4M3, nth(block, BLOCK), True, True)
             nc.vector.scalar_tensor_tensor(
@@ -212,7 +212,7 @@ def tile_attend_gat_pl_k_kernel(tc, qT, kT, vT, doT, rw, qm, offs, out_0, out_1,
         ds_grp0 = new_grouped()
         ds_mx0 = mx_tiles(N, "ds0_codes", "ds0_scales")
         for block in range(BLOCKS):
-            ds_block(block, q_mx0, dp_blocks0, ds_grp0)
+            ds_block(block, q_mx0, dp_blocks0, ds_grp0, block)
         q_codes1, q_scales1 = mx_tiles(K_PASS, "k0", "q1_scales")
         quantize((q_codes1, q_scales1), E4M3, q_grp1, 0, K_PASS)
         quantize(ds_mx0, E5M2, ds_grp0, 0, N)
@@ -221,63 +221,90 @@ def tile_attend_gat_pl_k_kernel(tc, qT, kT, vT, doT, rw, qm, offs, out_0, out_1,
         ds_grp1 = keep.tile([P, N * PACK], BF16, name="ds_grp1", align_bytes=64)
         ds_mx1 = mx_tiles(N, "v2", "v3")
 
-        def quantize_qm(grouped, first, count, codes_name, scales_name):
-            codes, scales = mx_tiles(count, codes_name, scales_name)
-            nc.vector.quantize_mx(
-                out=codes[:].bitcast(E4M3), scales=scales[:], in_=grouped[:, PACK * first : PACK * (first + count)]
-            )
-            return [(codes[:, i : i + P], scales[:, i : i + P]) for i in range(0, count, P)]
+        def quantize_qm(grouped, codes_name, scales_name):
+            codes, scales = mx_tiles(HALF, codes_name, scales_name)
+            quantize((codes, scales), E4M3, grouped, 0, HALF)
+            return [(codes[:, nth(i, P)], scales[:, nth(i, P)]) for i in range(2)]
 
-        qm_grp = [keep.tile([P, K_PASS * PACK], BF16, name="qm_grp%d" % half, align_bytes=64) for half in range(2)]
-        for g in range(PASSES):
-            for half in range(2):
-                dealt = qm_grp[half][:].rearrange("p (t g m j) -> p g m j t", t=2, g=PASSES, j=PACK)[:, g]
-                deal(False, qm_raw[g][:], dealt, half, 0)
-        ds_block(0, q_mx1, dp_blocks1, ds_grp1)
-        ds_block(1, q_mx1, dp_blocks1, ds_grp1)
-        qm_mx = quantize_qm(qm_grp[0], 0, P, "qm00_codes", "qm00_scales")
-        ds_block(2, q_mx1, dp_blocks1, ds_grp1)
+        def deal_qm(how, g, half, name):
+            grouped = keep.tile([P, HALF * PACK], BF16, name=name, align_bytes=64)
+            src = qm_raw[g][:].rearrange("p j (m t) -> p m j t", t=PACK)[:, :, :, 2 * half : 2 * half + 2]
+            how(dealt_half_alone(grouped), src)
+            return grouped
+
+        qm_early = deal_qm(nc.scalar.copy, 0, 0, "qm_grp00")
+        qm_spare = deal_qm(nc.scalar.copy, 0, 1, "qm_grp01")
+        qm_last = deal_qm(nc.scalar.copy, 1, 0, "qm_grp10")
+        qm_late = deal_qm(nc.scalar.copy, 1, 1, "qm_grp11")
+        ds_block(0, q_mx1, dp_blocks1, ds_grp1, 4)
+        ds_block(1, q_mx1, dp_blocks1, ds_grp1, 5)
+        qm_mx = {(0, 0): quantize_qm(qm_early, "qm00_codes", "qm00_scales")}
+        ds_block(2, q_mx1, dp_blocks1, ds_grp1, 6)
         quantize(ds_mx1, E5M2, ds_grp1, 0, 2 * BLOCK)
-        ds_block(3, q_mx1, dp_blocks1, ds_grp1)
-        warm_up(ds_mx1, E5M2, k_mx)
-        quantize(ds_mx1, E5M2, ds_grp1, 2 * BLOCK, BLOCK)
-        qm_mx.extend(quantize_qm(qm_grp[0], P, P, "k_grp", "qm10_scales"))
-        quantize(ds_mx1, E5M2, ds_grp1, 3 * BLOCK, BLOCK)
-        late_codes = keep.tile([P, 6 * P], U32, name="ds_grp1", align_bytes=64)
-        for half, first, count, place in ((0, 2 * P, 2 * P, 0), (1, 0, 4 * P, 2 * P)):
-            scales = keep.tile([P, count], U8, name="qm_late%d_scales" % half, align_bytes=64)
-            nc.vector.quantize_mx(
-                out=late_codes[:, place : place + count].bitcast(E4M3),
-                scales=scales[:],
-                in_=qm_grp[half][:, PACK * first : PACK * (first + count)],
-            )
-            qm_mx.extend((late_codes[:, place + i : place + i + P], scales[:, i : i + P]) for i in range(0, count, P))
+        qm_mx[1, 0] = quantize_qm(qm_last, "qm10_codes", "qm10_scales")
         ds_mx = [ds_mx0, ds_mx1]
+
+        def dk_pass(bank, lane, g, slots):
+            matmul(bank[:], qm_mx[g, lane // 2][lane % 2], E4M3, slice(0, P), ds_mx[g], E5M2, slots, g == 0, g == PASSES - 1)
+
+        def dk_half(lane, half, number):
+            bank = in_bank(number, [P, HALF])
+            for g in range(PASSES):
+                dk_pass(bank, lane, g, nth(half, HALF))
+            return bank
+
+        ds_block(3, q_mx1, dp_blocks1, ds_grp1, 7)
+        banks = {(lane, 0): dk_half(lane, 0, lane) for lane in (0, 1)}
+        qm_mx[0, 1] = quantize_qm(qm_spare, "qm_grp10", "qm01_scales")
+        quantize(ds_mx1, E5M2, ds_grp1, 2 * BLOCK, 2 * BLOCK)
+        qm_mx[1, 1] = quantize_qm(qm_late, "qm11_codes", "qm11_scales")
+        banks[2, 0] = dk_half(2, 0, 2)
+        banks.update({(lane, 1): dk_half(lane, 1, 3 + lane) for lane in range(3)})
 
         out_rows = out_0.rearrange("(p t) c -> p t c", t=PACK)
 
-        def dk_plane(lane):
-            bank = ps_result.tile([P, N], F32, name="dk")
-            for g in range(PASSES):
-                matmul(bank[:], qm_mx[PASSES * lane + g], E4M3, slice(0, P), ds_mx[g], E5M2, slice(0, N), g == 0, g == PASSES - 1)
-            dk = keep.tile([P, N], F32, name="gdp0_%d" % lane, align_bytes=64)
-            copy(lane % 2 == 0, dk[:], bank[:])
-            return dk
+        def new_dk(width, name):
+            return keep.tile([P, width], F32, name=name, align_bytes=64)
 
-        def scatter(lane, dk):
+        def scatter_half(lane, half, dk):
+            places = windows[lane][:].indirect(offsets[:, nth(half, HALF // BAND)])
             if lane % 2 == 0:
-                nc.vector.tensor_copy(windows[lane][:].indirect(offsets[:]), dk[:])
+                nc.vector.tensor_copy(places, dk)
             else:
-                for half in range(2):
-                    listed = offsets[:, nth(half, HALF // BAND)]
-                    nc.scalar.activation(windows[lane][:].indirect(listed), dk[:, nth(half, HALF)], ACT.Copy)
+                nc.scalar.activation(places, dk, ACT.Copy)
+
+        def store(lane):
             nc.sync.dma_start(out_rows[:, lane, :], windows[lane][:])
 
-        for lane in range(PACK):
-            scatter(lane, dk_plane(lane))
+        dk0 = [new_dk(HALF, "dk0_%d" % half) for half in range(2)]
+        dk1 = [new_dk(HALF, "dk1_%d" % half) for half in range(2)]
+        dk2 = new_dk(N, "gdp0_2")
+        nc.scalar.copy(dk0[0][:], banks[0, 0][:])
+        nc.scalar.copy(dk1[0][:], banks[1, 0][:])
+        nc.scalar.copy(dk0[1][:], banks[0, 1][:])
+        scatter_half(1, 0, dk1[0][:])
+        scatter_half(0, 0, dk0[0][:])
+        nc.vector.tensor_copy(dk2[:, nth(0, HALF)], banks[2, 0][:])
+        nc.scalar.copy(dk1[1][:], banks[1, 1][:])
+        nc.scalar.copy(dk2[:, nth(1, HALF)], banks[2, 1][:])
+        scatter_half(0, 1, dk0[1][:])
+        scatter_half(1, 1, dk1[1][:])
+        store(0)
+        store(1)
+        nc.vector.tensor_copy(windows[2][:].indirect(offsets[:]), dk2[:])
+        store(2)
+        bank3 = in_bank(0, [P, N])
+        for g in range(PASSES):
+            dk_pass(bank3, 3, g, slice(0, N))
+        dk3 = new_dk(N, "gdp0_3")
+        for half in range(2):
+            nc.scalar.copy(dk3[:, nth(half, HALF)], bank3[:, nth(half, HALF)])
+        for half in range(2):
+            scatter_half(3, half, dk3[:, nth(half, HALF)])
+        store(3)
 
         rounded = [keep.tile([P, PACK, CHUNK], BF16, name="k%d" % (1 + chunk), align_bytes=64) for chunk in range(3)]
-        rounded.append(keep.tile([P, PACK, CHUNK], BF16, name="gdp0_3", align_bytes=64))
+        rounded.append(keep.tile([P, PACK, CHUNK], BF16, name="gdp0_2", align_bytes=64))
 
         def round_chunk(how, lane, chunk):
             how(rounded[chunk][:, lane, :], windows[lane][:, nth(chunk, CHUNK)])
@@ -294,36 +321,40 @@ def tile_attend_gat_pl_k_kernel(tc, qT, kT, vT, doT, rw, qm, offs, out_0, out_1,
         def halves_of(grouped):
             return [grouped[:, nth(half, HALF * PACK)] for half in range(2)]
 
-        def finish(chunk, halves):
+        def finish(chunk, halves, stores=1):
             for half in range(2):
                 nc.vector.quantize_mx(
                     out=y_codes[chunk][:, nth(half, HALF)].bitcast(E4M3),
                     scales=y_scales[SCALE_ROWS * chunk :, nth(half, HALF)],
                     in_=halves[half],
                 )
-            nc.sync.dma_start(words_out[:, nth(chunk, CHUNK)], y_codes[chunk][:].bitcast(I32))
+            for i in range(stores):
+                piece = nth(i, CHUNK // stores)
+                nc.sync.dma_start(words_out[:, nth(chunk, CHUNK)][:, piece], y_codes[chunk][:, piece].bitcast(I32))
 
         on_vector, on_scalar = nc.vector.tensor_copy, nc.scalar.copy
         for lane in range(2):
             for chunk in range(3):
                 round_chunk(gpsimd_copy, lane, chunk)
-        round_chunk(on_scalar, 3, 0)
-        for chunk in range(3):
+        for lane in range(2):
+            round_chunk(on_vector, lane, 3)
+        for chunk in range(CHUNKS):
             round_chunk(on_vector, 2, chunk)
-        for chunk in (1, 2):
+        for chunk in range(2):
             round_chunk(on_vector, 3, chunk)
-        for lane in range(PACK):
-            round_chunk(on_scalar, lane, 3)
+            round_chunk(on_scalar, 3, 3 - chunk)
         whole = slice(0, CHUNK)
         y_grp3 = group(on_scalar, 3, whole, new_grouped())
-        y_half2b = group(on_scalar, 2, nth(1, HALF), keep.tile([P, HALF * PACK], BF16, name="v2", align_bytes=64))
+        y_halves2 = [
+            group(on_scalar, 2, nth(half, HALF), keep.tile([P, HALF * PACK], BF16, name="v%d" % (2 + half), align_bytes=64))[:]
+            for half in range(2)
+        ]
         y_grp0 = group(on_vector, 0, whole, new_grouped())
         y_grp1 = group(on_vector, 1, whole, new_grouped())
         finish(0, halves_of(y_grp0))
-        y_half2a = group(on_vector, 2, nth(0, HALF), keep.tile([P, HALF * PACK], BF16, name="v3", align_bytes=64))
         finish(1, halves_of(y_grp1))
         finish(3, halves_of(y_grp3))
-        finish(2, [y_half2a[:], y_half2b[:]])
+        finish(2, y_halves2, 2)
         for quad in range(P // 32):
             rows = out_2[0][nth(quad, SCALE_ROWS), :].bitcast(I32).rearrange("r (c x) -> c r x", c=CHUNKS)
             nc.sync.dma_start(rows, y_scales[32 * quad : 32 * quad + SCALE_ROWS * CHUNKS, :].bitcast(I32))

@@ -27,7 +27,7 @@ BLOCKS = N // BLOCK
 CHUNK = 512
 CHUNKS = T // CHUNK
 SCALE_ROWS = 4
-GROUPED_BUFFERS = 6
+GROUPED_BUFFERS = 4
 
 
 def tile_attend_gat_pl_k_kernel(tc, qT, kT, vT, doT, rw, qm, offs, out_0, out_1, out_2):
@@ -113,7 +113,7 @@ def tile_attend_gat_pl_k_kernel(tc, qT, kT, vT, doT, rw, qm, offs, out_0, out_1,
             return grouped[:].rearrange("p (t m j) -> p m j t", t=PACK, j=PACK)[:, :, :, 2 * half : 2 * half + 2]
 
         def dealt_half_alone(grouped):
-            return grouped[:].rearrange("p (t m j) -> p m j t", t=2, j=PACK)
+            return grouped[:, :].rearrange("p (t m j) -> p m j t", t=2, j=PACK)
 
         def matmul(out, lhs, lhs_fmt, lhs_cols, rhs, rhs_fmt, rhs_cols, start, stop):
             nc.tensor.matmul_mx(
@@ -168,30 +168,37 @@ def tile_attend_gat_pl_k_kernel(tc, qT, kT, vT, doT, rw, qm, offs, out_0, out_1,
         k_grp = keep.tile([P, N * PACK], BF16, name="k_grp", align_bytes=64)
         for lane in range(PACK):
             gather(k_grp, k_planes, lane)
-        k_mx = mx_tiles(N, "k_codes", "k_scales")
-        quantize(k_mx, E4M3, k_grp, 0, BLOCK)
+        k_first = mx_tiles(BLOCK, "k_codes", "k_scales")
+        quantize(k_first, E4M3, k_grp, 0, BLOCK)
+        k_mx = [k_first]
 
         def warm_up(lhs, lhs_fmt, rhs):
             bank = in_bank(7, [P, N])
             for repeat in range(2):
                 matmul(bank[:], lhs, lhs_fmt, slice(0, P), rhs, E4M3, slice(0, N), True, True)
 
-        warm_up(k_mx, E4M3, v_mx)
+        warm_up(k_first, E4M3, v_mx)
 
-        def ds_block(block, q_mx, dp_blocks, ds_grp, number):
+        def scores(block, q_mx, number):
             bank = in_bank(number, [P, PACK, BLOCK])
             for lane in (2, 3, 0, 1):
-                matmul(bank[:, lane, :], q_mx[lane // 2], E4M3, nth(lane % 2, P), k_mx, E4M3, nth(block, BLOCK), True, True)
+                matmul(bank[:, lane, :], q_mx[lane // 2], E4M3, nth(lane % 2, P), k_mx[block], E4M3, slice(0, BLOCK), True, True)
+            return bank[:].rearrange("p j n -> p n j")
+
+        def by_slot(grouped):
+            return grouped.rearrange("p (n j) -> p n j", j=PACK)
+
+        def ds_block(block, q_mx, dp_blocks, grouped, number):
             nc.vector.scalar_tensor_tensor(
-                out=ds_grp[:, nth(block, PACK * BLOCK)].rearrange("p (n j) -> p n j", j=PACK),
-                in0=bank[:].rearrange("p j n -> p n j"),
+                out=by_slot(grouped),
+                in0=scores(block, q_mx, number),
                 scalar=0.0,
                 in1=dp_blocks[block],
                 op0=ALU.max,
                 op1=ALU.mult,
             )
 
-        q_grp0 = [grp.tile([P, HALF * PACK], BF16, name="grouped", align_bytes=64) for half in range(2)]
+        q_grp0 = [keep.tile([P, HALF * PACK], BF16, name="q_grp0%d" % half, align_bytes=64) for half in range(2)]
         q_mx0 = [mx_tiles(HALF, "q0_%d_codes" % half, "q0_%d_scales" % half) for half in range(2)]
         deal(False, q_raw[0][:], dealt_half_alone(q_grp0[1]), 1, 0)
         deal(False, q_raw[0][:], dealt_half_alone(q_grp0[0]), 0, 0)
@@ -199,8 +206,9 @@ def tile_attend_gat_pl_k_kernel(tc, qT, kT, vT, doT, rw, qm, offs, out_0, out_1,
         deal(False, q_raw[1][:], dealt_half_alone(q_grp0[0]), 0, HALF // PACK)
         for half in (1, 0):
             quantize(q_mx0[half], E4M3, q_grp0[half], 0, HALF)
-        quantize(k_mx, E4M3, k_grp, BLOCK, BLOCK)
-        quantize(k_mx, E4M3, k_grp, 2 * BLOCK, 2 * BLOCK)
+        rest_codes, rest_scales = mx_tiles(N - BLOCK, "q_grp01", "k_rest_scales")
+        nc.vector.quantize_mx(out=rest_codes[:].bitcast(E4M3), scales=rest_scales[:], in_=k_grp[:, PACK * BLOCK :])
+        k_mx.extend((rest_codes[:, nth(i, BLOCK)], rest_scales[:, nth(i, BLOCK)]) for i in range(BLOCKS - 1))
         late = keep.tile([P, BLOCKS // 2, BLOCK, PACK], F32, name="k_grp", align_bytes=64)
         dp_blocks1.extend(weave_dp(True, 1, BLOCKS // 2 + i, late[:, i]) for i in range(BLOCKS // 2))
 
@@ -209,17 +217,20 @@ def tile_attend_gat_pl_k_kernel(tc, qT, kT, vT, doT, rw, qm, offs, out_0, out_1,
             for half in range(2):
                 deal(False, q_raw[2 + piece][:], dealt_half_of_whole(q_grp1, half), half, piece * HALF // PACK)
 
+        def new_ds_grouped(blocks, name):
+            return keep.tile([P, blocks * BLOCK * PACK], BF16, name=name, align_bytes=64)
+
+        def quantize_ds(codes, scales, grouped):
+            nc.vector.quantize_mx(out=codes.bitcast(E5M2), scales=scales, in_=grouped[:])
+
         ds_grp0 = new_grouped()
-        ds_mx0 = mx_tiles(N, "ds0_codes", "ds0_scales")
         for block in range(BLOCKS):
-            ds_block(block, q_mx0, dp_blocks0, ds_grp0, block)
+            ds_block(block, q_mx0, dp_blocks0, ds_grp0[:, nth(block, PACK * BLOCK)], block)
         q_codes1, q_scales1 = mx_tiles(K_PASS, "k0", "q1_scales")
         quantize((q_codes1, q_scales1), E4M3, q_grp1, 0, K_PASS)
+        ds_mx0 = mx_tiles(N, "ds0_codes", "ds0_scales")
         quantize(ds_mx0, E5M2, ds_grp0, 0, N)
         q_mx1 = [(q_codes1[:, nth(half, HALF)], q_scales1[:, nth(half, HALF)]) for half in range(2)]
-
-        ds_grp1 = keep.tile([P, N * PACK], BF16, name="ds_grp1", align_bytes=64)
-        ds_mx1 = mx_tiles(N, "v2", "v3")
 
         def quantize_qm(grouped, codes_name, scales_name):
             codes, scales = mx_tiles(HALF, codes_name, scales_name)
@@ -233,33 +244,37 @@ def tile_attend_gat_pl_k_kernel(tc, qT, kT, vT, doT, rw, qm, offs, out_0, out_1,
             return grouped
 
         qm_early = deal_qm(nc.scalar.copy, 0, 0, "qm_grp00")
-        qm_spare = deal_qm(nc.scalar.copy, 0, 1, "qm_grp01")
+        qm_late = keep.tile([P, K_PASS * PACK], BF16, name="qm_late", align_bytes=64)
+        deal(False, qm_raw[0][:], dealt_half_alone(qm_late[:, nth(0, HALF * PACK)]), 1, 0)
         qm_last = deal_qm(nc.scalar.copy, 1, 0, "qm_grp10")
-        qm_late = deal_qm(nc.scalar.copy, 1, 1, "qm_grp11")
-        ds_block(0, q_mx1, dp_blocks1, ds_grp1, 4)
-        ds_block(1, q_mx1, dp_blocks1, ds_grp1, 5)
+        deal(False, qm_raw[1][:], dealt_half_alone(qm_late[:, nth(1, HALF * PACK)]), 1, 0)
+        ds_grp1 = new_ds_grouped(2, "ds_grp1")
+        for block in range(2):
+            ds_block(block, q_mx1, dp_blocks1, ds_grp1[:, nth(block, PACK * BLOCK)], 4 + block)
         qm_mx = {(0, 0): quantize_qm(qm_early, "qm00_codes", "qm00_scales")}
-        ds_block(2, q_mx1, dp_blocks1, ds_grp1, 6)
-        quantize(ds_mx1, E5M2, ds_grp1, 0, 2 * BLOCK)
+        ds_grp12 = new_ds_grouped(1, "gdp1_0")
+        ds_block(2, q_mx1, dp_blocks1, ds_grp12[:], 6)
+        ds_mx1 = [mx_tiles(HALF, "v2", "v3"), mx_tiles(HALF, "ds11_codes", "ds11_scales")]
+        quantize_ds(ds_mx1[0][0][:], ds_mx1[0][1][:], ds_grp1)
+        quantize_ds(ds_mx1[1][0][:, 0:BLOCK], ds_mx1[1][1][:, 0:BLOCK], ds_grp12)
         qm_mx[1, 0] = quantize_qm(qm_last, "qm10_codes", "qm10_scales")
-        ds_mx = [ds_mx0, ds_mx1]
+        ds_grp13 = new_ds_grouped(1, "qm_grp10")
+        ds_block(3, q_mx1, dp_blocks1, ds_grp13[:], 7)
+        late_codes, late_scales = mx_tiles(K_PASS, "qm_late_codes", "qm_late_scales")
+        quantize((late_codes, late_scales), E4M3, qm_late, 0, K_PASS)
+        for g in range(PASSES):
+            qm_mx[g, 1] = [(late_codes[:, nth(2 * g + i, P)], late_scales[:, nth(2 * g + i, P)]) for i in range(2)]
+        quantize_ds(ds_mx1[1][0][:, BLOCK:HALF], ds_mx1[1][1][:, BLOCK:HALF], ds_grp13)
 
-        def dk_pass(bank, lane, g, slots):
-            matmul(bank[:], qm_mx[g, lane // 2][lane % 2], E4M3, slice(0, P), ds_mx[g], E5M2, slots, g == 0, g == PASSES - 1)
-
-        def dk_half(lane, half, number):
-            bank = in_bank(number, [P, HALF])
-            for g in range(PASSES):
-                dk_pass(bank, lane, g, nth(half, HALF))
+        def dk_half(lane, half, bank):
+            stationary = [qm_mx[g, lane // 2][lane % 2] for g in range(PASSES)]
+            matmul(bank, stationary[0], E4M3, slice(0, P), ds_mx0, E5M2, nth(half, HALF), True, False)
+            matmul(bank, stationary[1], E4M3, slice(0, P), ds_mx1[half], E5M2, slice(0, HALF), False, True)
             return bank
 
-        ds_block(3, q_mx1, dp_blocks1, ds_grp1, 7)
-        banks = {(lane, 0): dk_half(lane, 0, lane) for lane in (0, 1)}
-        qm_mx[0, 1] = quantize_qm(qm_spare, "qm_grp10", "qm01_scales")
-        quantize(ds_mx1, E5M2, ds_grp1, 2 * BLOCK, 2 * BLOCK)
-        qm_mx[1, 1] = quantize_qm(qm_late, "qm11_codes", "qm11_scales")
-        banks[2, 0] = dk_half(2, 0, 2)
-        banks.update({(lane, 1): dk_half(lane, 1, 3 + lane) for lane in range(3)})
+        banks = {(lane, 0): dk_half(lane, 0, in_bank(lane, [P, HALF])[:]) for lane in (0, 1)}
+        banks[2, 0] = dk_half(2, 0, in_bank(2, [P, HALF])[:])
+        banks.update({(lane, 1): dk_half(lane, 1, in_bank(3 + lane, [P, HALF])[:]) for lane in range(3)})
 
         out_rows = out_0.rearrange("(p t) c -> p t c", t=PACK)
 
@@ -278,15 +293,15 @@ def tile_attend_gat_pl_k_kernel(tc, qT, kT, vT, doT, rw, qm, offs, out_0, out_1,
 
         dk0 = [new_dk(HALF, "dk0_%d" % half) for half in range(2)]
         dk1 = [new_dk(HALF, "dk1_%d" % half) for half in range(2)]
-        dk2 = new_dk(N, "gdp0_2")
-        nc.scalar.copy(dk0[0][:], banks[0, 0][:])
-        nc.scalar.copy(dk1[0][:], banks[1, 0][:])
-        nc.scalar.copy(dk0[1][:], banks[0, 1][:])
+        dk2 = new_dk(N, "gdp0_1")
+        nc.scalar.copy(dk0[0][:], banks[0, 0])
+        nc.scalar.copy(dk1[0][:], banks[1, 0])
+        nc.scalar.copy(dk0[1][:], banks[0, 1])
         scatter_half(1, 0, dk1[0][:])
         scatter_half(0, 0, dk0[0][:])
-        nc.vector.tensor_copy(dk2[:, nth(0, HALF)], banks[2, 0][:])
-        nc.scalar.copy(dk1[1][:], banks[1, 1][:])
-        nc.scalar.copy(dk2[:, nth(1, HALF)], banks[2, 1][:])
+        nc.vector.tensor_copy(dk2[:, nth(0, HALF)], banks[2, 0])
+        nc.scalar.copy(dk1[1][:], banks[1, 1])
+        nc.scalar.copy(dk2[:, nth(1, HALF)], banks[2, 1])
         scatter_half(0, 1, dk0[1][:])
         scatter_half(1, 1, dk1[1][:])
         store(0)
@@ -294,8 +309,8 @@ def tile_attend_gat_pl_k_kernel(tc, qT, kT, vT, doT, rw, qm, offs, out_0, out_1,
         nc.vector.tensor_copy(windows[2][:].indirect(offsets[:]), dk2[:])
         store(2)
         bank3 = in_bank(0, [P, N])
-        for g in range(PASSES):
-            dk_pass(bank3, 3, g, slice(0, N))
+        for half in range(2):
+            dk_half(3, half, bank3[:, nth(half, HALF)])
         dk3 = new_dk(N, "gdp0_3")
         for half in range(2):
             nc.scalar.copy(dk3[:, nth(half, HALF)], bank3[:, nth(half, HALF)])
@@ -303,58 +318,56 @@ def tile_attend_gat_pl_k_kernel(tc, qT, kT, vT, doT, rw, qm, offs, out_0, out_1,
             scatter_half(3, half, dk3[:, nth(half, HALF)])
         store(3)
 
-        rounded = [keep.tile([P, PACK, CHUNK], BF16, name="k%d" % (1 + chunk), align_bytes=64) for chunk in range(3)]
-        rounded.append(keep.tile([P, PACK, CHUNK], BF16, name="gdp0_2", align_bytes=64))
+        def new_rounded(chunks, name):
+            return keep.tile([P, PACK, chunks * CHUNK], BF16, name=name, align_bytes=64)
 
-        def round_chunk(how, lane, chunk):
-            how(rounded[chunk][:, lane, :], windows[lane][:, nth(chunk, CHUNK)])
+        rounded01 = new_rounded(2, "k1")
+        rounded2 = new_rounded(1, "gdp0_1")
+        rounded3 = new_rounded(1, "k2")
 
-        def group(how, chunk, span, grouped):
-            src = rounded[chunk][:, :, span].rearrange("p j (c i) -> p c j i", i=PACK)
+        def round_plane(how, lane, rounded, first):
+            how(rounded[:, lane, :], windows[lane][:, first * CHUNK : first * CHUNK + rounded.shape[2]])
+
+        def group(how, rounded, span, grouped):
+            src = rounded[:, :, span].rearrange("p j (c i) -> p c j i", i=PACK)
             how(grouped[:].rearrange("p (c i j) -> p c j i", i=PACK, j=PACK), src)
             return grouped
 
         y_codes = [keep.tile([P, CHUNK], U32, name="y_codes%d" % chunk, align_bytes=64) for chunk in range(CHUNKS)]
-        y_scales = keep.tile([P, CHUNK], U8, name="y_scales", align_bytes=64)
+        y_scales = keep.tile([P, 2 * CHUNK], U8, name="y_scales", align_bytes=64)
         words_out = out_1[0].rearrange("p t l -> p (t l)").bitcast(I32)
 
-        def halves_of(grouped):
-            return [grouped[:, nth(half, HALF * PACK)] for half in range(2)]
-
-        def finish(chunk, halves, stores=1):
-            for half in range(2):
-                nc.vector.quantize_mx(
-                    out=y_codes[chunk][:, nth(half, HALF)].bitcast(E4M3),
-                    scales=y_scales[SCALE_ROWS * chunk :, nth(half, HALF)],
-                    in_=halves[half],
-                )
-            for i in range(stores):
-                piece = nth(i, CHUNK // stores)
-                nc.sync.dma_start(words_out[:, nth(chunk, CHUNK)][:, piece], y_codes[chunk][:, piece].bitcast(I32))
+        def finish(chunk, span, grouped):
+            nc.vector.quantize_mx(
+                out=y_codes[chunk][:, span].bitcast(E4M3),
+                scales=y_scales[SCALE_ROWS * (chunk // 2) :, nth(chunk % 2, CHUNK)][:, span],
+                in_=grouped[:],
+            )
+            nc.sync.dma_start(words_out[:, nth(chunk, CHUNK)][:, span], y_codes[chunk][:, span].bitcast(I32))
 
         on_vector, on_scalar = nc.vector.tensor_copy, nc.scalar.copy
         for lane in range(2):
-            for chunk in range(3):
-                round_chunk(gpsimd_copy, lane, chunk)
-        for lane in range(2):
-            round_chunk(on_vector, lane, 3)
-        for chunk in range(CHUNKS):
-            round_chunk(on_vector, 2, chunk)
-        for chunk in range(2):
-            round_chunk(on_vector, 3, chunk)
-            round_chunk(on_scalar, 3, 3 - chunk)
+            round_plane(gpsimd_copy, lane, rounded01, 0)
+            round_plane(gpsimd_copy, lane, rounded3, 3)
+        for lane in range(3):
+            round_plane(on_vector, lane, rounded2, 2)
+        round_plane(on_vector, 2, rounded3, 3)
+        round_plane(on_vector, 2, rounded01, 0)
+        round_plane(on_vector, 3, rounded01, 0)
+        round_plane(on_scalar, 3, rounded2, 2)
+        round_plane(on_scalar, 3, rounded3, 3)
         whole = slice(0, CHUNK)
-        y_grp3 = group(on_scalar, 3, whole, new_grouped())
-        y_halves2 = [
-            group(on_scalar, 2, nth(half, HALF), keep.tile([P, HALF * PACK], BF16, name="v%d" % (2 + half), align_bytes=64))[:]
+        y_grp2 = group(on_scalar, rounded2, whole, new_grouped())
+        y_halves3 = [
+            group(on_scalar, rounded3, nth(half, HALF), keep.tile([P, HALF * PACK], BF16, name="v%d" % (2 + half), align_bytes=64))
             for half in range(2)
         ]
-        y_grp0 = group(on_vector, 0, whole, new_grouped())
-        y_grp1 = group(on_vector, 1, whole, new_grouped())
-        finish(0, halves_of(y_grp0))
-        finish(1, halves_of(y_grp1))
-        finish(3, halves_of(y_grp3))
-        finish(2, y_halves2, 2)
+        y_grp01 = [group(on_vector, rounded01, nth(chunk, CHUNK), new_grouped()) for chunk in range(2)]
+        for chunk in range(2):
+            finish(chunk, whole, y_grp01[chunk])
+        finish(2, whole, y_grp2)
+        for half in range(2):
+            finish(3, nth(half, HALF), y_halves3[half])
         for quad in range(P // 32):
-            rows = out_2[0][nth(quad, SCALE_ROWS), :].bitcast(I32).rearrange("r (c x) -> c r x", c=CHUNKS)
-            nc.sync.dma_start(rows, y_scales[32 * quad : 32 * quad + SCALE_ROWS * CHUNKS, :].bitcast(I32))
+            rows = out_2[0][nth(quad, SCALE_ROWS), :].bitcast(I32).rearrange("r (c x) -> c r x", c=2)
+            nc.sync.dma_start(rows, y_scales[32 * quad : 32 * quad + 2 * SCALE_ROWS, :].bitcast(I32))

@@ -34,307 +34,223 @@ def tile_attend_gat_pl_k_kernel(tc, qT, kT, vT, doT, rw, qm, offs, out_0, out_1,
     nc = tc.nc
     with ExitStack() as ctx:
         keep = ctx.enter_context(tc.tile_pool(name="keep", bufs=1))
-        raws = ctx.enter_context(tc.tile_pool(name="raws", bufs=1))
         grp = ctx.enter_context(tc.tile_pool(name="grp", bufs=GROUPED_BUFFERS))
         psum = ctx.enter_context(tc.psum_pool(name="psum", bufs=1))
+        on_vector, on_scalar = nc.vector.tensor_copy, nc.scalar.copy
 
-        def in_bank(number, shape):
-            return psum.tile(shape, F32, name="bank%d" % number)
-
-        offsets = keep.tile([P, N // BAND], U16, name="offsets")
-
-        def load_planes(src, name):
-            planes = []
-            rows = src.rearrange("(p j) t -> p j t", j=PACK)
-            for lane in range(PACK):
-                plane = keep.tile([P, T], F32, name="%s%d" % (name, lane), align_bytes=64)
-                nc.sync.dma_start(plane[:], rows[:, lane, :])
-                planes.append(plane)
-            return planes
-
-        def load_raw(src, name):
-            raw = raws.tile([P, PACK, src.shape[1]], F32, name=name, align_bytes=64)
-            nc.sync.dma_start(raw[:], src.rearrange("(p j) c -> p j c", j=PACK))
-            return raw
-
-        do_raw = load_raw(doT[0], "do_raw")
-        nc.sync.dma_start(offsets[:], offs)
-        gate = keep.tile([P, PASSES, 2 * PACK], F32, name="gate")
-        nc.scalar.dma_start(gate[:, :, 0:PACK], rw[0].rearrange("(g p j) o -> p g (j o)", g=PASSES, j=PACK))
-        v_planes = load_planes(vT, "v")
-        k_planes = load_planes(kT, "k")
-        q_raw = [load_raw(qT[0][:, i * HALF : (i + 1) * HALF], "q_raw%d" % i) for i in range(R // HALF)]
-        qm_raw = [load_raw(qm[0][g * K_PASS : (g + 1) * K_PASS, :], "qm_raw%d" % g) for g in range(PASSES)]
-
-        windows = []
-        for lane in range(PACK):
-            window = keep.tile([P, T], F32, name="window%d" % lane)
-            nc.vector.memset(window[:], 0.0)
-            windows.append(window)
-
-        gate2 = keep.tile([P, PASSES, PACK], F32, name="gate2")
-        nc.scalar.mul(gate2[:], gate[:, :, 0:PACK], 2.0)
-
-        def copy(on_vector, dst, src):
-            if on_vector:
-                nc.vector.tensor_copy(dst, src)
-            else:
-                nc.scalar.copy(dst, src)
-
-        def gpsimd_copy(dst, src):
+        def on_gpsimd(dst, src):
             nc.gpsimd.tensor_scalar(dst, src, 1.0, -0.0, ALU.mult, ALU.add)
-
-        def mx_tiles(width, codes_name, scales_name):
-            codes = keep.tile([P, width], U32, name=codes_name, align_bytes=64)
-            scales = keep.tile([P, width], U8, name=scales_name, align_bytes=64)
-            return codes, scales
-
-        def new_grouped():
-            return grp.tile([P, K_PASS * PACK], BF16, name="grouped", align_bytes=64)
-
-        def quantize(mx, fmt, grouped, first, count):
-            codes, scales = mx
-            nc.vector.quantize_mx(
-                out=codes[:, first : first + count].bitcast(fmt),
-                scales=scales[:, first : first + count],
-                in_=grouped[:, PACK * first : PACK * (first + count)],
-            )
-
-        def gather(grouped, planes, lane):
-            words = grouped[:].rearrange("p (n j) -> p n j", j=PACK)
-            nc.vector.tensor_copy(words[:, :, lane], planes[lane][:].indirect(offsets[:]))
-
-        def deal(on_vector, raw, dealt, half, first):
-            count = raw.shape[2] // PACK
-            src = raw.rearrange("p j (m t) -> p m j t", t=PACK)[:, :, :, 2 * half : 2 * half + 2]
-            copy(on_vector, dealt[:, first : first + count], src)
-
-        def dealt_half_of_whole(grouped, half):
-            return grouped[:].rearrange("p (t m j) -> p m j t", t=PACK, j=PACK)[:, :, :, 2 * half : 2 * half + 2]
-
-        def dealt_half_alone(grouped):
-            return grouped[:, :].rearrange("p (t m j) -> p m j t", t=2, j=PACK)
-
-        def matmul(out, lhs, lhs_fmt, lhs_cols, rhs, rhs_fmt, rhs_cols, start, stop):
-            nc.tensor.matmul_mx(
-                out=out,
-                lhsT=lhs[0][:, lhs_cols].bitcast(lhs_fmt),
-                lhsT_scale=lhs[1][:, lhs_cols],
-                rhs=rhs[0][:, rhs_cols].bitcast(rhs_fmt),
-                rhs_scale=rhs[1][:, rhs_cols],
-                start=start,
-                stop=stop,
-            )
 
         def nth(i, width):
             return slice(i * width, (i + 1) * width)
 
-        def quantize_do(g):
-            grouped = new_grouped()
-            for half in range(2):
-                deal(False, do_raw[:, :, nth(g, K_PASS)], dealt_half_of_whole(grouped, half), half, 0)
-            mx = mx_tiles(K_PASS, "do%d_codes" % g, "do%d_scales" % g)
-            quantize(mx, E5M2, grouped, 0, K_PASS)
-            return mx
+        def sbuf(shape, dtype, name):
+            return keep.tile([P] + shape, dtype, name=name, align_bytes=64)
 
-        def gated_dp(g):
-            by_lane = keep.tile([P, PACK, N], F32, name="v%d" % g, align_bytes=64)
+        def in_bank(number, shape):
+            return psum.tile([P] + shape, F32, name="bank%d" % number)
+
+        def new_grouped():
+            return grp.tile([P, K_PASS * PACK], BF16, name="grouped", align_bytes=64)
+
+        def load_raw(src, name):
+            raw = sbuf([PACK, src.shape[1]], F32, name)
+            nc.sync.dma_start(raw[:], src.rearrange("(p j) c -> p j c", j=PACK))
+            return raw
+
+        def load_planes(src, name):
+            rows = src.rearrange("(p j) t -> p j t", j=PACK)
+            planes = [sbuf([T], F32, "%s%d" % (name, lane)) for lane in range(PACK)]
             for lane in range(PACK):
-                bank = in_bank(PACK * g + lane, [P, N])
-                matmul(bank[:], do_mx[g], E5M2, nth(lane, P), v_mx, E4M3, slice(0, N), True, True)
-                nc.scalar.activation(by_lane[:, lane, :], bank[:], ACT.Copy, scale=gate2[:, g, lane : lane + 1])
-            return by_lane
+                nc.sync.dma_start(planes[lane][:], rows[:, lane, :])
+            return planes
 
-        def weave_dp(on_gpsimd, g, block, woven):
-            src = dp_by_lane[g][:, :, nth(block, BLOCK)]
-            if on_gpsimd:
-                gpsimd_copy(woven, src.rearrange("p j n -> p n j"))
-            else:
-                nc.scalar.copy(woven.rearrange("p (n i) j -> p n j i", i=2), src.rearrange("p j (n i) -> p n j i", i=2))
-            return woven
+        q_raw = load_raw(qT[0], "q_raw")
+        offsets = keep.tile([P, N // BAND], U16, name="offsets")
+        nc.sync.dma_start(offsets[:], offs)
+        gate = keep.tile([P, PASSES, 2 * PACK], F32, name="gate")
+        nc.scalar.dma_start(gate[:, :, 0:PACK], rw[0].rearrange("(g p j) o -> p g (j o)", g=PASSES, j=PACK))
+        k_planes = load_planes(kT, "k")
+        v_planes = load_planes(vT, "v")
+        do_raw = [load_raw(doT[0][:, nth(i, HALF)], "do_raw%d" % i) for i in range(R // HALF)]
+        qm_raw = [load_raw(qm[0][nth(g, K_PASS), :], "qm_raw%d" % g) for g in range(PASSES)]
 
-        def new_woven(g, block):
-            return keep.tile([P, BLOCK, PACK], F32, name="gdp%d_%d" % (g, block), align_bytes=64)[:]
+        windows = [keep.tile([P, T], F32, name="window%d" % lane) for lane in range(PACK)]
+        for window in windows:
+            nc.vector.memset(window[:], 0.0)
 
-        do_mx = [quantize_do(g) for g in range(PASSES)]
-        v_grp = new_grouped()
-        for lane in range(PACK):
-            gather(v_grp, v_planes, lane)
-        v_mx = mx_tiles(N, "v_codes", "v_scales")
-        quantize(v_mx, E4M3, v_grp, 0, N)
-        dp_by_lane = [gated_dp(g) for g in range(PASSES)]
-        dp_blocks0 = [weave_dp(True, 0, block, new_woven(0, block)) for block in range(BLOCKS)]
-        dp_blocks1 = [weave_dp(False, 1, block, new_woven(1, block)) for block in range(BLOCKS // 2)]
-        k_grp = keep.tile([P, N * PACK], BF16, name="k_grp", align_bytes=64)
-        for lane in range(PACK):
-            gather(k_grp, k_planes, lane)
-        k_first = mx_tiles(BLOCK, "k_codes", "k_scales")
-        quantize(k_first, E4M3, k_grp, 0, BLOCK)
-        k_mx = [k_first]
+        def quantize(fmt, grouped, codes_name, scales_name):
+            width = grouped.shape[1] // PACK
+            codes, scales = sbuf([width], U32, codes_name), sbuf([width], U8, scales_name)
+            nc.vector.quantize_mx(out=codes[:].bitcast(fmt), scales=scales[:], in_=grouped)
+            return codes[:], scales[:]
 
-        def warm_up(lhs, lhs_fmt, rhs):
-            bank = in_bank(7, [P, N])
-            for repeat in range(2):
-                matmul(bank[:], lhs, lhs_fmt, slice(0, P), rhs, E4M3, slice(0, N), True, True)
+        def columns(mx, span):
+            return mx[0][:, span], mx[1][:, span]
 
-        warm_up(k_first, E4M3, v_mx)
-
-        def scores(block, q_mx, number):
-            bank = in_bank(number, [P, PACK, BLOCK])
-            for lane in (2, 3, 0, 1):
-                matmul(bank[:, lane, :], q_mx[lane // 2], E4M3, nth(lane % 2, P), k_mx[block], E4M3, slice(0, BLOCK), True, True)
-            return bank[:].rearrange("p j n -> p n j")
-
-        def by_slot(grouped):
-            return grouped.rearrange("p (n j) -> p n j", j=PACK)
-
-        def ds_block(block, q_mx, dp_blocks, grouped, number):
-            nc.vector.scalar_tensor_tensor(
-                out=by_slot(grouped),
-                in0=scores(block, q_mx, number),
-                scalar=0.0,
-                in1=dp_blocks[block],
-                op0=ALU.max,
-                op1=ALU.mult,
+        def matmul(out, lhs, lhs_fmt, rhs, rhs_fmt, start, stop):
+            nc.tensor.matmul_mx(
+                out=out,
+                lhsT=lhs[0].bitcast(lhs_fmt),
+                lhsT_scale=lhs[1],
+                rhs=rhs[0].bitcast(rhs_fmt),
+                rhs_scale=rhs[1],
+                start=start,
+                stop=stop,
             )
 
-        q_grp0 = [keep.tile([P, HALF * PACK], BF16, name="q_grp0%d" % half, align_bytes=64) for half in range(2)]
-        q_mx0 = [mx_tiles(HALF, "q0_%d_codes" % half, "q0_%d_scales" % half) for half in range(2)]
-        deal(False, q_raw[0][:], dealt_half_alone(q_grp0[1]), 1, 0)
-        deal(False, q_raw[0][:], dealt_half_alone(q_grp0[0]), 0, 0)
-        deal(True, q_raw[1][:], dealt_half_alone(q_grp0[1]), 1, HALF // PACK)
-        deal(False, q_raw[1][:], dealt_half_alone(q_grp0[0]), 0, HALF // PACK)
-        for half in (1, 0):
-            quantize(q_mx0[half], E4M3, q_grp0[half], 0, HALF)
-        rest_codes, rest_scales = mx_tiles(N - BLOCK, "q_grp01", "k_rest_scales")
-        nc.vector.quantize_mx(out=rest_codes[:].bitcast(E4M3), scales=rest_scales[:], in_=k_grp[:, PACK * BLOCK :])
-        k_mx.extend((rest_codes[:, nth(i, BLOCK)], rest_scales[:, nth(i, BLOCK)]) for i in range(BLOCKS - 1))
-        late = keep.tile([P, BLOCKS // 2, BLOCK, PACK], F32, name="k_grp", align_bytes=64)
-        dp_blocks1.extend(weave_dp(True, 1, BLOCKS // 2 + i, late[:, i]) for i in range(BLOCKS // 2))
+        def deal(how, raw, half, grouped, first=0):
+            count = raw.shape[2] // PACK
+            src = raw.rearrange("p j (m t) -> p m j t", t=PACK)[:, :, :, nth(half, 2)]
+            how(grouped.rearrange("p (t m j) -> p m j t", t=2, j=PACK)[:, first : first + count], src)
 
-        q_grp1 = new_grouped()
+        def group(how, by_lane, grouped):
+            src = by_lane.rearrange("p j (c i) -> p c j i", i=PACK)
+            how(grouped.rearrange("p (c i j) -> p c j i", i=PACK, j=PACK), src)
+
+        q_mx = []
+        for g in range(PASSES):
+            grouped = new_grouped()
+            for half in range(2):
+                deal(on_scalar, q_raw[:, :, nth(g, K_PASS)], half, grouped[:, nth(half, HALF * PACK)])
+            q_mx.append(quantize(E4M3, grouped[:], "q%d_codes" % g, "q%d_scales" % g))
+        k_listed = sbuf([PACK, N], BF16, "k_listed")
+        for lane in range(PACK):
+            on_vector(k_listed[:, lane, :], k_planes[lane][:].indirect(offsets[:]))
+        k_grp = new_grouped()
+        for half, how in enumerate((on_vector, on_scalar)):
+            group(how, k_listed[:, :, nth(half, HALF)], k_grp[:, nth(half, HALF * PACK)])
+        k_mx = quantize(E4M3, k_grp[:], "k_codes", "k_scales")
+        weight = []
+        for g in range(PASSES):
+            by_lane = sbuf([PACK, N], F32, "k%d" % g)
+            for lane in range(PACK):
+                bank = in_bank(PACK * g + lane, [N])
+                matmul(bank[:], columns(q_mx[g], nth(lane, P)), E4M3, k_mx, E4M3, True, True)
+                nc.scalar.activation(by_lane[:, lane, :], bank[:], ACT.Relu, scale=2.0)
+                nc.gpsimd.tensor_scalar(
+                    by_lane[:, lane, :], by_lane[:, lane, :], gate[:, g, lane : lane + 1], -0.0, ALU.mult, ALU.add
+                )
+            weight.append(by_lane)
+
+        v_grp = sbuf([N, PACK], BF16, "v_grp")
+        for lane in range(PACK):
+            on_vector(v_grp[:, :, lane], v_planes[lane][:].indirect(offsets[:]))
+        v_words = v_grp[:].rearrange("p n j -> p (n j)")
+        v_mx = [quantize(E4M3, v_words[:, 0 : PACK * BLOCK], "v_codes", "v_scales")]
+
+        def ds_block(g, block, do_mx, grouped, number):
+            bank = in_bank(number, [PACK, BLOCK])
+            for lane in (2, 3, 0, 1):
+                matmul(bank[:, lane, :], columns(do_mx[lane // 2], nth(lane % 2, P)), E5M2, v_mx[block], E4M3, True, True)
+            nc.vector.tensor_tensor(
+                grouped.rearrange("p (c i j) -> p c j i", i=2, j=PACK),
+                bank[:].rearrange("p j (c i) -> p c j i", i=2),
+                weight[g][:, :, nth(block, BLOCK)].rearrange("p j (c i) -> p c j i", i=2),
+                ALU.mult,
+            )
+
+        do_grp0 = [sbuf([HALF * PACK], BF16, "do_grp0%d" % half) for half in range(2)]
+        for half in (1, 0):
+            deal(on_scalar, do_raw[0][:], half, do_grp0[half][:])
+        deal(on_vector, do_raw[1][:], 1, do_grp0[1][:], HALF // PACK)
+        deal(on_scalar, do_raw[1][:], 0, do_grp0[0][:], HALF // PACK)
+        do_mx0 = {half: quantize(E5M2, do_grp0[half][:], "do0%d_codes" % half, "do0%d_scales" % half) for half in (1, 0)}
+        v_rest = quantize(E4M3, v_words[:, PACK * BLOCK :], "do_grp01", "v_rest_scales")
+        v_mx.extend(columns(v_rest, nth(i, BLOCK)) for i in range(BLOCKS - 1))
+
+        do_grp1 = new_grouped()
         for piece in range(2):
             for half in range(2):
-                deal(False, q_raw[2 + piece][:], dealt_half_of_whole(q_grp1, half), half, piece * HALF // PACK)
-
-        def new_ds_grouped(blocks, name):
-            return keep.tile([P, blocks * BLOCK * PACK], BF16, name=name, align_bytes=64)
-
-        def quantize_ds(codes, scales, grouped):
-            nc.vector.quantize_mx(out=codes.bitcast(E5M2), scales=scales, in_=grouped[:])
-
+                deal(on_scalar, do_raw[2 + piece][:], half, do_grp1[:, nth(half, HALF * PACK)], piece * HALF // PACK)
         ds_grp0 = new_grouped()
         for block in range(BLOCKS):
-            ds_block(block, q_mx0, dp_blocks0, ds_grp0[:, nth(block, PACK * BLOCK)], block)
-        q_codes1, q_scales1 = mx_tiles(K_PASS, "k0", "q1_scales")
-        quantize((q_codes1, q_scales1), E4M3, q_grp1, 0, K_PASS)
-        ds_mx0 = mx_tiles(N, "ds0_codes", "ds0_scales")
-        quantize(ds_mx0, E5M2, ds_grp0, 0, N)
-        q_mx1 = [(q_codes1[:, nth(half, HALF)], q_scales1[:, nth(half, HALF)]) for half in range(2)]
+            ds_block(0, block, do_mx0, ds_grp0[:, nth(block, PACK * BLOCK)], block)
+        do_whole1 = quantize(E5M2, do_grp1[:], "do1_codes", "do1_scales")
+        do_mx1 = [columns(do_whole1, nth(half, HALF)) for half in range(2)]
+        ds_mx0 = quantize(E5M2, ds_grp0[:], "ds0_codes", "ds0_scales")
 
-        def quantize_qm(grouped, codes_name, scales_name):
-            codes, scales = mx_tiles(HALF, codes_name, scales_name)
-            quantize((codes, scales), E4M3, grouped, 0, HALF)
-            return [(codes[:, nth(i, P)], scales[:, nth(i, P)]) for i in range(2)]
-
-        def deal_qm(how, g, half, name):
-            grouped = keep.tile([P, HALF * PACK], BF16, name=name, align_bytes=64)
-            src = qm_raw[g][:].rearrange("p j (m t) -> p m j t", t=PACK)[:, :, :, 2 * half : 2 * half + 2]
-            how(dealt_half_alone(grouped), src)
-            return grouped
-
-        qm_early = deal_qm(nc.scalar.copy, 0, 0, "qm_grp00")
-        qm_late = keep.tile([P, K_PASS * PACK], BF16, name="qm_late", align_bytes=64)
-        deal(False, qm_raw[0][:], dealt_half_alone(qm_late[:, nth(0, HALF * PACK)]), 1, 0)
-        qm_last = deal_qm(nc.scalar.copy, 1, 0, "qm_grp10")
-        deal(False, qm_raw[1][:], dealt_half_alone(qm_late[:, nth(1, HALF * PACK)]), 1, 0)
-        ds_grp1 = new_ds_grouped(2, "ds_grp1")
-        for block in range(2):
-            ds_block(block, q_mx1, dp_blocks1, ds_grp1[:, nth(block, PACK * BLOCK)], 4 + block)
-        qm_mx = {(0, 0): quantize_qm(qm_early, "qm00_codes", "qm00_scales")}
-        ds_grp12 = new_ds_grouped(1, "gdp1_0")
-        ds_block(2, q_mx1, dp_blocks1, ds_grp12[:], 6)
-        ds_mx1 = [mx_tiles(HALF, "v2", "v3"), mx_tiles(HALF, "ds11_codes", "ds11_scales")]
-        quantize_ds(ds_mx1[0][0][:], ds_mx1[0][1][:], ds_grp1)
-        quantize_ds(ds_mx1[1][0][:, 0:BLOCK], ds_mx1[1][1][:, 0:BLOCK], ds_grp12)
-        qm_mx[1, 0] = quantize_qm(qm_last, "qm10_codes", "qm10_scales")
-        ds_grp13 = new_ds_grouped(1, "qm_grp10")
-        ds_block(3, q_mx1, dp_blocks1, ds_grp13[:], 7)
-        late_codes, late_scales = mx_tiles(K_PASS, "qm_late_codes", "qm_late_scales")
-        quantize((late_codes, late_scales), E4M3, qm_late, 0, K_PASS)
+        qm_grp = [sbuf([HALF * PACK], BF16, "qm_grp%d" % g) for g in range(PASSES)]
+        qm_late = sbuf([K_PASS * PACK], BF16, "qm_late")
         for g in range(PASSES):
-            qm_mx[g, 1] = [(late_codes[:, nth(2 * g + i, P)], late_scales[:, nth(2 * g + i, P)]) for i in range(2)]
-        quantize_ds(ds_mx1[1][0][:, BLOCK:HALF], ds_mx1[1][1][:, BLOCK:HALF], ds_grp13)
+            deal(on_scalar, qm_raw[g][:], 0, qm_grp[g][:])
+            deal(on_scalar, qm_raw[g][:], 1, qm_late[:, nth(g, HALF * PACK)])
+
+        ds_grp1 = sbuf([HALF * PACK], BF16, "ds_grp1")
+        for block in range(2):
+            ds_block(1, block, do_mx1, ds_grp1[:, nth(block, PACK * BLOCK)], 4 + block)
+        qm_mx = {(0, 0): quantize(E4M3, qm_grp[0][:], "qm00_codes", "qm00_scales")}
+        ds_mx1 = [quantize(E5M2, ds_grp1[:], "ds10_codes", "ds10_scales")]
+        ds_grp12 = sbuf([BLOCK * PACK], BF16, "qm_grp0")
+        ds_block(1, 2, do_mx1, ds_grp12[:], 6)
+
+        def quantize_last_block(i, grouped):
+            codes, scales = columns(ds_mx1[1], nth(i, BLOCK))
+            nc.vector.quantize_mx(out=codes.bitcast(E5M2), scales=scales, in_=grouped[:])
+
+        qm_mx[1, 0] = quantize(E4M3, qm_grp[1][:], "qm10_codes", "qm10_scales")
+        ds_grp13 = sbuf([BLOCK * PACK], BF16, "qm_grp1")
+        ds_block(1, 3, do_mx1, ds_grp13[:], 7)
+        late_mx = quantize(E4M3, qm_late[:], "qm_late_codes", "qm_late_scales")
+        qm_mx.update({(g, 1): columns(late_mx, nth(g, HALF)) for g in range(PASSES)})
+        ds_mx1.append((sbuf([HALF], U32, "k1")[:], sbuf([HALF], U8, "ds11_scales")[:]))
+        quantize_last_block(0, ds_grp12)
+        quantize_last_block(1, ds_grp13)
 
         def dk_half(lane, half, bank):
-            stationary = [qm_mx[g, lane // 2][lane % 2] for g in range(PASSES)]
-            matmul(bank, stationary[0], E4M3, slice(0, P), ds_mx0, E5M2, nth(half, HALF), True, False)
-            matmul(bank, stationary[1], E4M3, slice(0, P), ds_mx1[half], E5M2, slice(0, HALF), False, True)
+            moving = [columns(ds_mx0, nth(half, HALF)), ds_mx1[half]]
+            for g in range(PASSES):
+                stationary = columns(qm_mx[g, lane // 2], nth(lane % 2, P))
+                matmul(bank, stationary, E4M3, moving[g], E5M2, g == 0, g == PASSES - 1)
             return bank
 
-        banks = {(lane, 0): dk_half(lane, 0, in_bank(lane, [P, HALF])[:]) for lane in (0, 1)}
-        banks[2, 0] = dk_half(2, 0, in_bank(2, [P, HALF])[:])
-        banks.update({(lane, 1): dk_half(lane, 1, in_bank(3 + lane, [P, HALF])[:]) for lane in range(3)})
-
-        out_rows = out_0.rearrange("(p t) c -> p t c", t=PACK)
-
-        def new_dk(width, name):
-            return keep.tile([P, width], F32, name=name, align_bytes=64)
-
-        def scatter_half(lane, half, dk):
-            places = windows[lane][:].indirect(offsets[:, nth(half, HALF // BAND)])
+        def scatter(lane, listed, dk):
             if lane % 2 == 0:
-                nc.vector.tensor_copy(places, dk)
+                on_vector(windows[lane][:].indirect(listed), dk)
             else:
-                nc.scalar.activation(places, dk, ACT.Copy)
+                nc.scalar.activation(windows[lane][:].indirect(listed), dk, ACT.Copy)
 
         def store(lane):
-            nc.sync.dma_start(out_rows[:, lane, :], windows[lane][:])
+            nc.sync.dma_start(out_0.rearrange("(p t) c -> p t c", t=PACK)[:, lane, :], windows[lane][:])
 
-        dk0 = [new_dk(HALF, "dk0_%d" % half) for half in range(2)]
-        dk1 = [new_dk(HALF, "dk1_%d" % half) for half in range(2)]
-        dk2 = new_dk(N, "gdp0_1")
-        nc.scalar.copy(dk0[0][:], banks[0, 0])
-        nc.scalar.copy(dk1[0][:], banks[1, 0])
-        nc.scalar.copy(dk0[1][:], banks[0, 1])
-        scatter_half(1, 0, dk1[0][:])
-        scatter_half(0, 0, dk0[0][:])
-        nc.vector.tensor_copy(dk2[:, nth(0, HALF)], banks[2, 0])
-        nc.scalar.copy(dk1[1][:], banks[1, 1])
-        nc.scalar.copy(dk2[:, nth(1, HALF)], banks[2, 1])
-        scatter_half(0, 1, dk0[1][:])
-        scatter_half(1, 1, dk1[1][:])
-        store(0)
-        store(1)
-        nc.vector.tensor_copy(windows[2][:].indirect(offsets[:]), dk2[:])
+        banks = {(lane, 0): dk_half(lane, 0, in_bank(lane, [HALF])[:]) for lane in range(3)}
+        banks.update({(lane, 1): dk_half(lane, 1, in_bank(3 + lane, [HALF])[:]) for lane in range(3)})
+        bank3 = in_bank(0, [N])
+        halves = [offsets[:, nth(half, HALF // BAND)] for half in range(2)]
+        dk0 = [sbuf([HALF], F32, "dk0%d" % half) for half in range(2)]
+        dk1 = [sbuf([HALF], F32, "dk1%d" % half) for half in range(2)]
+        dk2 = sbuf([N], F32, "dk2")
+        dk3 = sbuf([N], F32, "dk3")
+        on_scalar(dk0[0][:], banks[0, 0])
+        on_scalar(dk1[0][:], banks[1, 0])
+        on_scalar(dk0[1][:], banks[0, 1])
+        scatter(1, halves[0], dk1[0][:])
+        scatter(0, halves[0], dk0[0][:])
+        on_vector(dk2[:, nth(0, HALF)], banks[2, 0])
+        on_scalar(dk1[1][:], banks[1, 1])
+        on_scalar(dk2[:, nth(1, HALF)], banks[2, 1])
+        for lane, dk in enumerate((dk0, dk1)):
+            scatter(lane, halves[1], dk[1][:])
+            store(lane)
+        scatter(2, offsets[:], dk2[:])
         store(2)
-        bank3 = in_bank(0, [P, N])
         for half in range(2):
             dk_half(3, half, bank3[:, nth(half, HALF)])
-        dk3 = new_dk(N, "gdp0_3")
         for half in range(2):
-            nc.scalar.copy(dk3[:, nth(half, HALF)], bank3[:, nth(half, HALF)])
+            on_scalar(dk3[:, nth(half, HALF)], bank3[:, nth(half, HALF)])
         for half in range(2):
-            scatter_half(3, half, dk3[:, nth(half, HALF)])
+            scatter(3, halves[half], dk3[:, nth(half, HALF)])
         store(3)
 
-        def new_rounded(chunks, name):
-            return keep.tile([P, PACK, chunks * CHUNK], BF16, name=name, align_bytes=64)
-
-        rounded01 = new_rounded(2, "k1")
-        rounded2 = new_rounded(1, "gdp0_1")
-        rounded3 = new_rounded(1, "k2")
+        rounded01 = sbuf([PACK, 2 * CHUNK], BF16, "v0")
+        rounded2 = sbuf([PACK, CHUNK], BF16, "dk2")
+        rounded3 = sbuf([PACK, CHUNK], BF16, "v1")
 
         def round_plane(how, lane, rounded, first):
             how(rounded[:, lane, :], windows[lane][:, first * CHUNK : first * CHUNK + rounded.shape[2]])
 
-        def group(how, rounded, span, grouped):
-            src = rounded[:, :, span].rearrange("p j (c i) -> p c j i", i=PACK)
-            how(grouped[:].rearrange("p (c i j) -> p c j i", i=PACK, j=PACK), src)
-            return grouped
-
-        y_codes = [keep.tile([P, CHUNK], U32, name="y_codes%d" % chunk, align_bytes=64) for chunk in range(CHUNKS)]
-        y_scales = keep.tile([P, 2 * CHUNK], U8, name="y_scales", align_bytes=64)
+        y_codes = [sbuf([CHUNK], U32, "y_codes%d" % chunk) for chunk in range(CHUNKS)]
+        y_scales = sbuf([2 * CHUNK], U8, "y_scales")
         words_out = out_1[0].rearrange("p t l -> p (t l)").bitcast(I32)
 
         def finish(chunk, span, grouped):
@@ -345,10 +261,9 @@ def tile_attend_gat_pl_k_kernel(tc, qT, kT, vT, doT, rw, qm, offs, out_0, out_1,
             )
             nc.sync.dma_start(words_out[:, nth(chunk, CHUNK)][:, span], y_codes[chunk][:, span].bitcast(I32))
 
-        on_vector, on_scalar = nc.vector.tensor_copy, nc.scalar.copy
         for lane in range(2):
-            round_plane(gpsimd_copy, lane, rounded01, 0)
-            round_plane(gpsimd_copy, lane, rounded3, 3)
+            round_plane(on_gpsimd, lane, rounded01, 0)
+            round_plane(on_gpsimd, lane, rounded3, 3)
         for lane in range(3):
             round_plane(on_vector, lane, rounded2, 2)
         round_plane(on_vector, 2, rounded3, 3)
@@ -356,16 +271,15 @@ def tile_attend_gat_pl_k_kernel(tc, qT, kT, vT, doT, rw, qm, offs, out_0, out_1,
         round_plane(on_vector, 3, rounded01, 0)
         round_plane(on_scalar, 3, rounded2, 2)
         round_plane(on_scalar, 3, rounded3, 3)
-        whole = slice(0, CHUNK)
-        y_grp2 = group(on_scalar, rounded2, whole, new_grouped())
-        y_halves3 = [
-            group(on_scalar, rounded3, nth(half, HALF), keep.tile([P, HALF * PACK], BF16, name="v%d" % (2 + half), align_bytes=64))
-            for half in range(2)
-        ]
-        y_grp01 = [group(on_vector, rounded01, nth(chunk, CHUNK), new_grouped()) for chunk in range(2)]
+        y_grp = [new_grouped() for chunk in range(3)]
+        y_halves3 = [sbuf([HALF * PACK], BF16, "v%d" % (2 + half)) for half in range(2)]
+        group(on_scalar, rounded2[:], y_grp[2][:])
+        for half in range(2):
+            group(on_scalar, rounded3[:, :, nth(half, HALF)], y_halves3[half][:])
         for chunk in range(2):
-            finish(chunk, whole, y_grp01[chunk])
-        finish(2, whole, y_grp2)
+            group(on_vector, rounded01[:, :, nth(chunk, CHUNK)], y_grp[chunk][:])
+        for chunk in range(3):
+            finish(chunk, slice(0, CHUNK), y_grp[chunk])
         for half in range(2):
             finish(3, nth(half, HALF), y_halves3[half])
         for quad in range(P // 32):

@@ -138,6 +138,9 @@ def tile_attend_gat_pl_k_kernel(tc, qT, kT, vT, doT, rw, qm, offs, out_0, out_1,
             on_vector(v_grp[:, :, lane], v_planes[lane][:].indirect(offsets[:]))
         v_words = v_grp[:].rearrange("p n j -> p (n j)")
         v_mx = [quantize(E4M3, v_words[:, 0 : PACK * BLOCK], "v_codes", "v_scales")]
+        idle_bank = in_bank(7, [N])
+        for repeat in range(2):
+            matmul(idle_bank[:], v_mx[0], E4M3, k_mx, E4M3, True, True)
 
         def ds_block(g, block, do_mx, grouped, number):
             bank = in_bank(number, [PACK, BLOCK])

@@ -27,6 +27,7 @@ BLOCKS = N // BLOCK
 CHUNK = 512
 CHUNKS = T // CHUNK
 SCALE_ROWS = 4
+GPSIMD_DEALS = 128
 GROUPED_BUFFERS = 4
 
 
@@ -58,11 +59,14 @@ def tile_attend_gat_pl_k_kernel(tc, qT, kT, vT, doT, rw, qm, offs, out_0, out_1,
             nc.sync.dma_start(raw[:], src.rearrange("(p j) c -> p j c", j=PACK))
             return raw
 
-        def load_planes(src, name):
+        def load_planes(src, name, counts):
             rows = src.rearrange("(p j) t -> p j t", j=PACK)
-            planes = [sbuf([T], F32, "%s%d" % (name, lane)) for lane in range(PACK)]
-            for lane in range(PACK):
-                nc.sync.dma_start(planes[lane][:], rows[:, lane, :])
+            planes = []
+            for count in counts:
+                first = len(planes)
+                loaded = sbuf([count, T], F32, "%s%d" % (name, first))
+                nc.sync.dma_start(loaded[:], rows[:, first : first + count, :])
+                planes.extend(loaded[:, i, :] for i in range(count))
             return planes
 
         q_raw = load_raw(qT[0], "q_raw")
@@ -70,9 +74,10 @@ def tile_attend_gat_pl_k_kernel(tc, qT, kT, vT, doT, rw, qm, offs, out_0, out_1,
         nc.sync.dma_start(offsets[:], offs)
         gate = keep.tile([P, PASSES, 2 * PACK], F32, name="gate")
         nc.scalar.dma_start(gate[:, :, 0:PACK], rw[0].rearrange("(g p j) o -> p g (j o)", g=PASSES, j=PACK))
-        k_planes = load_planes(kT, "k")
-        v_planes = load_planes(vT, "v")
-        do_raw = [load_raw(doT[0][:, nth(i, HALF)], "do_raw%d" % i) for i in range(R // HALF)]
+        k_planes = load_planes(kT, "k", (2, 1, 1))
+        v_planes = load_planes(vT, "v", (1, 1, 1, 1))
+        do_raw = [load_raw(doT[0][:, nth(i, HALF)], "do_raw%d" % i) for i in range(2)]
+        do_raw1 = load_raw(doT[0][:, nth(1, K_PASS)], "do_raw_pass1")
         qm_raw = [load_raw(qm[0][nth(g, K_PASS), :], "qm_raw%d" % g) for g in range(PASSES)]
 
         windows = [keep.tile([P, T], F32, name="window%d" % lane) for lane in range(PACK)]
@@ -114,16 +119,16 @@ def tile_attend_gat_pl_k_kernel(tc, qT, kT, vT, doT, rw, qm, offs, out_0, out_1,
             for half in range(2):
                 deal(on_scalar, q_raw[:, :, nth(g, K_PASS)], half, grouped[:, nth(half, HALF * PACK)])
             q_mx.append(quantize(E4M3, grouped[:], "q%d_codes" % g, "q%d_scales" % g))
-        k_listed = sbuf([PACK, N], BF16, "k_listed")
+        k_listed = sbuf([PACK, N], F32, "k_listed")
         for lane in range(PACK):
-            on_vector(k_listed[:, lane, :], k_planes[lane][:].indirect(offsets[:]))
+            on_vector(k_listed[:, lane, :], k_planes[lane].indirect(offsets[:]))
         k_grp = new_grouped()
         for half, how in enumerate((on_vector, on_scalar)):
             group(how, k_listed[:, :, nth(half, HALF)], k_grp[:, nth(half, HALF * PACK)])
         k_mx = quantize(E4M3, k_grp[:], "k_codes", "k_scales")
         weight = []
         for g in range(PASSES):
-            by_lane = sbuf([PACK, N], F32, "k%d" % g)
+            by_lane = sbuf([PACK, N], F32, "k%d" % (2 + g))
             for lane in range(PACK):
                 bank = in_bank(PACK * g + lane, [N])
                 matmul(bank[:], columns(q_mx[g], nth(lane, P)), E4M3, k_mx, E4M3, True, True)
@@ -135,7 +140,7 @@ def tile_attend_gat_pl_k_kernel(tc, qT, kT, vT, doT, rw, qm, offs, out_0, out_1,
 
         v_grp = sbuf([N, PACK], BF16, "v_grp")
         for lane in range(PACK):
-            on_vector(v_grp[:, :, lane], v_planes[lane][:].indirect(offsets[:]))
+            on_vector(v_grp[:, :, lane], v_planes[lane].indirect(offsets[:]))
         v_words = v_grp[:].rearrange("p n j -> p (n j)")
         v_mx = [quantize(E4M3, v_words[:, 0 : PACK * BLOCK], "v_codes", "v_scales")]
         idle_bank = in_bank(7, [N])
@@ -163,9 +168,12 @@ def tile_attend_gat_pl_k_kernel(tc, qT, kT, vT, doT, rw, qm, offs, out_0, out_1,
         v_mx.extend(columns(v_rest, nth(i, BLOCK)) for i in range(BLOCKS - 1))
 
         do_grp1 = new_grouped()
-        for piece in range(2):
-            for half in range(2):
-                deal(on_scalar, do_raw[2 + piece][:], half, do_grp1[:, nth(half, HALF * PACK)], piece * HALF // PACK)
+        on_gpsimd(
+            do_grp1[:].rearrange("p (t m j) -> p t m j", t=PACK, j=PACK)[:, :, 0 : GPSIMD_DEALS // PACK],
+            do_raw1[:, :, 0:GPSIMD_DEALS].rearrange("p j (m t) -> p t m j", t=PACK),
+        )
+        for half in range(2):
+            deal(on_scalar, do_raw1[:, :, GPSIMD_DEALS:], half, do_grp1[:, nth(half, HALF * PACK)], GPSIMD_DEALS // PACK)
         ds_grp0 = new_grouped()
         for block in range(BLOCKS):
             ds_block(0, block, do_mx0, ds_grp0[:, nth(block, PACK * BLOCK)], block)
@@ -196,7 +204,7 @@ def tile_attend_gat_pl_k_kernel(tc, qT, kT, vT, doT, rw, qm, offs, out_0, out_1,
         ds_block(1, 3, do_mx1, ds_grp13[:], 7)
         late_mx = quantize(E4M3, qm_late[:], "qm_late_codes", "qm_late_scales")
         qm_mx.update({(g, 1): columns(late_mx, nth(g, HALF)) for g in range(PASSES)})
-        ds_mx1.append((sbuf([HALF], U32, "k1")[:], sbuf([HALF], U8, "ds11_scales")[:]))
+        ds_mx1.append((sbuf([HALF], U32, "k3")[:], sbuf([HALF], U8, "ds11_scales")[:]))
         quantize_last_block(0, ds_grp12)
         quantize_last_block(1, ds_grp13)
 

from contextlib import ExitStack

import concourse.mybir as mybir

N, T, D, DV, R = 512, 2048, 512, 512, 1024
FLOPS = 2 * R * N * (D + DV + D)

F32 = mybir.dt.float32
BF16 = mybir.dt.bfloat16
I32 = mybir.dt.int32
U32 = mybir.dt.uint32
U16 = mybir.dt.uint16
U8 = mybir.dt.uint8
E4M3 = mybir.dt.float8_e4m3fn_x4
E5M2 = mybir.dt.float8_e5m2_x4
ACT = mybir.ActivationFunctionType
ALU = mybir.AluOpType

P = 128
PACK = 4
K_PASS = P * PACK
PASSES = R // K_PASS
HALF = K_PASS // 2
BAND = 16
BLOCK = 128
BLOCKS = N // BLOCK
CHUNK = 512
CHUNKS = T // CHUNK
SCALE_ROWS = 4
GPSIMD_DEALS = 128
GROUPED_BUFFERS = 4


def tile_attend_gat_pl_k_kernel(tc, qT, kT, vT, doT, rw, qm, offs, out_0, out_1, out_2):
    nc = tc.nc
    with ExitStack() as ctx:
        keep = ctx.enter_context(tc.tile_pool(name="keep", bufs=1))
        grp = ctx.enter_context(tc.tile_pool(name="grp", bufs=GROUPED_BUFFERS))
        psum = ctx.enter_context(tc.psum_pool(name="psum", bufs=1))
        on_vector, on_scalar = nc.vector.tensor_copy, nc.scalar.copy

        def on_gpsimd(dst, src):
            nc.gpsimd.tensor_scalar(dst, src, 1.0, -0.0, ALU.mult, ALU.add)

        def nth(i, width):
            return slice(i * width, (i + 1) * width)

        def sbuf(shape, dtype, name):
            return keep.tile([P] + shape, dtype, name=name, align_bytes=64)

        def in_bank(number, shape):
            return psum.tile([P] + shape, F32, name="bank%d" % number)

        def new_grouped():
            return grp.tile([P, K_PASS * PACK], BF16, name="grouped", align_bytes=64)

        def load_raw(src, name):
            raw = sbuf([PACK, src.shape[1]], F32, name)
            nc.sync.dma_start(raw[:], src.rearrange("(p j) c -> p j c", j=PACK))
            return raw

        def load_planes(src, name, counts):
            rows = src.rearrange("(p j) t -> p j t", j=PACK)
            planes = []
            for count in counts:
                first = len(planes)
                loaded = sbuf([count, T], F32, "%s%d" % (name, first))
                nc.sync.dma_start(loaded[:], rows[:, first : first + count, :])
                planes.extend(loaded[:, i, :] for i in range(count))
            return planes

        q_raw = load_raw(qT[0], "q_raw")
        offsets = keep.tile([P, N // BAND], U16, name="offsets")
        nc.sync.dma_start(offsets[:], offs)
        gate = keep.tile([P, PASSES, 2 * PACK], F32, name="gate")
        nc.scalar.dma_start(gate[:, :, 0:PACK], rw[0].rearrange("(g p j) o -> p g (j o)", g=PASSES, j=PACK))
        k_planes = load_planes(kT, "k", (2, 1, 1))
        v_planes = load_planes(vT, "v", (1, 1, 1, 1))
        do_raw = [load_raw(doT[0][:, nth(i, HALF)], "do_raw%d" % i) for i in range(2)]
        do_raw1 = load_raw(doT[0][:, nth(1, K_PASS)], "do_raw_pass1")
        qm_raw = [load_raw(qm[0][nth(g, K_PASS), :], "qm_raw%d" % g) for g in range(PASSES)]

        windows = [keep.tile([P, T], F32, name="window%d" % lane) for lane in range(PACK)]
        for window in windows:
            nc.vector.memset(window[:], 0.0)

        def quantize(fmt, grouped, codes_name, scales_name):
            width = grouped.shape[1] // PACK
            codes, scales = sbuf([width], U32, codes_name), sbuf([width], U8, scales_name)
            nc.vector.quantize_mx(out=codes[:].bitcast(fmt), scales=scales[:], in_=grouped)
            return codes[:], scales[:]

        def columns(mx, span):
            return mx[0][:, span], mx[1][:, span]

        def matmul(out, lhs, lhs_fmt, rhs, rhs_fmt, start, stop):
            nc.tensor.matmul_mx(
                out=out,
                lhsT=lhs[0].bitcast(lhs_fmt),
                lhsT_scale=lhs[1],
                rhs=rhs[0].bitcast(rhs_fmt),
                rhs_scale=rhs[1],
                start=start,
                stop=stop,
            )

        def deal(how, raw, half, grouped, first=0):
            count = raw.shape[2] // PACK
            src = raw.rearrange("p j (m t) -> p m j t", t=PACK)[:, :, :, nth(half, 2)]
            how(grouped.rearrange("p (t m j) -> p m j t", t=2, j=PACK)[:, first : first + count], src)

        def group(how, by_lane, grouped):
            src = by_lane.rearrange("p j (c i) -> p c j i", i=PACK)
            how(grouped.rearrange("p (c i j) -> p c j i", i=PACK, j=PACK), src)

        q_mx = []
        for g in range(PASSES):
            grouped = new_grouped()
            for half in range(2):
                deal(on_scalar, q_raw[:, :, nth(g, K_PASS)], half, grouped[:, nth(half, HALF * PACK)])
            q_mx.append(quantize(E4M3, grouped[:], "q%d_codes" % g, "q%d_scales" % g))
        k_listed = sbuf([PACK, N], F32, "k_listed")
        for lane in range(PACK):
            on_vector(k_listed[:, lane, :], k_planes[lane].indirect(offsets[:]))
        k_grp = new_grouped()
        for half, how in enumerate((on_vector, on_scalar)):
            group(how, k_listed[:, :, nth(half, HALF)], k_grp[:, nth(half, HALF * PACK)])
        k_mx = quantize(E4M3, k_grp[:], "k_codes", "k_scales")
        weight = []
        for g in range(PASSES):
            by_lane = sbuf([PACK, N], F32, "k%d" % (2 + g))
            for lane in range(PACK):
                bank = in_bank(PACK * g + lane, [N])
                matmul(bank[:], columns(q_mx[g], nth(lane, P)), E4M3, k_mx, E4M3, True, True)
                nc.scalar.activation(by_lane[:, lane, :], bank[:], ACT.Relu, scale=2.0)
                nc.gpsimd.tensor_scalar(
                    by_lane[:, lane, :], by_lane[:, lane, :], gate[:, g, lane : lane + 1], -0.0, ALU.mult, ALU.add
                )
            weight.append(by_lane)

        v_grp = sbuf([N, PACK], BF16, "v_grp")
        for lane in range(PACK):
            on_vector(v_grp[:, :, lane], v_planes[lane].indirect(offsets[:]))
        v_words = v_grp[:].rearrange("p n j -> p (n j)")
        v_mx = [quantize(E4M3, v_words[:, 0 : PACK * BLOCK], "v_codes", "v_scales")]
        idle_bank = in_bank(7, [N])
        for repeat in range(2):
            matmul(idle_bank[:], v_mx[0], E4M3, k_mx, E4M3, True, True)

        def ds_block(g, block, do_mx, grouped, number):
            bank = in_bank(number, [PACK, BLOCK])
            for lane in (2, 3, 0, 1):
                matmul(bank[:, lane, :], columns(do_mx[lane // 2], nth(lane % 2, P)), E5M2, v_mx[block], E4M3, True, True)
            nc.vector.tensor_tensor(
                grouped.rearrange("p (c i j) -> p c j i", i=2, j=PACK),
                bank[:].rearrange("p j (c i) -> p c j i", i=2),
                weight[g][:, :, nth(block, BLOCK)].rearrange("p j (c i) -> p c j i", i=2),
                ALU.mult,
            )

        do_grp0 = [sbuf([HALF * PACK], BF16, "do_grp0%d" % half) for half in range(2)]
        for half in (1, 0):
            deal(on_scalar, do_raw[0][:], half, do_grp0[half][:])
        deal(on_vector, do_raw[1][:], 1, do_grp0[1][:], HALF // PACK)
        deal(on_scalar, do_raw[1][:], 0, do_grp0[0][:], HALF // PACK)
        do_mx0 = {half: quantize(E5M2, do_grp0[half][:], "do0%d_codes" % half, "do0%d_scales" % half) for half in (1, 0)}
        v_rest = quantize(E4M3, v_words[:, PACK * BLOCK :], "do_grp01", "v_rest_scales")
        v_mx.extend(columns(v_rest, nth(i, BLOCK)) for i in range(BLOCKS - 1))

        do_grp1 = new_grouped()
        on_gpsimd(
            do_grp1[:].rearrange("p (t m j) -> p t m j", t=PACK, j=PACK)[:, :, 0 : GPSIMD_DEALS // PACK],
            do_raw1[:, :, 0:GPSIMD_DEALS].rearrange("p j (m t) -> p t m j", t=PACK),
        )
        for half in range(2):
            deal(on_scalar, do_raw1[:, :, GPSIMD_DEALS:], half, do_grp1[:, nth(half, HALF * PACK)], GPSIMD_DEALS // PACK)
        ds_grp0 = new_grouped()
        for block in range(BLOCKS):
            ds_block(0, block, do_mx0, ds_grp0[:, nth(block, PACK * BLOCK)], block)
        do_whole1 = quantize(E5M2, do_grp1[:], "do1_codes", "do1_scales")
        do_mx1 = [columns(do_whole1, nth(half, HALF)) for half in range(2)]
        ds_mx0 = quantize(E5M2, ds_grp0[:], "ds0_codes", "ds0_scales")

        qm_grp = [sbuf([HALF * PACK], BF16, "qm_grp%d" % g) for g in range(PASSES)]
        qm_late = sbuf([K_PASS * PACK], BF16, "qm_late")
        for g in range(PASSES):
            deal(on_scalar, qm_raw[g][:], 0, qm_grp[g][:])
            deal(on_scalar, qm_raw[g][:], 1, qm_late[:, nth(g, HALF * PACK)])

        ds_grp1 = sbuf([HALF * PACK], BF16, "ds_grp1")
        for block in range(2):
            ds_block(1, block, do_mx1, ds_grp1[:, nth(block, PACK * BLOCK)], 4 + block)
        qm_mx = {(0, 0): quantize(E4M3, qm_grp[0][:], "qm00_codes", "qm00_scales")}
        ds_mx1 = [quantize(E5M2, ds_grp1[:], "ds10_codes", "ds10_scales")]
        ds_grp12 = sbuf([BLOCK * PACK], BF16, "qm_grp0")
        ds_block(1, 2, do_mx1, ds_grp12[:], 6)

        def quantize_last_block(i, grouped):
            codes, scales = columns(ds_mx1[1], nth(i, BLOCK))
            nc.vector.quantize_mx(out=codes.bitcast(E5M2), scales=scales, in_=grouped[:])

        qm_mx[1, 0] = quantize(E4M3, qm_grp[1][:], "qm10_codes", "qm10_scales")
        ds_grp13 = sbuf([BLOCK * PACK], BF16, "qm_grp1")
        ds_block(1, 3, do_mx1, ds_grp13[:], 7)
        late_mx = quantize(E4M3, qm_late[:], "qm_late_codes", "qm_late_scales")
        qm_mx.update({(g, 1): columns(late_mx, nth(g, HALF)) for g in range(PASSES)})
        ds_mx1.append((sbuf([HALF], U32, "k3")[:], sbuf([HALF], U8, "ds11_scales")[:]))
        quantize_last_block(0, ds_grp12)
        quantize_last_block(1, ds_grp13)

        def dk_half(lane, half, bank):
            moving = [columns(ds_mx0, nth(half, HALF)), ds_mx1[half]]
            for g in range(PASSES):
                stationary = columns(qm_mx[g, lane // 2], nth(lane % 2, P))
                matmul(bank, stationary, E4M3, moving[g], E5M2, g == 0, g == PASSES - 1)
            return bank

        def scatter(lane, listed, dk):
            if lane % 2 == 0:
                on_vector(windows[lane][:].indirect(listed), dk)
            else:
                nc.scalar.activation(windows[lane][:].indirect(listed), dk, ACT.Copy)

        def store(lane):
            nc.sync.dma_start(out_0.rearrange("(p t) c -> p t c", t=PACK)[:, lane, :], windows[lane][:])

        banks = {(lane, 0): dk_half(lane, 0, in_bank(lane, [HALF])[:]) for lane in range(3)}
        banks.update({(lane, 1): dk_half(lane, 1, in_bank(3 + lane, [HALF])[:]) for lane in range(3)})
        bank3 = in_bank(0, [N])
        halves = [offsets[:, nth(half, HALF // BAND)] for half in range(2)]
        dk0 = [sbuf([HALF], F32, "dk0%d" % half) for half in range(2)]
        dk1 = [sbuf([HALF], F32, "dk1%d" % half) for half in range(2)]
        dk2 = sbuf([N], F32, "dk2")
        dk3 = sbuf([N], F32, "dk3")
        on_scalar(dk0[0][:], banks[0, 0])
        on_scalar(dk1[0][:], banks[1, 0])
        on_scalar(dk0[1][:], banks[0, 1])
        scatter(1, halves[0], dk1[0][:])
        scatter(0, halves[0], dk0[0][:])
        on_vector(dk2[:, nth(0, HALF)], banks[2, 0])
        on_scalar(dk1[1][:], banks[1, 1])
        on_scalar(dk2[:, nth(1, HALF)], banks[2, 1])
        for lane, dk in enumerate((dk0, dk1)):
            scatter(lane, halves[1], dk[1][:])
            store(lane)
        scatter(2, offsets[:], dk2[:])
        store(2)
        for half in range(2):
            dk_half(3, half, bank3[:, nth(half, HALF)])
        for half in range(2):
            on_scalar(dk3[:, nth(half, HALF)], bank3[:, nth(half, HALF)])
        for half in range(2):
            scatter(3, halves[half], dk3[:, nth(half, HALF)])
        store(3)

        rounded01 = sbuf([PACK, 2 * CHUNK], BF16, "v0")
        rounded2 = sbuf([PACK, CHUNK], BF16, "dk2")
        rounded3 = sbuf([PACK, CHUNK], BF16, "v1")

        def round_plane(how, lane, rounded, first):
            how(rounded[:, lane, :], windows[lane][:, first * CHUNK : first * CHUNK + rounded.shape[2]])

        y_codes = [sbuf([CHUNK], U32, "y_codes%d" % chunk) for chunk in range(CHUNKS)]
        y_scales = sbuf([2 * CHUNK], U8, "y_scales")
        words_out = out_1[0].rearrange("p t l -> p (t l)").bitcast(I32)

        def finish(chunk, span, grouped):
            nc.vector.quantize_mx(
                out=y_codes[chunk][:, span].bitcast(E4M3),
                scales=y_scales[SCALE_ROWS * (chunk // 2) :, nth(chunk % 2, CHUNK)][:, span],
                in_=grouped[:],
            )
            nc.sync.dma_start(words_out[:, nth(chunk, CHUNK)][:, span], y_codes[chunk][:, span].bitcast(I32))

        for lane in range(2):
            round_plane(on_gpsimd, lane, rounded01, 0)
            round_plane(on_gpsimd, lane, rounded3, 3)
        for lane in range(3):
            round_plane(on_vector, lane, rounded2, 2)
        round_plane(on_vector, 2, rounded3, 3)
        round_plane(on_vector, 2, rounded01, 0)
        round_plane(on_vector, 3, rounded01, 0)
        round_plane(on_scalar, 3, rounded2, 2)
        round_plane(on_scalar, 3, rounded3, 3)
        y_grp = [new_grouped() for chunk in range(3)]
        y_halves3 = [sbuf([HALF * PACK], BF16, "v%d" % (2 + half)) for half in range(2)]
        group(on_scalar, rounded2[:], y_grp[2][:])
        for half in range(2):
            group(on_scalar, rounded3[:, :, nth(half, HALF)], y_halves3[half][:])
        for chunk in range(2):
            group(on_vector, rounded01[:, :, nth(chunk, CHUNK)], y_grp[chunk][:])
        for chunk in range(3):
            finish(chunk, slice(0, CHUNK), y_grp[chunk])
        for half in range(2):
            finish(3, nth(half, HALF), y_halves3[half])
        for quad in range(P // 32):
            rows = out_2[0][nth(quad, SCALE_ROWS), :].bitcast(I32).rearrange("r (c x) -> c r x", c=2)
            nc.sync.dma_start(rows, y_scales[32 * quad : 32 * quad + 2 * SCALE_ROWS, :].bitcast(I32))
